import numpy as np
import ml_dtypes


def mxq(x, axis, fmt="e4m3"):
    dtype, down = {"e4m3": (ml_dtypes.float8_e4m3fn, 7), "e5m2": (ml_dtypes.float8_e5m2, 14)}[fmt]
    v = np.moveaxis(np.asarray(x, np.float32).astype(ml_dtypes.bfloat16).astype(np.float64), axis, -1)
    blocks = v.reshape(v.shape[:-1] + (-1, 32))
    amax = np.abs(blocks).max(-1, keepdims=True)
    byte = np.maximum(np.where(amax > 0, np.frexp(amax)[1] - 1 + 127, 0) - down, 1)
    scale = np.exp2(byte - 127.0)
    codes = (blocks / scale).astype(np.float32).astype(dtype).astype(np.float64)
    return np.moveaxis((codes * scale).reshape(v.shape), -1, axis)


WIDE = False


def mx_kscale(k):
    if not WIDE:
        return np.ones(k)
    levels = np.array([10, -10, 5, -5, 0])
    if k % 512:
        return np.exp2(np.random.permutation(np.resize(levels, k // 32))).repeat(32)
    a = np.empty((k // 512, 16))
    for p in range(k // 512):
        a[p, :8] = np.random.permutation(np.resize(levels, 8))
        for g in range(8):
            far = levels[np.abs(levels - a[p, g]) >= 10]
            a[p, g + 8] = far[np.random.randint(len(far))]
    return np.exp2(a.ravel()).repeat(32)


def f64(x):
    return np.asarray(x).astype(np.float64)


def striped(idx):
    return np.tile(idx.reshape(-1, 16).T, (8, 1)).astype(np.uint16)


def unstriped(offs):
    return offs[:16].T.reshape(-1).astype(np.int64)


E2M1 = np.array([0.0, 0.5, 1.0, 1.5, 2.0, 3.0, 4.0, 6.0, -0.0, -0.5, -1.0, -1.5, -2.0, -3.0, -4.0, -6.0])


def pack_weight(w, fmt):
    k, n = w.shape
    w = f64(np.asarray(w, np.float32).astype(ml_dtypes.bfloat16)).reshape(k // 32, 32, n)
    amax = np.abs(w).max(1)
    if fmt == "e4m3":
        byte = np.frexp(amax)[1] - 1 + 127 - 7
    else:
        mant, ex = np.frexp(amax / 6.0)
        byte = np.where(mant > 0.5, ex, ex - 1) + 127
    byte = np.clip(np.where(amax > 0, byte, 1), 1, 254)
    scaled = (w * np.exp2(127.0 - byte)[:, None, :]).reshape(k, n).astype(np.float32)
    by_word = np.ascontiguousarray(scaled.reshape(k // 512, 128, 4, n).transpose(0, 1, 3, 2))
    if fmt == "e4m3":
        words = by_word.astype(ml_dtypes.float8_e4m3fn).view(np.uint8)
    else:
        c = by_word.astype(ml_dtypes.float4_e2m1fn).view(np.uint8) & 0xF
        words = (c[..., 0::2] | (c[..., 1::2] << 4)).reshape(k // 512, 128, 2 * n)
    return np.ascontiguousarray(words), np.ascontiguousarray(byte.astype(np.uint8).reshape(k // 512, 16, n))


def unpack_weight(words, scales, fmt):
    g, _, n = scales.shape
    words = np.ascontiguousarray(words).reshape(g, 128, n, -1)
    if fmt == "e4m3":
        vals = words.view(ml_dtypes.float8_e4m3fn).astype(np.float64)
    else:
        nib = np.empty((g, 128, n, 4), np.uint8)
        nib[..., 0::2] = words & 0xF
        nib[..., 1::2] = words >> 4
        vals = E2M1[nib]
    vals = vals * np.repeat(np.exp2(scales.astype(np.float64) - 127.0), 8, axis=1)[..., None]
    return vals.transpose(0, 1, 3, 2).reshape(g * 512, n)


def gelu(v):
    return 0.5 * v * (1.0 + np.tanh(np.sqrt(2.0 / np.pi) * (v + 0.044715 * v**3)))


K, H, N, T, S, T2, P = 1536, 1024, 768, 2048, 1024, 2048, 1024

def setup_inputs():
    n = np.random.standard_normal
    s = mx_kscale(K)[:, None]
    u = mx_kscale(H)[:, None]
    d = {}
    d["tab_words"], d["tab_scales"] = pack_weight(n((K, T)) * s, "e4m3")
    d["offs"] = striped(np.random.permutation(T)[:S])
    d["w1_words"], d["w1_scales"] = pack_weight(n((K, H)) / np.sqrt(K) / s * u.T, "e2m1")
    d["wgs"] = np.exp(0.3 * n((128, S))).astype(np.float32)
    d["page0"] = (n((H, T2)) * u).astype(np.float32)
    d["offs2"] = striped(np.random.permutation(T2)[:S])
    d["offs3"] = striped(np.random.permutation(T2)[:P])
    d["reserve"] = (-(0.4 + 0.3 * np.abs(n(H))) * u[:, 0]).astype(np.float32)
    d["ceiling"] = ((0.5 + 0.4 * np.abs(n(H))) * u[:, 0]).astype(np.float32)
    d["w2"] = (1.5 * n((H, N)) / np.sqrt(H) / u).astype(np.float32)
    d["seller"] = (1.0 + 0.5 * n((N, P))).astype(np.float32)
    return d

def reference(tab_words, tab_scales, offs, w1_words, w1_scales, wgs, page0, offs2, offs3,
              reserve, ceiling, w2, seller):
    v = unpack_weight(tab_words, tab_scales, "e4m3")[:, unstriped(offs)]
    w1 = unpack_weight(w1_words, w1_scales, "e2m1")
    h = w1.T @ v
    page = f64(page0).copy()
    page[:, unstriped(offs2)] = np.tile(f64(wgs), (H // 128, 1)) * h
    x = page[:, unstriped(offs3)]
    z = np.minimum(np.maximum(x, f64(reserve)[:, None]), f64(ceiling)[:, None])
    y = mxq(f64(w2), 0, "e4m3").T @ mxq(z, 0, "e4m3")
    return y * f64(seller)

@@ -1,0 +1,247 @@
+from contextlib import ExitStack
+
+import concourse.mybir as mybir
+
+K, H, N, T, S, M = 1536, 1024, 768, 2048, 1024, 1024
+FLOPS = 2 * K * H * S + 2 * H * N * M
+
+F32 = mybir.dt.float32
+BF16 = mybir.dt.bfloat16
+I32 = mybir.dt.int32
+U32 = mybir.dt.uint32
+U16 = mybir.dt.uint16
+U8 = mybir.dt.uint8
+FP8X4 = mybir.dt.float8_e4m3fn_x4
+FP4X4 = mybir.dt.float4_e2m1fn_x4
+MULT = mybir.AluOpType.mult
+MAX = mybir.AluOpType.max
+MIN = mybir.AluOpType.min
+
+P = 128
+PACK = 4
+K_PASSES = K // (P * PACK)
+R_PASSES = H // (P * PACK)
+BANK = 512
+CHUNK = 256
+CHUNKS = M // CHUNK
+N_TILES = N // P
+SPARE = 32 - PACK * K_PASSES
+SHIFT_ROWS = 100
+
+
+def tile_list_auction_guide_clip_kernel(
+    tc, tab_words, tab_scales, offs, w1_words, w1_scales, wgs, page0, offs2, offs3,
+    reserve, ceiling, w2, seller, out,
+):
+    nc = tc.nc
+    with ExitStack() as ctx:
+        keep = ctx.enter_context(tc.tile_pool(name="keep", bufs=1))
+        big = ctx.enter_context(tc.tile_pool(name="big", bufs=4))
+        ring = ctx.enter_context(tc.tile_pool(name="ring", bufs=4))
+        stage = ctx.enter_context(tc.tile_pool(name="stage", bufs=6))
+        psum_h = ctx.enter_context(tc.psum_pool(name="psum_h", bufs=2))
+        psum_y = ctx.enter_context(tc.psum_pool(name="psum_y", bufs=6))
+
+        idx = keep.tile([P, S // 16], U16, name="idx")
+        idx2 = keep.tile([P, S // 16], U16, name="idx2")
+        idx3 = keep.tile([P, M // 16], U16, name="idx3")
+
+        tab_sc = keep.tile([P, T], U8, name="tab_sc", align_bytes=64)
+        w1_sc = keep.tile([P, H], U8, name="w1_sc", align_bytes=64)
+        v_sc = keep.tile([P, K_PASSES * S], U8, name="v_sc", align_bytes=64)
+        w1p_sc = keep.tile([P, K_PASSES * H], U8, name="w1p_sc", align_bytes=64)
+        for q in range(4):
+            nc.vector.memset(tab_sc[32 * q : 32 * q + SPARE, :].bitcast(I32), 0)
+        for q in range(4):
+            nc.gpsimd.memset(w1_sc[32 * q : 32 * q + SPARE, :].bitcast(I32), 0)
+        nc.gpsimd.memset(v_sc[96:P, :].bitcast(I32), 0)
+        nc.gpsimd.memset(w1p_sc[96:P, :].bitcast(I32), 0)
+
+        nc.sync.dma_start(idx[:], offs)
+        for packed, rows in ((tab_sc, tab_scales), (w1_sc, w1_scales)):
+            for q in range(4):
+                nc.scalar.dma_start(
+                    packed[32 * q + SPARE : 32 * q + 32, :].bitcast(I32),
+                    rows[:, 4 * q : 4 * q + 4, :].bitcast(I32),
+                )
+        w1_raw = [keep.tile([P, 2 * H], U8, name=f"w1_raw{a}", align_bytes=64) for a in range(K_PASSES)]
+        for a in range(K_PASSES):
+            nc.sync.dma_start(w1_raw[a][:].bitcast(I32), w1_words[a].bitcast(I32))
+        tab = [big.tile([P, T], I32, name=f"tab{a}", tag="big") for a in range(K_PASSES)]
+        for a in range(K_PASSES):
+            nc.sync.dma_start(tab[a][:], tab_words[a].rearrange("p t i -> p (t i)").bitcast(I32))
+
+        def lower_planes(planes, packed, width):
+            for a in range(K_PASSES):
+                first = SPARE + PACK * a
+                nc.scalar.dma_start(
+                    planes[0:SHIFT_ROWS, a * width : (a + 1) * width].bitcast(I32),
+                    packed[first : first + SHIFT_ROWS, :].bitcast(I32),
+                )
+
+        w1p = [keep.tile([P, 2 * H], U8, name=f"w1p{a}", align_bytes=64) for a in range(K_PASSES)]
+        for a in range(K_PASSES):
+            nc.vector.tensor_copy(
+                w1p[a][:].bitcast(U16).rearrange("p (b t c i) -> p b c t i", b=R_PASSES, t=PACK, i=8),
+                w1_raw[a][:].bitcast(U16).rearrange("p (b c i t) -> p b c t i", b=R_PASSES, t=PACK, i=8),
+            )
+        v_packed = keep.tile([P, S], U8, name="v_packed", align_bytes=64)
+        nc.vector.tensor_copy(v_packed[:], tab_sc[:].indirect(idx[:]))
+        lower_planes(v_sc, v_packed, S)
+        w1p_packed = keep.tile([P, H], U8, name="w1p_packed", align_bytes=64)
+        nc.vector.tensor_copy(
+            w1p_packed[:].rearrange("p (b t c i) -> p b c t i", b=R_PASSES, t=PACK, i=16),
+            w1_sc[:].rearrange("p (b c i t) -> p b c t i", b=R_PASSES, t=PACK, i=16),
+        )
+        lower_planes(w1p_sc, w1p_packed, H)
+
+        wgs_rows = wgs.rearrange("(q t) j -> q t j", t=PACK)
+        wgs_first = keep.tile([P, S], F32, name="wgs_first")
+        wgs_rest = keep.tile([P, (PACK - 1) * S], F32, name="wgs_rest")
+        pages = [keep.tile([P, T], F32, name=f"page{i}") for i in range(R_PASSES * PACK)]
+        page_rows = page0.rearrange("(b p t) c -> b t p c", t=PACK, p=P)
+
+        def load_page(i):
+            nc.sync.dma_start(pages[i][:], page_rows[i // PACK, i % PACK])
+
+        for q in range(4):
+            nc.sync.dma_start(wgs_first[32 * q : 32 * q + 32, :], wgs_rows[:, 0, :])
+        nc.sync.dma_start(idx2[:], offs2)
+        load_page(0)
+        load_page(1)
+        for q in range(4):
+            nc.sync.dma_start(
+                wgs_rest[32 * q : 32 * q + 32, :], wgs_rows[:, 1:, :].rearrange("q t j -> q (t j)")
+            )
+        load_page(2)
+        load_page(3)
+        nc.sync.dma_start(idx3[:], offs3)
+        lo = keep.tile([P, R_PASSES, PACK], F32, name="lo")
+        hi = keep.tile([P, R_PASSES, PACK], F32, name="hi")
+        nc.sync.dma_start(lo[:], reserve.rearrange("(b p t) -> p b t", p=P, t=PACK))
+        nc.sync.dma_start(hi[:], ceiling.rearrange("(b p t) -> p b t", p=P, t=PACK))
+
+        v = [keep.tile([P, S], U32, name=f"v{a}", align_bytes=64) for a in range(K_PASSES)]
+        for a in range(K_PASSES - 1):
+            nc.vector.tensor_copy(v[a][:], tab[a][:].bitcast(U32).indirect(idx[:]))
+        last = K_PASSES - 1
+        for half in range(S // BANK):
+            nc.vector.tensor_copy(
+                v[last][:, half * BANK : (half + 1) * BANK],
+                tab[last][:].bitcast(U32).indirect(idx[:, half * BANK // 16 : (half + 1) * BANK // 16]),
+            )
+
+        def put_rows(i):
+            t = i % PACK
+            weight = wgs_first[:] if t == 0 else wgs_rest[:, (t - 1) * S : t * S]
+            h = ring.tile([P, S], F32, name="h", tag="work")
+            for half in range(S // BANK):
+                cols = slice(half * BANK, (half + 1) * BANK)
+                acc = psum_h.tile([P, BANK], F32, name="acc_h")
+                for a in range(K_PASSES):
+                    nc.tensor.matmul_mx(
+                        acc[:],
+                        lhsT=w1p[a][:, 2 * P * i : 2 * P * (i + 1)].bitcast(FP4X4),
+                        lhsT_scale=w1p_sc[:, a * H + P * i : a * H + P * (i + 1)],
+                        rhs=v[a][:, cols].bitcast(FP8X4),
+                        rhs_scale=v_sc[:, a * S + half * BANK : a * S + (half + 1) * BANK],
+                        start=(a == 0),
+                        stop=(a == K_PASSES - 1),
+                    )
+                nc.scalar.copy(h[:, cols], acc[:])
+                if i == 0:
+                    nc.vector.tensor_tensor(
+                        pages[i][:].indirect(idx2[:, half * BANK // 16 : (half + 1) * BANK // 16]),
+                        h[:, cols], weight[:, cols], MULT,
+                    )
+            if i > 0:
+                nc.vector.tensor_tensor(pages[i][:].indirect(idx2[:]), h[:], weight, MULT)
+
+        w2_codes = [keep.tile([P, N], U32, name=f"w2_codes{b}", align_bytes=64) for b in range(R_PASSES)]
+        w2_sc = [keep.tile([P, N], U8, name=f"w2_sc{b}", align_bytes=64) for b in range(R_PASSES)]
+
+        def quantise_w2(b):
+            raw = keep.tile([P, PACK, N], F32, name="w2_raw")
+            nc.sync.dma_start(raw[:], w2[b * P * PACK : (b + 1) * P * PACK, :].rearrange("(p t) n -> p t n", t=PACK))
+            woven = keep.tile([P, N * PACK], BF16, name="w2_woven", align_bytes=64)
+            nc.scalar.copy(
+                woven[:].rearrange("p (c i t) -> p c t i", t=PACK, i=4),
+                raw[:].rearrange("p t (c i) -> p c t i", i=4),
+            )
+            for n0, n1 in ((0, 512), (512, N)):
+                nc.vector.quantize_mx(
+                    w2_codes[b][:, n0:n1].bitcast(FP8X4), w2_sc[b][:, n0:n1], woven[:, PACK * n0 : PACK * n1]
+                )
+
+        z_codes = {}
+        z_sc = {}
+        woven_z = {}
+
+        def fetch(b, c):
+            x = ring.tile([P, PACK, CHUNK], F32, name="x", tag="work")
+            offsets = idx3[:, c * CHUNK // 16 : (c + 1) * CHUNK // 16]
+            for t in range(PACK):
+                nc.vector.tensor_copy(x[:, t, :], pages[b * PACK + t][:].indirect(offsets))
+            for t in range(PACK):
+                nc.vector.tensor_scalar(x[:, t, :], x[:, t, :], lo[:, b, t : t + 1], hi[:, b, t : t + 1], MAX, MIN)
+            woven_z[b, c] = ring.tile([P, CHUNK * PACK], BF16, name="z_woven", align_bytes=64)
+            nc.scalar.copy(
+                woven_z[b, c][:].rearrange("p (c i t) -> p c t i", t=PACK, i=4),
+                x[:].rearrange("p t (c i) -> p c t i", i=4),
+            )
+
+        def quantise_z(b, c):
+            z_codes[b, c] = keep.tile([P, CHUNK], U32, name=f"z_codes{b}_{c}", align_bytes=64)
+            z_sc[b, c] = keep.tile([P, CHUNK], U8, name=f"z_sc{b}_{c}", align_bytes=64)
+            nc.vector.quantize_mx(z_codes[b, c][:].bitcast(FP8X4), z_sc[b, c][:], woven_z[b, c][:])
+
+        factors = {}
+
+        def load_seller(c):
+            factors[c] = big.tile([P, N_TILES, CHUNK], F32, name=f"seller{c}", tag="big")
+            nc.sync.dma_start(
+                factors[c][:], seller[:, c * CHUNK : (c + 1) * CHUNK].rearrange("(i p) m -> p i m", p=P)
+            )
+
+        per_bank = BANK // CHUNK
+
+        def finish(c):
+            for i0 in range(0, N_TILES, per_bank):
+                acc = psum_y.tile([P, per_bank, CHUNK], F32, name="acc_y")
+                for i in range(per_bank):
+                    n_cols = slice((i0 + i) * P, (i0 + i + 1) * P)
+                    for b in range(R_PASSES):
+                        nc.tensor.matmul_mx(
+                            acc[:, i, :],
+                            lhsT=w2_codes[b][:, n_cols].bitcast(FP8X4),
+                            lhsT_scale=w2_sc[b][:, n_cols],
+                            rhs=z_codes[b, c][:].bitcast(FP8X4),
+                            rhs_scale=z_sc[b, c][:],
+                            start=(b == 0),
+                            stop=(b == R_PASSES - 1),
+                        )
+                y = stage.tile([P, per_bank, CHUNK], F32, name="y")
+                nc.vector.tensor_tensor(y[:], acc[:], factors[c][:, i0 : i0 + per_bank, :], MULT)
+                nc.sync.dma_start(
+                    out[i0 * P : (i0 + per_bank) * P, c * CHUNK : (c + 1) * CHUNK].rearrange("(i p) m -> p i m", p=P),
+                    y[:],
+                )
+
+        for i in range(PACK):
+            put_rows(i)
+        for i in range(PACK, R_PASSES * PACK):
+            load_page(i)
+        for b in range(R_PASSES):
+            quantise_w2(b)
+        for c in range(CHUNKS):
+            load_seller(c)
+        for i in range(PACK, R_PASSES * PACK):
+            put_rows(i)
+        units = [(b, c) for c in range(CHUNKS) for b in range(R_PASSES)]
+        for step in range(len(units) + 2):
+            if step < len(units):
+                fetch(*units[step])
+            if step >= 2 and units[step - 2][0] == R_PASSES - 1:
+                finish(units[step - 2][1])
+            if 1 <= step <= len(units):
+                quantise_z(*units[step - 1])

@@ -22,8 +22,8 @@ PACK = 4
 K_PASSES = K // (P * PACK)
 R_PASSES = H // (P * PACK)
 BANK = 512
-CHUNK = 256
-CHUNKS = M // CHUNK
+CHUNKS = ((0, 512), (512, 256), (768, 256))
+SELLER_COLS = 1536
 N_TILES = N // P
 SPARE = 32 - PACK * K_PASSES
 SHIFT_ROWS = 100
@@ -37,10 +37,9 @@ def tile_list_auction_guide_clip_kernel(
     with ExitStack() as ctx:
         keep = ctx.enter_context(tc.tile_pool(name="keep", bufs=1))
         big = ctx.enter_context(tc.tile_pool(name="big", bufs=4))
-        ring = ctx.enter_context(tc.tile_pool(name="ring", bufs=4))
+        ring = ctx.enter_context(tc.tile_pool(name="ring", bufs=3))
         stage = ctx.enter_context(tc.tile_pool(name="stage", bufs=6))
-        psum_h = ctx.enter_context(tc.psum_pool(name="psum_h", bufs=2))
-        psum_y = ctx.enter_context(tc.psum_pool(name="psum_y", bufs=6))
+        psum = ctx.enter_context(tc.psum_pool(name="psum", bufs=8))
 
         idx = keep.tile([P, S // 16], U16, name="idx")
         idx2 = keep.tile([P, S // 16], U16, name="idx2")
@@ -96,25 +95,18 @@ def tile_list_auction_guide_clip_kernel(
         lower_planes(w1p_sc, w1p_packed, H)
 
         wgs_rows = wgs.rearrange("(q t) j -> q t j", t=PACK)
-        wgs_first = keep.tile([P, S], F32, name="wgs_first")
-        wgs_rest = keep.tile([P, (PACK - 1) * S], F32, name="wgs_rest")
+        weights = [keep.tile([P, S], F32, name=f"wgs{t}") for t in range(PACK)]
         pages = [keep.tile([P, T], F32, name=f"page{i}") for i in range(R_PASSES * PACK)]
         page_rows = page0.rearrange("(b p t) c -> b t p c", t=PACK, p=P)
 
         def load_page(i):
             nc.sync.dma_start(pages[i][:], page_rows[i // PACK, i % PACK])
 
-        for q in range(4):
-            nc.sync.dma_start(wgs_first[32 * q : 32 * q + 32, :], wgs_rows[:, 0, :])
         nc.sync.dma_start(idx2[:], offs2)
-        load_page(0)
-        load_page(1)
-        for q in range(4):
-            nc.sync.dma_start(
-                wgs_rest[32 * q : 32 * q + 32, :], wgs_rows[:, 1:, :].rearrange("q t j -> q (t j)")
-            )
-        load_page(2)
-        load_page(3)
+        for t in range(PACK):
+            for q in range(4):
+                nc.sync.dma_start(weights[t][32 * q : 32 * q + 32, :], wgs_rows[:, t, :])
+            load_page(t)
         nc.sync.dma_start(idx3[:], offs3)
         lo = keep.tile([P, R_PASSES, PACK], F32, name="lo")
         hi = keep.tile([P, R_PASSES, PACK], F32, name="hi")
@@ -131,13 +123,16 @@ def tile_list_auction_guide_clip_kernel(
                 tab[last][:].bitcast(U32).indirect(idx[:, half * BANK // 16 : (half + 1) * BANK // 16]),
             )
 
+        h_pairs = []
+
         def put_rows(i):
-            t = i % PACK
-            weight = wgs_first[:] if t == 0 else wgs_rest[:, (t - 1) * S : t * S]
-            h = ring.tile([P, S], F32, name="h", tag="work")
+            weight = weights[i % PACK]
+            if i % 2 == 0:
+                h_pairs.append(keep.tile([P, 2, S], F32, name="h_pair", tag=f"work{i // 2}"))
+            h = h_pairs[i // 2][:, i % 2, :]
             for half in range(S // BANK):
                 cols = slice(half * BANK, (half + 1) * BANK)
-                acc = psum_h.tile([P, BANK], F32, name="acc_h")
+                acc = psum.tile([P, BANK], F32, name="acc")
                 for a in range(K_PASSES):
                     nc.tensor.matmul_mx(
                         acc[:],
@@ -155,93 +150,102 @@ def tile_list_auction_guide_clip_kernel(
                         h[:, cols], weight[:, cols], MULT,
                     )
             if i > 0:
-                nc.vector.tensor_tensor(pages[i][:].indirect(idx2[:]), h[:], weight, MULT)
+                nc.vector.tensor_tensor(pages[i][:].indirect(idx2[:]), h, weight[:], MULT)
 
         w2_codes = [keep.tile([P, N], U32, name=f"w2_codes{b}", align_bytes=64) for b in range(R_PASSES)]
         w2_sc = [keep.tile([P, N], U8, name=f"w2_sc{b}", align_bytes=64) for b in range(R_PASSES)]
 
         def quantise_w2(b):
-            raw = keep.tile([P, PACK, N], F32, name="w2_raw")
-            nc.sync.dma_start(raw[:], w2[b * P * PACK : (b + 1) * P * PACK, :].rearrange("(p t) n -> p t n", t=PACK))
-            woven = keep.tile([P, N * PACK], BF16, name="w2_woven", align_bytes=64)
-            nc.scalar.copy(
-                woven[:].rearrange("p (c i t) -> p c t i", t=PACK, i=4),
-                raw[:].rearrange("p t (c i) -> p c t i", i=4),
-            )
+            rows = w2[b * P * PACK : (b + 1) * P * PACK, :].rearrange("(p t) n -> p t n", t=PACK)
             for n0, n1 in ((0, 512), (512, N)):
-                nc.vector.quantize_mx(
-                    w2_codes[b][:, n0:n1].bitcast(FP8X4), w2_sc[b][:, n0:n1], woven[:, PACK * n0 : PACK * n1]
+                raw = big.tile([P, PACK, n1 - n0], F32, name="w2_raw", tag="big")
+                nc.sync.dma_start(raw[:], rows[:, :, n0:n1])
+                woven = ring.tile([P, (n1 - n0) * PACK], BF16, name="woven", align_bytes=64)
+                nc.scalar.copy(
+                    woven[:].rearrange("p (c i t) -> p c t i", t=PACK, i=2),
+                    raw[:].rearrange("p t (c i) -> p c t i", i=2),
                 )
+                nc.vector.quantize_mx(w2_codes[b][:, n0:n1].bitcast(FP8X4), w2_sc[b][:, n0:n1], woven[:])
 
-        z_codes = {}
-        z_sc = {}
         woven_z = {}
 
         def fetch(b, c):
-            x = ring.tile([P, PACK, CHUNK], F32, name="x", tag="work")
-            offsets = idx3[:, c * CHUNK // 16 : (c + 1) * CHUNK // 16]
+            m0, width = CHUNKS[c]
+            x = keep.tile([P, PACK, width], F32, name="x", tag=f"work{3 if b == 0 else c}")
+            offsets = idx3[:, m0 // 16 : (m0 + width) // 16]
             for t in range(PACK):
                 nc.vector.tensor_copy(x[:, t, :], pages[b * PACK + t][:].indirect(offsets))
             for t in range(PACK):
                 nc.vector.tensor_scalar(x[:, t, :], x[:, t, :], lo[:, b, t : t + 1], hi[:, b, t : t + 1], MAX, MIN)
-            woven_z[b, c] = ring.tile([P, CHUNK * PACK], BF16, name="z_woven", align_bytes=64)
+            woven_z[b, c] = ring.tile([P, width * PACK], BF16, name="woven", align_bytes=64)
             nc.scalar.copy(
-                woven_z[b, c][:].rearrange("p (c i t) -> p c t i", t=PACK, i=4),
-                x[:].rearrange("p t (c i) -> p c t i", i=4),
+                woven_z[b, c][:].rearrange("p (c i t) -> p c t i", t=PACK, i=2),
+                x[:].rearrange("p t (c i) -> p c t i", i=2),
             )
-
-        def quantise_z(b, c):
-            z_codes[b, c] = keep.tile([P, CHUNK], U32, name=f"z_codes{b}_{c}", align_bytes=64)
-            z_sc[b, c] = keep.tile([P, CHUNK], U8, name=f"z_sc{b}_{c}", align_bytes=64)
-            nc.vector.quantize_mx(z_codes[b, c][:].bitcast(FP8X4), z_sc[b, c][:], woven_z[b, c][:])
 
         factors = {}
 
         def load_seller(c):
-            factors[c] = big.tile([P, N_TILES, CHUNK], F32, name=f"seller{c}", tag="big")
-            nc.sync.dma_start(
-                factors[c][:], seller[:, c * CHUNK : (c + 1) * CHUNK].rearrange("(i p) m -> p i m", p=P)
-            )
+            m0, width = CHUNKS[c]
+            per_load = SELLER_COLS // width
+            for i0 in range(0, N_TILES, per_load):
+                tile = big.tile([P, per_load, width], F32, name=f"seller{c}_{i0}", tag="big")
+                nc.sync.dma_start(
+                    tile[:], seller[i0 * P : (i0 + per_load) * P, m0 : m0 + width].rearrange("(i p) m -> p i m", p=P)
+                )
+                for i in range(per_load):
+                    factors[c, i0 + i] = (tile, i)
 
-        per_bank = BANK // CHUNK
+        banks = {}
 
-        def finish(c):
+        def multiply(b, c):
+            width = CHUNKS[c][1]
+            per_bank = BANK // width
+            codes = keep.tile([P, width], U32, name=f"z_codes{b}_{c}", align_bytes=64)
+            scales = keep.tile([P, width], U8, name=f"z_sc{b}_{c}", align_bytes=64)
+            nc.vector.quantize_mx(codes[:].bitcast(FP8X4), scales[:], woven_z[b, c][:])
             for i0 in range(0, N_TILES, per_bank):
-                acc = psum_y.tile([P, per_bank, CHUNK], F32, name="acc_y")
+                if b == 0:
+                    banks[c, i0] = psum.tile([P, per_bank, width], F32, name="acc")
                 for i in range(per_bank):
                     n_cols = slice((i0 + i) * P, (i0 + i + 1) * P)
-                    for b in range(R_PASSES):
-                        nc.tensor.matmul_mx(
-                            acc[:, i, :],
-                            lhsT=w2_codes[b][:, n_cols].bitcast(FP8X4),
-                            lhsT_scale=w2_sc[b][:, n_cols],
-                            rhs=z_codes[b, c][:].bitcast(FP8X4),
-                            rhs_scale=z_sc[b, c][:],
-                            start=(b == 0),
-                            stop=(b == R_PASSES - 1),
-                        )
-                y = stage.tile([P, per_bank, CHUNK], F32, name="y")
-                nc.vector.tensor_tensor(y[:], acc[:], factors[c][:, i0 : i0 + per_bank, :], MULT)
+                    nc.tensor.matmul_mx(
+                        banks[c, i0][:, i, :],
+                        lhsT=w2_codes[b][:, n_cols].bitcast(FP8X4),
+                        lhsT_scale=w2_sc[b][:, n_cols],
+                        rhs=codes[:].bitcast(FP8X4),
+                        rhs_scale=scales[:],
+                        start=(b == 0 and i == 0),
+                        stop=(b == R_PASSES - 1 and i == per_bank - 1),
+                    )
+
+        def finish(c):
+            m0, width = CHUNKS[c]
+            per_bank = BANK // width
+            for i0 in range(0, N_TILES, per_bank):
+                tile, i = factors[c, i0]
+                y = stage.tile([P, per_bank, width], F32, name="y")
+                nc.vector.tensor_tensor(y[:], banks[c, i0][:], tile[:, i : i + per_bank, :], MULT)
                 nc.sync.dma_start(
-                    out[i0 * P : (i0 + per_bank) * P, c * CHUNK : (c + 1) * CHUNK].rearrange("(i p) m -> p i m", p=P),
-                    y[:],
+                    out[i0 * P : (i0 + per_bank) * P, m0 : m0 + width].rearrange("(i p) m -> p i m", p=P), y[:]
                 )
 
         for i in range(PACK):
             put_rows(i)
-        for i in range(PACK, R_PASSES * PACK):
-            load_page(i)
         for b in range(R_PASSES):
             quantise_w2(b)
-        for c in range(CHUNKS):
+            load_page(PACK + b)
+        for i in range(PACK + R_PASSES, R_PASSES * PACK):
+            load_page(i)
+        for c in range(len(CHUNKS)):
             load_seller(c)
         for i in range(PACK, R_PASSES * PACK):
             put_rows(i)
-        units = [(b, c) for c in range(CHUNKS) for b in range(R_PASSES)]
+        units = [(b, c) for c in range(len(CHUNKS)) for b in range(R_PASSES)]
         for step in range(len(units) + 2):
             if step < len(units):
                 fetch(*units[step])
             if step >= 2 and units[step - 2][0] == R_PASSES - 1:
                 finish(units[step - 2][1])
             if 1 <= step <= len(units):
-                quantise_z(*units[step - 1])
+                multiply(*units[step - 1])

@@ -46,66 +46,70 @@ def tile_list_auction_guide_clip_kernel(
         idx3 = keep.tile([P, M // 16], U16, name="idx3")
 
         tab_sc = keep.tile([P, T], U8, name="tab_sc", align_bytes=64)
-        w1_sc = keep.tile([P, H], U8, name="w1_sc", align_bytes=64)
+        w1_sc = keep.tile([P, K_PASSES, H], U8, name="w1_sc", align_bytes=64)
         v_sc = keep.tile([P, K_PASSES * S], U8, name="v_sc", align_bytes=64)
-        w1p_sc = keep.tile([P, K_PASSES * H], U8, name="w1p_sc", align_bytes=64)
+        nc.gpsimd.memset(w1_sc[:].bitcast(I32), 0)
         for q in range(4):
             nc.vector.memset(tab_sc[32 * q : 32 * q + SPARE, :].bitcast(I32), 0)
-        for q in range(4):
-            nc.gpsimd.memset(w1_sc[32 * q : 32 * q + SPARE, :].bitcast(I32), 0)
         nc.gpsimd.memset(v_sc[96:P, :].bitcast(I32), 0)
-        nc.gpsimd.memset(w1p_sc[96:P, :].bitcast(I32), 0)
 
-        nc.sync.dma_start(idx[:], offs)
-        for packed, rows in ((tab_sc, tab_scales), (w1_sc, w1_scales)):
-            for q in range(4):
-                nc.scalar.dma_start(
-                    packed[32 * q + SPARE : 32 * q + 32, :].bitcast(I32),
-                    rows[:, 4 * q : 4 * q + 4, :].bitcast(I32),
-                )
-        w1_raw = [keep.tile([P, 2 * H], U8, name=f"w1_raw{a}", align_bytes=64) for a in range(K_PASSES)]
-        for a in range(K_PASSES):
-            nc.sync.dma_start(w1_raw[a][:].bitcast(I32), w1_words[a].bitcast(I32))
         tab = [big.tile([P, T], I32, name=f"tab{a}", tag="big") for a in range(K_PASSES)]
-        for a in range(K_PASSES):
+
+        def load_tab(a):
             nc.sync.dma_start(tab[a][:], tab_words[a].rearrange("p t i -> p (t i)").bitcast(I32))
-
-        def lower_planes(planes, packed, width):
-            for a in range(K_PASSES):
-                first = SPARE + PACK * a
-                nc.scalar.dma_start(
-                    planes[0:SHIFT_ROWS, a * width : (a + 1) * width].bitcast(I32),
-                    packed[first : first + SHIFT_ROWS, :].bitcast(I32),
-                )
-
-        w1p = [keep.tile([P, 2 * H], U8, name=f"w1p{a}", align_bytes=64) for a in range(K_PASSES)]
-        for a in range(K_PASSES):
-            nc.vector.tensor_copy(
-                w1p[a][:].bitcast(U16).rearrange("p (b t c i) -> p b c t i", b=R_PASSES, t=PACK, i=8),
-                w1_raw[a][:].bitcast(U16).rearrange("p (b c i t) -> p b c t i", b=R_PASSES, t=PACK, i=8),
-            )
-        v_packed = keep.tile([P, S], U8, name="v_packed", align_bytes=64)
-        nc.vector.tensor_copy(v_packed[:], tab_sc[:].indirect(idx[:]))
-        lower_planes(v_sc, v_packed, S)
-        w1p_packed = keep.tile([P, H], U8, name="w1p_packed", align_bytes=64)
-        nc.vector.tensor_copy(
-            w1p_packed[:].rearrange("p (b t c i) -> p b c t i", b=R_PASSES, t=PACK, i=16),
-            w1_sc[:].rearrange("p (b c i t) -> p b c t i", b=R_PASSES, t=PACK, i=16),
-        )
-        lower_planes(w1p_sc, w1p_packed, H)
 
         wgs_rows = wgs.rearrange("(q t) j -> q t j", t=PACK)
         weights = [keep.tile([P, S], F32, name=f"wgs{t}") for t in range(PACK)]
         pages = [keep.tile([P, T], F32, name=f"page{i}") for i in range(R_PASSES * PACK)]
         page_rows = page0.rearrange("(b p t) c -> b t p c", t=PACK, p=P)
 
+        def load_wgs(t):
+            for q in range(4):
+                nc.sync.dma_start(weights[t][32 * q : 32 * q + 32, :], wgs_rows[:, t, :])
+
         def load_page(i):
             nc.sync.dma_start(pages[i][:], page_rows[i // PACK, i % PACK])
 
+        nc.sync.dma_start(idx[:], offs)
+        w1_raw = keep.tile([P, K_PASSES, 2 * H], U8, name="w1_raw", align_bytes=64)
+        nc.sync.dma_start(w1_raw[:].bitcast(I32), w1_words.rearrange("a p c -> p a c").bitcast(I32))
+        load_tab(0)
+        for q in range(4):
+            nc.sync.dma_start(
+                tab_sc[32 * q + SPARE : 32 * q + 32, :].bitcast(I32),
+                tab_scales[:, 4 * q : 4 * q + 4, :].bitcast(I32),
+            )
+        load_tab(1)
+        for q in range(4):
+            nc.sync.dma_start(
+                w1_sc[32 * q : 32 * q + 4, :, :].bitcast(I32),
+                w1_scales[:, 4 * q : 4 * q + 4, :].rearrange("a r c -> r a c").bitcast(I32),
+            )
+        load_tab(2)
         nc.sync.dma_start(idx2[:], offs2)
-        for t in range(PACK):
-            for q in range(4):
-                nc.sync.dma_start(weights[t][32 * q : 32 * q + 32, :], wgs_rows[:, t, :])
+        load_wgs(0)
+        load_page(0)
+
+        w1p = keep.tile([P, K_PASSES * R_PASSES, 2 * P * PACK], U8, name="w1p", align_bytes=64)
+        w1p_sc = keep.tile([P, K_PASSES * R_PASSES, P * PACK], U8, name="w1p_sc", align_bytes=64)
+        nc.vector.tensor_copy(
+            w1p[:].bitcast(U16).rearrange("p g (t c i) -> p g c t i", t=PACK, i=8),
+            w1_raw[:].bitcast(U16).rearrange("p a (b c i t) -> p (a b) c t i", b=R_PASSES, t=PACK, i=8),
+        )
+        v_packed = keep.tile([P, S], U8, name="v_packed", align_bytes=64)
+        nc.vector.tensor_copy(v_packed[:], tab_sc[:].indirect(idx[:]))
+        for a in range(K_PASSES):
+            first = SPARE + PACK * a
+            nc.sync.dma_start(
+                v_sc[0:SHIFT_ROWS, a * S : (a + 1) * S].bitcast(I32),
+                v_packed[first : first + SHIFT_ROWS, :].bitcast(I32),
+            )
+        nc.vector.tensor_copy(
+            w1p_sc[:].rearrange("p g (t c i) -> p g c t i", t=PACK, i=16),
+            w1_sc[:].rearrange("p a (b c i t) -> p (a b) c t i", b=R_PASSES, t=PACK, i=16),
+        )
+        for t in range(1, PACK):
+            load_wgs(t)
             load_page(t)
         nc.sync.dma_start(idx3[:], offs3)
         lo = keep.tile([P, R_PASSES, PACK], F32, name="lo")
@@ -126,7 +130,8 @@ def tile_list_auction_guide_clip_kernel(
         h_pairs = []
 
         def put_rows(i):
-            weight = weights[i % PACK]
+            b, t = divmod(i, PACK)
+            weight = weights[t]
             if i % 2 == 0:
                 h_pairs.append(keep.tile([P, 2, S], F32, name="h_pair", tag=f"work{i // 2}"))
             h = h_pairs[i // 2][:, i % 2, :]
@@ -136,8 +141,8 @@ def tile_list_auction_guide_clip_kernel(
                 for a in range(K_PASSES):
                     nc.tensor.matmul_mx(
                         acc[:],
-                        lhsT=w1p[a][:, 2 * P * i : 2 * P * (i + 1)].bitcast(FP4X4),
-                        lhsT_scale=w1p_sc[:, a * H + P * i : a * H + P * (i + 1)],
+                        lhsT=w1p[:, a * R_PASSES + b, 2 * P * t : 2 * P * (t + 1)].bitcast(FP4X4),
+                        lhsT_scale=w1p_sc[:, a * R_PASSES + b, P * t : P * (t + 1)],
                         rhs=v[a][:, cols].bitcast(FP8X4),
                         rhs_scale=v_sc[:, a * S + half * BANK : a * S + (half + 1) * BANK],
                         start=(a == 0),

@@ -19,14 +19,17 @@ MIN = mybir.AluOpType.min
 
 P = 128
 PACK = 4
+QUADRANTS = 4
+PER_COLUMN = 16
 K_PASSES = K // (P * PACK)
 R_PASSES = H // (P * PACK)
+ROW_SETS = R_PASSES * PACK
 BANK = 512
-CHUNKS = ((0, 512), (512, 256), (768, 256))
-SELLER_COLS = 1536
 N_TILES = N // P
-SPARE = 32 - PACK * K_PASSES
-SHIFT_ROWS = 100
+CHUNKS = ((0, 512), (512, 256), (768, 256))
+W2_PIECES = ((0, 512), (512, N))
+SELLER_COLS = N_TILES * M // 4
+MOVED_ROWS = 112
 
 
 def tile_list_auction_guide_clip_kernel(
@@ -37,79 +40,81 @@ def tile_list_auction_guide_clip_kernel(
     with ExitStack() as ctx:
         keep = ctx.enter_context(tc.tile_pool(name="keep", bufs=1))
         big = ctx.enter_context(tc.tile_pool(name="big", bufs=4))
-        ring = ctx.enter_context(tc.tile_pool(name="ring", bufs=3))
-        stage = ctx.enter_context(tc.tile_pool(name="stage", bufs=6))
+        ring = ctx.enter_context(tc.tile_pool(name="ring", bufs=4))
+        stage = ctx.enter_context(tc.tile_pool(name="stage", bufs=8))
         psum = ctx.enter_context(tc.psum_pool(name="psum", bufs=8))
 
-        idx = keep.tile([P, S // 16], U16, name="idx")
-        idx2 = keep.tile([P, S // 16], U16, name="idx2")
-        idx3 = keep.tile([P, M // 16], U16, name="idx3")
+        idx = keep.tile([P, S // PER_COLUMN], U16, name="idx")
+        idx2 = keep.tile([P, S // PER_COLUMN], U16, name="idx2")
+        idx3 = keep.tile([P, M // PER_COLUMN], U16, name="idx3")
+
+        def entries(offsets, first, count):
+            return offsets[:, first // PER_COLUMN : (first + count) // PER_COLUMN]
 
         tab_sc = keep.tile([P, T], U8, name="tab_sc", align_bytes=64)
-        w1_sc = keep.tile([P, K_PASSES, H], U8, name="w1_sc", align_bytes=64)
-        v_sc = keep.tile([P, K_PASSES * S], U8, name="v_sc", align_bytes=64)
+        w1_sc = keep.tile([P, H], U8, name="w1_sc", align_bytes=64)
+        v_sc = [keep.tile([P, S], U8, name=f"v_sc{a}", align_bytes=64) for a in range(K_PASSES)]
+        w1p_sc = [keep.tile([P, H], U8, name=f"w1p_sc{a}", align_bytes=64) for a in range(K_PASSES)]
         nc.gpsimd.memset(w1_sc[:].bitcast(I32), 0)
-        for q in range(4):
-            nc.vector.memset(tab_sc[32 * q : 32 * q + SPARE, :].bitcast(I32), 0)
-        nc.gpsimd.memset(v_sc[96:P, :].bitcast(I32), 0)
+        nc.gpsimd.memset(tab_sc[:].bitcast(I32), 0)
+        for scales in (w1p_sc, v_sc):
+            for a in range(1, K_PASSES):
+                nc.vector.memset(scales[a][P - 32 : P, :].bitcast(I32), 0)
 
         tab = [big.tile([P, T], I32, name=f"tab{a}", tag="big") for a in range(K_PASSES)]
 
         def load_tab(a):
             nc.sync.dma_start(tab[a][:], tab_words[a].rearrange("p t i -> p (t i)").bitcast(I32))
 
-        wgs_rows = wgs.rearrange("(q t) j -> q t j", t=PACK)
+        wgs_rows = wgs.rearrange("(u t) j -> u t j", t=PACK)
         weights = [keep.tile([P, S], F32, name=f"wgs{t}") for t in range(PACK)]
-        pages = [keep.tile([P, T], F32, name=f"page{i}") for i in range(R_PASSES * PACK)]
+        pages = [keep.tile([P, T], F32, name=f"page{i}") for i in range(ROW_SETS)]
         page_rows = page0.rearrange("(b p t) c -> b t p c", t=PACK, p=P)
 
-        def load_wgs(t):
-            for q in range(4):
-                nc.sync.dma_start(weights[t][32 * q : 32 * q + 32, :], wgs_rows[:, t, :])
+        def load_wgs(t, queue):
+            for q in range(QUADRANTS):
+                queue.dma_start(weights[t][32 * q : 32 * q + 32, :], wgs_rows[:, t, :])
 
         def load_page(i):
             nc.sync.dma_start(pages[i][:], page_rows[i // PACK, i % PACK])
 
         nc.sync.dma_start(idx[:], offs)
+        load_tab(0)
         w1_raw = keep.tile([P, K_PASSES, 2 * H], U8, name="w1_raw", align_bytes=64)
         nc.sync.dma_start(w1_raw[:].bitcast(I32), w1_words.rearrange("a p c -> p a c").bitcast(I32))
-        load_tab(0)
-        for q in range(4):
-            nc.sync.dma_start(
-                tab_sc[32 * q + SPARE : 32 * q + 32, :].bitcast(I32),
-                tab_scales[:, 4 * q : 4 * q + 4, :].bitcast(I32),
-            )
+        load_wgs(0, nc.gpsimd)
+        for packed, source in ((w1_sc, w1_scales), (tab_sc, tab_scales)):
+            for q in range(QUADRANTS):
+                nc.sync.dma_start(
+                    packed[32 * q : 32 * q + 4 * K_PASSES, :].bitcast(I32),
+                    source[:, 4 * q : 4 * q + 4, :].bitcast(I32),
+                )
         load_tab(1)
-        for q in range(4):
-            nc.sync.dma_start(
-                w1_sc[32 * q : 32 * q + 4, :, :].bitcast(I32),
-                w1_scales[:, 4 * q : 4 * q + 4, :].rearrange("a r c -> r a c").bitcast(I32),
-            )
-        load_tab(2)
         nc.sync.dma_start(idx2[:], offs2)
-        load_wgs(0)
+        load_tab(2)
         load_page(0)
 
-        w1p = keep.tile([P, K_PASSES * R_PASSES, 2 * P * PACK], U8, name="w1p", align_bytes=64)
-        w1p_sc = keep.tile([P, K_PASSES * R_PASSES, P * PACK], U8, name="w1p_sc", align_bytes=64)
+        def lower_scale_rows(scales):
+            for a in range(1, K_PASSES):
+                nc.sync.dma_start(
+                    scales[a][0:MOVED_ROWS, :].bitcast(I32),
+                    scales[0][4 * a : 4 * a + MOVED_ROWS, :].bitcast(I32),
+                )
+
         nc.vector.tensor_copy(
-            w1p[:].bitcast(U16).rearrange("p g (t c i) -> p g c t i", t=PACK, i=8),
-            w1_raw[:].bitcast(U16).rearrange("p a (b c i t) -> p (a b) c t i", b=R_PASSES, t=PACK, i=8),
+            w1p_sc[0][:].rearrange("p (b t c e) -> p b c t e", b=R_PASSES, t=PACK, e=16),
+            w1_sc[:].rearrange("p (b c e t) -> p b c t e", b=R_PASSES, t=PACK, e=16),
         )
-        v_packed = keep.tile([P, S], U8, name="v_packed", align_bytes=64)
-        nc.vector.tensor_copy(v_packed[:], tab_sc[:].indirect(idx[:]))
-        for a in range(K_PASSES):
-            first = SPARE + PACK * a
-            nc.sync.dma_start(
-                v_sc[0:SHIFT_ROWS, a * S : (a + 1) * S].bitcast(I32),
-                v_packed[first : first + SHIFT_ROWS, :].bitcast(I32),
-            )
+        lower_scale_rows(w1p_sc)
+        nc.vector.tensor_copy(v_sc[0][:], tab_sc[:].indirect(idx[:]))
+        lower_scale_rows(v_sc)
+        w1p = keep.tile([P, K_PASSES * R_PASSES, 2 * P * PACK], U8, name="w1p", align_bytes=64)
         nc.vector.tensor_copy(
-            w1p_sc[:].rearrange("p g (t c i) -> p g c t i", t=PACK, i=16),
-            w1_sc[:].rearrange("p a (b c i t) -> p (a b) c t i", b=R_PASSES, t=PACK, i=16),
+            w1p[:].bitcast(U16).rearrange("p g (t c e) -> p g c t e", t=PACK, e=8),
+            w1_raw[:].bitcast(U16).rearrange("p a (b c e t) -> p (a b) c t e", b=R_PASSES, t=PACK, e=8),
         )
         for t in range(1, PACK):
-            load_wgs(t)
+            load_wgs(t, nc.sync)
             load_page(t)
         nc.sync.dma_start(idx3[:], offs3)
         lo = keep.tile([P, R_PASSES, PACK], F32, name="lo")
@@ -118,88 +123,87 @@ def tile_list_auction_guide_clip_kernel(
         nc.sync.dma_start(hi[:], ceiling.rearrange("(b p t) -> p b t", p=P, t=PACK))
 
         v = [keep.tile([P, S], U32, name=f"v{a}", align_bytes=64) for a in range(K_PASSES)]
-        for a in range(K_PASSES - 1):
-            nc.vector.tensor_copy(v[a][:], tab[a][:].bitcast(U32).indirect(idx[:]))
         last = K_PASSES - 1
-        for half in range(S // BANK):
+        for a in range(last):
+            nc.vector.tensor_copy(v[a][:], tab[a][:].bitcast(U32).indirect(idx[:]))
+        for j0 in range(0, S, BANK):
             nc.vector.tensor_copy(
-                v[last][:, half * BANK : (half + 1) * BANK],
-                tab[last][:].bitcast(U32).indirect(idx[:, half * BANK // 16 : (half + 1) * BANK // 16]),
+                v[last][:, j0 : j0 + BANK], tab[last][:].bitcast(U32).indirect(entries(idx, j0, BANK))
             )
 
         h_pairs = []
 
         def put_rows(i):
             b, t = divmod(i, PACK)
-            weight = weights[t]
             if i % 2 == 0:
                 h_pairs.append(keep.tile([P, 2, S], F32, name="h_pair", tag=f"work{i // 2}"))
             h = h_pairs[i // 2][:, i % 2, :]
-            for half in range(S // BANK):
-                cols = slice(half * BANK, (half + 1) * BANK)
+            for j0 in range(0, S, BANK):
+                cols = slice(j0, j0 + BANK)
                 acc = psum.tile([P, BANK], F32, name="acc")
                 for a in range(K_PASSES):
                     nc.tensor.matmul_mx(
                         acc[:],
                         lhsT=w1p[:, a * R_PASSES + b, 2 * P * t : 2 * P * (t + 1)].bitcast(FP4X4),
-                        lhsT_scale=w1p_sc[:, a * R_PASSES + b, P * t : P * (t + 1)],
+                        lhsT_scale=w1p_sc[a][:, P * i : P * (i + 1)],
                         rhs=v[a][:, cols].bitcast(FP8X4),
-                        rhs_scale=v_sc[:, a * S + half * BANK : a * S + (half + 1) * BANK],
+                        rhs_scale=v_sc[a][:, cols],
                         start=(a == 0),
-                        stop=(a == K_PASSES - 1),
+                        stop=(a == last),
                     )
                 nc.scalar.copy(h[:, cols], acc[:])
                 if i == 0:
                     nc.vector.tensor_tensor(
-                        pages[i][:].indirect(idx2[:, half * BANK // 16 : (half + 1) * BANK // 16]),
-                        h[:, cols], weight[:, cols], MULT,
+                        pages[i][:].indirect(entries(idx2, j0, BANK)), h[:, cols], weights[t][:, cols], MULT
                     )
             if i > 0:
-                nc.vector.tensor_tensor(pages[i][:].indirect(idx2[:]), h, weight[:], MULT)
+                nc.vector.tensor_tensor(pages[i][:].indirect(idx2[:]), h, weights[t][:], MULT)
+
+        def interleave(rows):
+            woven = ring.tile([P, rows.shape[2] * PACK], BF16, name="woven", align_bytes=64)
+            nc.scalar.copy(
+                woven[:].rearrange("p (c e t) -> p c t e", t=PACK, e=2),
+                rows.rearrange("p t (c e) -> p c t e", e=2),
+            )
+            return woven
 
         w2_codes = [keep.tile([P, N], U32, name=f"w2_codes{b}", align_bytes=64) for b in range(R_PASSES)]
         w2_sc = [keep.tile([P, N], U8, name=f"w2_sc{b}", align_bytes=64) for b in range(R_PASSES)]
 
         def quantise_w2(b):
-            rows = w2[b * P * PACK : (b + 1) * P * PACK, :].rearrange("(p t) n -> p t n", t=PACK)
-            for n0, n1 in ((0, 512), (512, N)):
-                raw = big.tile([P, PACK, n1 - n0], F32, name="w2_raw", tag="big")
-                nc.sync.dma_start(raw[:], rows[:, :, n0:n1])
-                woven = ring.tile([P, (n1 - n0) * PACK], BF16, name="woven", align_bytes=64)
-                nc.scalar.copy(
-                    woven[:].rearrange("p (c i t) -> p c t i", t=PACK, i=2),
-                    raw[:].rearrange("p t (c i) -> p c t i", i=2),
-                )
-                nc.vector.quantize_mx(w2_codes[b][:, n0:n1].bitcast(FP8X4), w2_sc[b][:, n0:n1], woven[:])
+            w2_pass = w2[b * P * PACK : (b + 1) * P * PACK, :].rearrange("(p t) n -> p t n", t=PACK)
+            for col0, col1 in W2_PIECES:
+                raw = big.tile([P, PACK, col1 - col0], F32, name="w2_raw", tag="big")
+                nc.sync.dma_start(raw[:], w2_pass[:, :, col0:col1])
+                woven = interleave(raw[:])
+                nc.vector.quantize_mx(w2_codes[b][:, col0:col1].bitcast(FP8X4), w2_sc[b][:, col0:col1], woven[:])
 
-        woven_z = {}
+        z_woven = {}
 
-        def fetch(b, c):
-            m0, width = CHUNKS[c]
-            x = keep.tile([P, PACK, width], F32, name="x", tag=f"work{3 if b == 0 else c}")
-            offsets = idx3[:, m0 // 16 : (m0 + width) // 16]
+        def fetch(b, chunks, pair):
+            first = CHUNKS[chunks[0]][0]
+            count = sum(CHUNKS[c][1] for c in chunks)
+            x = keep.tile([P, PACK, count], F32, name="x", tag=f"work{pair}")
             for t in range(PACK):
-                nc.vector.tensor_copy(x[:, t, :], pages[b * PACK + t][:].indirect(offsets))
+                nc.vector.tensor_copy(x[:, t, :], pages[b * PACK + t][:].indirect(entries(idx3, first, count)))
             for t in range(PACK):
                 nc.vector.tensor_scalar(x[:, t, :], x[:, t, :], lo[:, b, t : t + 1], hi[:, b, t : t + 1], MAX, MIN)
-            woven_z[b, c] = ring.tile([P, width * PACK], BF16, name="woven", align_bytes=64)
-            nc.scalar.copy(
-                woven_z[b, c][:].rearrange("p (c i t) -> p c t i", t=PACK, i=2),
-                x[:].rearrange("p t (c i) -> p c t i", i=2),
-            )
+            for c in chunks:
+                m0, width = CHUNKS[c]
+                z_woven[b, c] = interleave(x[:, :, m0 - first : m0 - first + width])
 
         factors = {}
 
         def load_seller(c):
             m0, width = CHUNKS[c]
             per_load = SELLER_COLS // width
-            for i0 in range(0, N_TILES, per_load):
-                tile = big.tile([P, per_load, width], F32, name=f"seller{c}_{i0}", tag="big")
+            for n0 in range(0, N_TILES, per_load):
+                tile = big.tile([P, per_load, width], F32, name=f"seller{c}_{n0}", tag="big")
                 nc.sync.dma_start(
-                    tile[:], seller[i0 * P : (i0 + per_load) * P, m0 : m0 + width].rearrange("(i p) m -> p i m", p=P)
+                    tile[:], seller[n0 * P : (n0 + per_load) * P, m0 : m0 + width].rearrange("(n p) m -> p n m", p=P)
                 )
-                for i in range(per_load):
-                    factors[c, i0 + i] = (tile, i)
+                for n in range(per_load):
+                    factors[c, n0 + n] = (tile, n)
 
         banks = {}
 
@@ -207,32 +211,32 @@ def tile_list_auction_guide_clip_kernel(
             width = CHUNKS[c][1]
             per_bank = BANK // width
             codes = keep.tile([P, width], U32, name=f"z_codes{b}_{c}", align_bytes=64)
-            scales = keep.tile([P, width], U8, name=f"z_sc{b}_{c}", align_bytes=64)
-            nc.vector.quantize_mx(codes[:].bitcast(FP8X4), scales[:], woven_z[b, c][:])
-            for i0 in range(0, N_TILES, per_bank):
+            z_sc = keep.tile([P, width], U8, name=f"z_sc{b}_{c}", align_bytes=64)
+            nc.vector.quantize_mx(codes[:].bitcast(FP8X4), z_sc[:], z_woven[b, c][:])
+            for n0 in range(0, N_TILES, per_bank):
                 if b == 0:
-                    banks[c, i0] = psum.tile([P, per_bank, width], F32, name="acc")
-                for i in range(per_bank):
-                    n_cols = slice((i0 + i) * P, (i0 + i + 1) * P)
+                    banks[c, n0] = psum.tile([P, per_bank, width], F32, name="acc")
+                for n in range(per_bank):
+                    n_cols = slice((n0 + n) * P, (n0 + n + 1) * P)
                     nc.tensor.matmul_mx(
-                        banks[c, i0][:, i, :],
+                        banks[c, n0][:, n, :],
                         lhsT=w2_codes[b][:, n_cols].bitcast(FP8X4),
                         lhsT_scale=w2_sc[b][:, n_cols],
                         rhs=codes[:].bitcast(FP8X4),
-                        rhs_scale=scales[:],
-                        start=(b == 0 and i == 0),
-                        stop=(b == R_PASSES - 1 and i == per_bank - 1),
+                        rhs_scale=z_sc[:],
+                        start=(b == 0 and n == 0),
+                        stop=(b == R_PASSES - 1 and n == per_bank - 1),
                     )
 
         def finish(c):
             m0, width = CHUNKS[c]
             per_bank = BANK // width
-            for i0 in range(0, N_TILES, per_bank):
-                tile, i = factors[c, i0]
+            for n0 in range(0, N_TILES, per_bank):
+                tile, n = factors[c, n0]
                 y = stage.tile([P, per_bank, width], F32, name="y")
-                nc.vector.tensor_tensor(y[:], banks[c, i0][:], tile[:, i : i + per_bank, :], MULT)
+                nc.vector.tensor_tensor(y[:], banks[c, n0][:], tile[:, n : n + per_bank, :], MULT)
                 nc.sync.dma_start(
-                    out[i0 * P : (i0 + per_bank) * P, m0 : m0 + width].rearrange("(i p) m -> p i m", p=P), y[:]
+                    out[n0 * P : (n0 + per_bank) * P, m0 : m0 + width].rearrange("(n p) m -> p n m", p=P), y[:]
                 )
 
         for i in range(PACK):
@@ -240,17 +244,25 @@ def tile_list_auction_guide_clip_kernel(
         for b in range(R_PASSES):
             quantise_w2(b)
             load_page(PACK + b)
-        for i in range(PACK + R_PASSES, R_PASSES * PACK):
+        for i in range(PACK + R_PASSES, ROW_SETS):
             load_page(i)
         for c in range(len(CHUNKS)):
             load_seller(c)
-        for i in range(PACK, R_PASSES * PACK):
+        for i in range(PACK, ROW_SETS):
             put_rows(i)
-        units = [(b, c) for c in range(len(CHUNKS)) for b in range(R_PASSES)]
-        for step in range(len(units) + 2):
-            if step < len(units):
-                fetch(*units[step])
-            if step >= 2 and units[step - 2][0] == R_PASSES - 1:
-                finish(units[step - 2][1])
-            if 1 <= step <= len(units):
-                multiply(*units[step - 1])
+
+        h_last = ROW_SETS // 2 - 1
+        fetch(0, (0,), h_last)
+        fetch(1, (0,), h_last - 1)
+        multiply(0, 0)
+        fetch(0, (1, 2), h_last)
+        multiply(1, 0)
+        fetch(1, (1,), h_last - 1)
+        finish(0)
+        multiply(0, 1)
+        fetch(1, (2,), h_last)
+        multiply(1, 1)
+        multiply(0, 2)
+        finish(1)
+        multiply(1, 2)
+        finish(2)

@@ -30,6 +30,7 @@ CHUNKS = ((0, 512), (512, 256), (768, 256))
 W2_PIECES = ((0, 512), (512, N))
 SELLER_COLS = N_TILES * M // 4
 MOVED_ROWS = 112
+LEAD = 256
 
 
 def tile_list_auction_guide_clip_kernel(
@@ -42,7 +43,7 @@ def tile_list_auction_guide_clip_kernel(
         big = ctx.enter_context(tc.tile_pool(name="big", bufs=4))
         ring = ctx.enter_context(tc.tile_pool(name="ring", bufs=4))
         stage = ctx.enter_context(tc.tile_pool(name="stage", bufs=8))
-        psum = ctx.enter_context(tc.psum_pool(name="psum", bufs=8))
+        psum = ctx.enter_context(tc.psum_pool(name="psum", bufs=1))
 
         idx = keep.tile([P, S // PER_COLUMN], U16, name="idx")
         idx2 = keep.tile([P, S // PER_COLUMN], U16, name="idx2")
@@ -51,13 +52,13 @@ def tile_list_auction_guide_clip_kernel(
         def entries(offsets, first, count):
             return offsets[:, first // PER_COLUMN : (first + count) // PER_COLUMN]
 
-        tab_sc = keep.tile([P, T], U8, name="tab_sc", align_bytes=64)
+        tab_sc = keep.tile([P, T], U8, name="tab_sc", tag="v1", align_bytes=64)
         w1_sc = keep.tile([P, H], U8, name="w1_sc", align_bytes=64)
         v_sc = [keep.tile([P, S], U8, name=f"v_sc{a}", align_bytes=64) for a in range(K_PASSES)]
         w1p_sc = [keep.tile([P, H], U8, name=f"w1p_sc{a}", align_bytes=64) for a in range(K_PASSES)]
         nc.gpsimd.memset(w1_sc[:].bitcast(I32), 0)
-        nc.gpsimd.memset(tab_sc[:].bitcast(I32), 0)
-        for scales in (w1p_sc, v_sc):
+        nc.vector.memset(tab_sc[:].bitcast(I32), 0)
+        for scales in (v_sc, w1p_sc):
             for a in range(1, K_PASSES):
                 nc.vector.memset(scales[a][P - 32 : P, :].bitcast(I32), 0)
 
@@ -68,7 +69,7 @@ def tile_list_auction_guide_clip_kernel(
 
         wgs_rows = wgs.rearrange("(u t) j -> u t j", t=PACK)
         weights = [keep.tile([P, S], F32, name=f"wgs{t}") for t in range(PACK)]
-        pages = [keep.tile([P, T], F32, name=f"page{i}") for i in range(ROW_SETS)]
+        pages = [keep.tile([P, T], F32, name=f"page{i}", tag=f"page{i}") for i in range(ROW_SETS)]
         page_rows = page0.rearrange("(b p t) c -> b t p c", t=PACK, p=P)
 
         def load_wgs(t, queue):
@@ -78,21 +79,24 @@ def tile_list_auction_guide_clip_kernel(
         def load_page(i):
             nc.sync.dma_start(pages[i][:], page_rows[i // PACK, i % PACK])
 
-        nc.sync.dma_start(idx[:], offs)
-        load_tab(0)
         w1_raw = keep.tile([P, K_PASSES, 2 * H], U8, name="w1_raw", align_bytes=64)
         nc.sync.dma_start(w1_raw[:].bitcast(I32), w1_words.rearrange("a p c -> p a c").bitcast(I32))
+        nc.sync.dma_start(idx[:], offs)
+        load_tab(0)
         load_wgs(0, nc.gpsimd)
-        for packed, source in ((w1_sc, w1_scales), (tab_sc, tab_scales)):
+
+        def load_scale_rows(packed, source):
             for q in range(QUADRANTS):
                 nc.sync.dma_start(
                     packed[32 * q : 32 * q + 4 * K_PASSES, :].bitcast(I32),
                     source[:, 4 * q : 4 * q + 4, :].bitcast(I32),
                 )
+
+        load_scale_rows(w1_sc, w1_scales)
         load_tab(1)
-        nc.sync.dma_start(idx2[:], offs2)
+        load_scale_rows(tab_sc, tab_scales)
         load_tab(2)
-        load_page(0)
+        nc.sync.dma_start(idx2[:], offs2)
 
         def lower_scale_rows(scales):
             for a in range(1, K_PASSES):
@@ -101,18 +105,21 @@ def tile_list_auction_guide_clip_kernel(
                     scales[0][4 * a : 4 * a + MOVED_ROWS, :].bitcast(I32),
                 )
 
-        nc.vector.tensor_copy(
-            w1p_sc[0][:].rearrange("p (b t c e) -> p b c t e", b=R_PASSES, t=PACK, e=16),
-            w1_sc[:].rearrange("p (b c e t) -> p b c t e", b=R_PASSES, t=PACK, e=16),
-        )
-        lower_scale_rows(w1p_sc)
-        nc.vector.tensor_copy(v_sc[0][:], tab_sc[:].indirect(idx[:]))
-        lower_scale_rows(v_sc)
         w1p = keep.tile([P, K_PASSES * R_PASSES, 2 * P * PACK], U8, name="w1p", align_bytes=64)
         nc.vector.tensor_copy(
             w1p[:].bitcast(U16).rearrange("p g (t c e) -> p g c t e", t=PACK, e=8),
             w1_raw[:].bitcast(U16).rearrange("p a (b c e t) -> p (a b) c t e", b=R_PASSES, t=PACK, e=8),
         )
+        v = [keep.tile([P, S], U32, name="v0", align_bytes=64)]
+        nc.vector.tensor_copy(v[0][:], tab[0][:].bitcast(U32).indirect(idx[:]))
+        nc.vector.tensor_copy(
+            w1p_sc[0][:].rearrange("p (b t c e) -> p b c t e", b=R_PASSES, t=PACK, e=16),
+            w1_sc[:].rearrange("p (b c e t) -> p b c t e", b=R_PASSES, t=PACK, e=16),
+        )
+        lower_scale_rows(w1p_sc)
+        load_page(0)
+        nc.vector.tensor_copy(v_sc[0][:], tab_sc[:].indirect(idx[:]))
+        lower_scale_rows(v_sc)
         for t in range(1, PACK):
             load_wgs(t, nc.sync)
             load_page(t)
@@ -122,45 +129,50 @@ def tile_list_auction_guide_clip_kernel(
         nc.sync.dma_start(lo[:], reserve.rearrange("(b p t) -> p b t", p=P, t=PACK))
         nc.sync.dma_start(hi[:], ceiling.rearrange("(b p t) -> p b t", p=P, t=PACK))
 
-        v = [keep.tile([P, S], U32, name=f"v{a}", align_bytes=64) for a in range(K_PASSES)]
+        v.extend(keep.tile([P, S], U32, name=f"v{a}", tag=f"v{a}", align_bytes=64) for a in range(1, K_PASSES))
         last = K_PASSES - 1
-        for a in range(last):
+        for a in range(1, last):
             nc.vector.tensor_copy(v[a][:], tab[a][:].bitcast(U32).indirect(idx[:]))
-        for j0 in range(0, S, BANK):
-            nc.vector.tensor_copy(
-                v[last][:, j0 : j0 + BANK], tab[last][:].bitcast(U32).indirect(entries(idx, j0, BANK))
-            )
+        for j0, j1 in ((0, LEAD), (LEAD, S)):
+            nc.vector.tensor_copy(v[last][:, j0:j1], tab[last][:].bitcast(U32).indirect(entries(idx, j0, j1 - j0)))
 
         h_pairs = []
 
-        def put_rows(i):
+        def make_h(i, h, j0, j1, bank):
             b, t = divmod(i, PACK)
-            if i % 2 == 0:
-                h_pairs.append(keep.tile([P, 2, S], F32, name="h_pair", tag=f"work{i // 2}"))
-            h = h_pairs[i // 2][:, i % 2, :]
-            for j0 in range(0, S, BANK):
-                cols = slice(j0, j0 + BANK)
-                acc = psum.tile([P, BANK], F32, name="acc")
-                for a in range(K_PASSES):
+            step = BANK if j1 - j0 == BANK else P
+            acc = psum.tile([P, j1 - j0], F32, name="acc", tag=f"bank{bank}")
+            for a in range(K_PASSES):
+                for c0 in range(j0, j1, step):
+                    cols = slice(c0, c0 + step)
                     nc.tensor.matmul_mx(
-                        acc[:],
+                        acc[:, c0 - j0 : c0 - j0 + step],
                         lhsT=w1p[:, a * R_PASSES + b, 2 * P * t : 2 * P * (t + 1)].bitcast(FP4X4),
                         lhsT_scale=w1p_sc[a][:, P * i : P * (i + 1)],
                         rhs=v[a][:, cols].bitcast(FP8X4),
                         rhs_scale=v_sc[a][:, cols],
-                        start=(a == 0),
-                        stop=(a == last),
+                        start=(a == 0 and c0 == j0),
+                        stop=(a == last and c0 + step == j1),
                     )
-                nc.scalar.copy(h[:, cols], acc[:])
-                if i == 0:
-                    nc.vector.tensor_tensor(
-                        pages[i][:].indirect(entries(idx2, j0, BANK)), h[:, cols], weights[t][:, cols], MULT
-                    )
-            if i > 0:
-                nc.vector.tensor_tensor(pages[i][:].indirect(idx2[:]), h, weights[t][:], MULT)
+            nc.scalar.copy(h[:, j0:j1], acc[:])
 
-        def interleave(rows):
-            woven = ring.tile([P, rows.shape[2] * PACK], BF16, name="woven", align_bytes=64)
+        def put_rows(i):
+            if i % 2 == 0:
+                h_pairs.append(keep.tile([P, 2, S], F32, name="h_pair", tag=f"work{i // 2}", align_bytes=64))
+            h = h_pairs[i // 2][:, i % 2, :]
+            cuts = (0, LEAD, BANK, S) if i == 0 else (0, BANK, S)
+            for n in range(len(cuts) - 1):
+                make_h(i, h, cuts[n], cuts[n + 1], n + 2 if i == 0 else n)
+            for j0, j1 in ((0, LEAD), (LEAD, S)) if i == 0 else ((0, S),):
+                nc.vector.tensor_tensor(
+                    pages[i][:].indirect(entries(idx2, j0, j1 - j0)), h[:, j0:j1], weights[i % PACK][:, j0:j1], MULT
+                )
+
+        def interleave(rows, tag=None):
+            if tag is None:
+                woven = ring.tile([P, rows.shape[2] * PACK], BF16, name="woven", align_bytes=64)
+            else:
+                woven = keep.tile([P, rows.shape[2] * PACK], BF16, name="woven", tag=tag, align_bytes=64)
             nc.scalar.copy(
                 woven[:].rearrange("p (c e t) -> p c t e", t=PACK, e=2),
                 rows.rearrange("p t (c e) -> p c t e", e=2),
@@ -178,19 +190,20 @@ def tile_list_auction_guide_clip_kernel(
                 woven = interleave(raw[:])
                 nc.vector.quantize_mx(w2_codes[b][:, col0:col1].bitcast(FP8X4), w2_sc[b][:, col0:col1], woven[:])
 
-        z_woven = {}
-
-        def fetch(b, chunks, pair):
-            first = CHUNKS[chunks[0]][0]
-            count = sum(CHUNKS[c][1] for c in chunks)
-            x = keep.tile([P, PACK, count], F32, name="x", tag=f"work{pair}")
+        def fetch(b, first, count, x_tag, woven_tag=None):
+            x = keep.tile([P, PACK, count], F32, name="x", tag=x_tag, align_bytes=64)
             for t in range(PACK):
                 nc.vector.tensor_copy(x[:, t, :], pages[b * PACK + t][:].indirect(entries(idx3, first, count)))
             for t in range(PACK):
                 nc.vector.tensor_scalar(x[:, t, :], x[:, t, :], lo[:, b, t : t + 1], hi[:, b, t : t + 1], MAX, MIN)
-            for c in chunks:
-                m0, width = CHUNKS[c]
-                z_woven[b, c] = interleave(x[:, :, m0 - first : m0 - first + width])
+            return interleave(x[:], woven_tag)
+
+        z_codes = [keep.tile([P, M], U32, name=f"z_codes{b}", align_bytes=64) for b in range(R_PASSES)]
+        z_sc = [keep.tile([P, M], U8, name=f"z_sc{b}", align_bytes=64) for b in range(R_PASSES)]
+
+        def quantise_z(b, first, woven):
+            cols = slice(first, first + woven.shape[1] // PACK)
+            nc.vector.quantize_mx(z_codes[b][:, cols].bitcast(FP8X4), z_sc[b][:, cols], woven[:])
 
         factors = {}
 
@@ -208,36 +221,36 @@ def tile_list_auction_guide_clip_kernel(
         banks = {}
 
         def multiply(b, c):
-            width = CHUNKS[c][1]
+            m0, width = CHUNKS[c]
             per_bank = BANK // width
-            codes = keep.tile([P, width], U32, name=f"z_codes{b}_{c}", align_bytes=64)
-            z_sc = keep.tile([P, width], U8, name=f"z_sc{b}_{c}", align_bytes=64)
-            nc.vector.quantize_mx(codes[:].bitcast(FP8X4), z_sc[:], z_woven[b, c][:])
+            cols = slice(m0, m0 + width)
             for n0 in range(0, N_TILES, per_bank):
                 if b == 0:
-                    banks[c, n0] = psum.tile([P, per_bank, width], F32, name="acc")
+                    banks[c, n0] = psum.tile([P, per_bank, width], F32, name="acc", tag=f"bank{(len(banks) + 2) % 8}")
                 for n in range(per_bank):
                     n_cols = slice((n0 + n) * P, (n0 + n + 1) * P)
                     nc.tensor.matmul_mx(
                         banks[c, n0][:, n, :],
                         lhsT=w2_codes[b][:, n_cols].bitcast(FP8X4),
                         lhsT_scale=w2_sc[b][:, n_cols],
-                        rhs=codes[:].bitcast(FP8X4),
-                        rhs_scale=z_sc[:],
+                        rhs=z_codes[b][:, cols].bitcast(FP8X4),
+                        rhs_scale=z_sc[b][:, cols],
                         start=(b == 0 and n == 0),
                         stop=(b == R_PASSES - 1 and n == per_bank - 1),
                     )
 
-        def finish(c):
+        def finish(c, n0, y=None):
             m0, width = CHUNKS[c]
             per_bank = BANK // width
-            for n0 in range(0, N_TILES, per_bank):
-                tile, n = factors[c, n0]
-                y = stage.tile([P, per_bank, width], F32, name="y")
-                nc.vector.tensor_tensor(y[:], banks[c, n0][:], tile[:, n : n + per_bank, :], MULT)
-                nc.sync.dma_start(
-                    out[n0 * P : (n0 + per_bank) * P, m0 : m0 + width].rearrange("(n p) m -> p n m", p=P), y[:]
-                )
+            tile, n = factors[c, n0]
+            if y is None:
+                fresh = stage.tile([P, BANK], F32, name="y")
+                y = fresh[:]
+            y = y.rearrange("p (n m) -> p n m", n=per_bank)
+            nc.vector.tensor_tensor(y, banks[c, n0][:], tile[:, n : n + per_bank, :], MULT)
+            nc.sync.dma_start(
+                out[n0 * P : (n0 + per_bank) * P, m0 : m0 + width].rearrange("(n p) m -> p n m", p=P), y
+            )
 
         for i in range(PACK):
             put_rows(i)
@@ -251,18 +264,30 @@ def tile_list_auction_guide_clip_kernel(
         for i in range(PACK, ROW_SETS):
             put_rows(i)
 
-        h_last = ROW_SETS // 2 - 1
-        fetch(0, (0,), h_last)
-        fetch(1, (0,), h_last - 1)
+        w00 = fetch(0, 0, 512, "work3")
+        w10 = fetch(1, 0, 512, "work2")
+        quantise_z(0, 0, w00)
         multiply(0, 0)
-        fetch(0, (1, 2), h_last)
+        w01 = fetch(0, 512, 512, "work3")
+        quantise_z(1, 0, w10)
         multiply(1, 0)
-        fetch(1, (1,), h_last - 1)
-        finish(0)
+        w11 = fetch(1, 512, 256, "work2", "late1")
+        for n0 in range(4):
+            finish(0, n0)
+        quantise_z(0, 512, w01)
         multiply(0, 1)
-        fetch(1, (2,), h_last)
+        quantise_z(1, 512, w11)
         multiply(1, 1)
         multiply(0, 2)
-        finish(1)
+        w12 = fetch(1, 768, 256, "late1", "late2")
+        held = keep.tile([P, 2, BANK], F32, name="held", tag="page4")
+        finish(0, 4, held[:, 0, :])
+        finish(0, 5, held[:, 1, :])
+        finish(1, 0)
+        quantise_z(1, 768, w12)
         multiply(1, 2)
-        finish(2)
+        held = keep.tile([P, 2, BANK], F32, name="held", tag="late2", align_bytes=64)
+        finish(1, 2, held[:, 0, :])
+        finish(1, 4, held[:, 1, :])
+        for n0 in range(0, N_TILES, 2):
+            finish(2, n0)

@@ -1,6 +1,7 @@
 from contextlib import ExitStack
 
 import concourse.mybir as mybir
+from concourse.masks import make_identity
 
 K, H, N, T, S, M = 1536, 1024, 768, 2048, 1024, 1024
 FLOPS = 2 * K * H * S + 2 * H * N * M
@@ -40,9 +41,8 @@ def tile_list_auction_guide_clip_kernel(
     nc = tc.nc
     with ExitStack() as ctx:
         keep = ctx.enter_context(tc.tile_pool(name="keep", bufs=1))
-        big = ctx.enter_context(tc.tile_pool(name="big", bufs=4))
         ring = ctx.enter_context(tc.tile_pool(name="ring", bufs=4))
-        stage = ctx.enter_context(tc.tile_pool(name="stage", bufs=8))
+        stage = ctx.enter_context(tc.tile_pool(name="stage", bufs=6))
         psum = ctx.enter_context(tc.psum_pool(name="psum", bufs=1))
 
         idx = keep.tile([P, S // PER_COLUMN], U16, name="idx")
@@ -52,49 +52,75 @@ def tile_list_auction_guide_clip_kernel(
         def entries(offsets, first, count):
             return offsets[:, first // PER_COLUMN : (first + count) // PER_COLUMN]
 
-        tab_sc = keep.tile([P, T], U8, name="tab_sc", tag="v1", align_bytes=64)
-        w1_sc = keep.tile([P, H], U8, name="w1_sc", align_bytes=64)
+        tab_sc = keep.tile([P, T], U8, name="tab_sc", align_bytes=64)
+        w1_sc = keep.tile([P, K_PASSES, H], U8, name="w1_sc", align_bytes=64)
         v_sc = [keep.tile([P, S], U8, name=f"v_sc{a}", align_bytes=64) for a in range(K_PASSES)]
-        w1p_sc = [keep.tile([P, H], U8, name=f"w1p_sc{a}", align_bytes=64) for a in range(K_PASSES)]
-        nc.gpsimd.memset(w1_sc[:].bitcast(I32), 0)
-        nc.vector.memset(tab_sc[:].bitcast(I32), 0)
-        for scales in (v_sc, w1p_sc):
-            for a in range(1, K_PASSES):
-                nc.vector.memset(scales[a][P - 32 : P, :].bitcast(I32), 0)
+        w1p_sc = keep.tile([P, K_PASSES, H], U8, name="w1p_sc", align_bytes=64)
+        nc.gpsimd.memset(tab_sc[:].bitcast(I32), 0)
+        nc.vector.memset(w1_sc[:].bitcast(I32), 0)
+        for a in range(1, K_PASSES):
+            nc.vector.memset(v_sc[a][P - 32 : P, :].bitcast(I32), 0)
 
-        tab = [big.tile([P, T], I32, name=f"tab{a}", tag="big") for a in range(K_PASSES)]
+        tab = [keep.tile([P, T], I32, name=f"tab{a}", tag=f"big{a}") for a in range(K_PASSES)]
 
         def load_tab(a):
             nc.sync.dma_start(tab[a][:], tab_words[a].rearrange("p t i -> p (t i)").bitcast(I32))
 
-        wgs_rows = wgs.rearrange("(u t) j -> u t j", t=PACK)
         weights = [keep.tile([P, S], F32, name=f"wgs{t}") for t in range(PACK)]
-        pages = [keep.tile([P, T], F32, name=f"page{i}", tag=f"page{i}") for i in range(ROW_SETS)]
+        pages = {}
         page_rows = page0.rearrange("(b p t) c -> b t p c", t=PACK, p=P)
 
-        def load_wgs(t, queue):
-            for q in range(QUADRANTS):
-                queue.dma_start(weights[t][32 * q : 32 * q + 32, :], wgs_rows[:, t, :])
+        turned = []
+        spread = []
+
+        def turn_wgs():
+            rows = keep.tile([P, S], F32, name="wgs_rows", tag="page5")
+            nc.sync.dma_start(rows[:], wgs)
+            for half in range(S // BANK):
+                bank = psum.tile([P, BANK // P, P], F32, name="turned", tag=f"bank{5 + half}")
+                for n in range(BANK // P):
+                    j0 = half * BANK + n * P
+                    nc.tensor.transpose(bank[:, n, :], rows[:, j0 : j0 + P], identity[:])
+                turned.append(bank)
+            spread.extend(keep.tile([P, 2, S], F32, name="spread", tag=f"page{6 + u}") for u in range(2))
+
+        def deal_wgs(t):
+            for half in range(S // BANK):
+                cols = slice(half * BANK, (half + 1) * BANK)
+                dealt = spread[t // 2][:, t % 2, cols]
+                nc.scalar.copy(
+                    dealt.rearrange("p (n q u) -> p n q u", q=QUADRANTS, u=32),
+                    turned[half][:].rearrange("p n (u t) -> p n t u", t=PACK)[:, :, t : t + 1, :].to_broadcast(
+                        [P, BANK // P, QUADRANTS, 32]
+                    ),
+                )
+                bank = psum.tile([P, BANK // P, P], F32, name="back", tag=f"bank{(7, 0, 1)[(2 * t + half) % 3]}")
+                for n in range(BANK // P):
+                    nc.tensor.transpose(bank[:, n, :], dealt[:, n * P : (n + 1) * P], identity[:])
+                nc.scalar.copy(weights[t][:, cols], bank[:].rearrange("p n j -> p (n j)"))
 
         def load_page(i):
+            pages[i] = keep.tile([P, T], F32, name=f"page{i}", tag=f"page{i}")
             nc.sync.dma_start(pages[i][:], page_rows[i // PACK, i % PACK])
 
         w1_raw = keep.tile([P, K_PASSES, 2 * H], U8, name="w1_raw", align_bytes=64)
         nc.sync.dma_start(w1_raw[:].bitcast(I32), w1_words.rearrange("a p c -> p a c").bitcast(I32))
         nc.sync.dma_start(idx[:], offs)
+        for q in range(QUADRANTS):
+            (nc.sync if q % 2 == 0 else nc.scalar).dma_start(
+                tab_sc[32 * q : 32 * q + 4 * K_PASSES, :].bitcast(I32),
+                tab_scales[:, 4 * q : 4 * q + 4, :].bitcast(I32),
+            )
         load_tab(0)
-        load_wgs(0, nc.gpsimd)
-
-        def load_scale_rows(packed, source):
-            for q in range(QUADRANTS):
-                nc.sync.dma_start(
-                    packed[32 * q : 32 * q + 4 * K_PASSES, :].bitcast(I32),
-                    source[:, 4 * q : 4 * q + 4, :].bitcast(I32),
-                )
-
-        load_scale_rows(w1_sc, w1_scales)
+        identity = keep.tile([P, P], F32, name="identity")
+        make_identity(nc, identity[:])
+        turn_wgs()
+        for q in range(QUADRANTS):
+            nc.sync.dma_start(
+                w1_sc[32 * q : 32 * q + 4, :, :].bitcast(I32),
+                w1_scales[:, 4 * q : 4 * q + 4, :].rearrange("a j c -> j a c").bitcast(I32),
+            )
         load_tab(1)
-        load_scale_rows(tab_sc, tab_scales)
         load_tab(2)
         nc.sync.dma_start(idx2[:], offs2)
 
@@ -110,28 +136,19 @@ def tile_list_auction_guide_clip_kernel(
             w1p[:].bitcast(U16).rearrange("p g (t c e) -> p g c t e", t=PACK, e=8),
             w1_raw[:].bitcast(U16).rearrange("p a (b c e t) -> p (a b) c t e", b=R_PASSES, t=PACK, e=8),
         )
-        v = [keep.tile([P, S], U32, name="v0", align_bytes=64)]
-        nc.vector.tensor_copy(v[0][:], tab[0][:].bitcast(U32).indirect(idx[:]))
-        nc.vector.tensor_copy(
-            w1p_sc[0][:].rearrange("p (b t c e) -> p b c t e", b=R_PASSES, t=PACK, e=16),
-            w1_sc[:].rearrange("p (b c e t) -> p b c t e", b=R_PASSES, t=PACK, e=16),
-        )
-        lower_scale_rows(w1p_sc)
-        load_page(0)
         nc.vector.tensor_copy(v_sc[0][:], tab_sc[:].indirect(idx[:]))
         lower_scale_rows(v_sc)
+        load_page(0)
+        nc.vector.tensor_copy(
+            w1p_sc[:].rearrange("p a (b t c e) -> p (a b) c t e", b=R_PASSES, t=PACK, e=16),
+            w1_sc[:].rearrange("p a (b c e t) -> p (a b) c t e", b=R_PASSES, t=PACK, e=16),
+        )
         for t in range(1, PACK):
-            load_wgs(t, nc.sync)
             load_page(t)
-        nc.sync.dma_start(idx3[:], offs3)
-        lo = keep.tile([P, R_PASSES, PACK], F32, name="lo")
-        hi = keep.tile([P, R_PASSES, PACK], F32, name="hi")
-        nc.sync.dma_start(lo[:], reserve.rearrange("(b p t) -> p b t", p=P, t=PACK))
-        nc.sync.dma_start(hi[:], ceiling.rearrange("(b p t) -> p b t", p=P, t=PACK))
 
-        v.extend(keep.tile([P, S], U32, name=f"v{a}", tag=f"v{a}", align_bytes=64) for a in range(1, K_PASSES))
+        v = [keep.tile([P, S], U32, name=f"v{a}", align_bytes=64) for a in range(K_PASSES)]
         last = K_PASSES - 1
-        for a in range(1, last):
+        for a in range(last):
             nc.vector.tensor_copy(v[a][:], tab[a][:].bitcast(U32).indirect(idx[:]))
         for j0, j1 in ((0, LEAD), (LEAD, S)):
             nc.vector.tensor_copy(v[last][:, j0:j1], tab[last][:].bitcast(U32).indirect(entries(idx, j0, j1 - j0)))
@@ -148,7 +165,7 @@ def tile_list_auction_guide_clip_kernel(
                     nc.tensor.matmul_mx(
                         acc[:, c0 - j0 : c0 - j0 + step],
                         lhsT=w1p[:, a * R_PASSES + b, 2 * P * t : 2 * P * (t + 1)].bitcast(FP4X4),
-                        lhsT_scale=w1p_sc[a][:, P * i : P * (i + 1)],
+                        lhsT_scale=w1p_sc[:, a, P * i : P * (i + 1)],
                         rhs=v[a][:, cols].bitcast(FP8X4),
                         rhs_scale=v_sc[a][:, cols],
                         start=(a == 0 and c0 == j0),
@@ -184,10 +201,10 @@ def tile_list_auction_guide_clip_kernel(
 
         def quantise_w2(b):
             w2_pass = w2[b * P * PACK : (b + 1) * P * PACK, :].rearrange("(p t) n -> p t n", t=PACK)
+            raw = keep.tile([P, PACK, N], F32, name="w2_raw", tag=f"big{b}")
+            nc.sync.dma_start(raw[:], w2_pass)
             for col0, col1 in W2_PIECES:
-                raw = big.tile([P, PACK, col1 - col0], F32, name="w2_raw", tag="big")
-                nc.sync.dma_start(raw[:], w2_pass[:, :, col0:col1])
-                woven = interleave(raw[:])
+                woven = interleave(raw[:, :, col0:col1])
                 nc.vector.quantize_mx(w2_codes[b][:, col0:col1].bitcast(FP8X4), w2_sc[b][:, col0:col1], woven[:])
 
         def fetch(b, first, count, x_tag, woven_tag=None):
@@ -205,18 +222,13 @@ def tile_list_auction_guide_clip_kernel(
             cols = slice(first, first + woven.shape[1] // PACK)
             nc.vector.quantize_mx(z_codes[b][:, cols].bitcast(FP8X4), z_sc[b][:, cols], woven[:])
 
-        factors = {}
+        factors = []
 
-        def load_seller(c):
-            m0, width = CHUNKS[c]
-            per_load = SELLER_COLS // width
-            for n0 in range(0, N_TILES, per_load):
-                tile = big.tile([P, per_load, width], F32, name=f"seller{c}_{n0}", tag="big")
-                nc.sync.dma_start(
-                    tile[:], seller[n0 * P : (n0 + per_load) * P, m0 : m0 + width].rearrange("(n p) m -> p n m", p=P)
-                )
-                for n in range(per_load):
-                    factors[c, n0 + n] = (tile, n)
+        def load_seller():
+            for pair, tag in enumerate(("big2", "big0", "big1")):
+                tile = keep.tile([P, 2, M], F32, name="factors", tag=tag)
+                nc.sync.dma_start(tile[:], seller[2 * pair * P : 2 * (pair + 1) * P, :].rearrange("(n p) m -> p n m", p=P))
+                factors.append(tile)
 
         banks = {}
 
@@ -242,25 +254,31 @@ def tile_list_auction_guide_clip_kernel(
         def finish(c, n0, y=None):
             m0, width = CHUNKS[c]
             per_bank = BANK // width
-            tile, n = factors[c, n0]
+            n = n0 % 2
+            factor = factors[n0 // 2][:, n : n + per_bank, m0 : m0 + width]
             if y is None:
                 fresh = stage.tile([P, BANK], F32, name="y")
                 y = fresh[:]
             y = y.rearrange("p (n m) -> p n m", n=per_bank)
-            nc.vector.tensor_tensor(y, banks[c, n0][:], tile[:, n : n + per_bank, :], MULT)
+            nc.vector.tensor_tensor(y, banks[c, n0][:], factor, MULT)
             nc.sync.dma_start(
                 out[n0 * P : (n0 + per_bank) * P, m0 : m0 + width].rearrange("(n p) m -> p n m", p=P), y
             )
 
         for i in range(PACK):
+            deal_wgs(i)
             put_rows(i)
+        load_page(4)
+        load_page(5)
         for b in range(R_PASSES):
             quantise_w2(b)
-            load_page(PACK + b)
-        for i in range(PACK + R_PASSES, ROW_SETS):
-            load_page(i)
-        for c in range(len(CHUNKS)):
-            load_seller(c)
+            load_page(6 + b)
+        nc.sync.dma_start(idx3[:], offs3)
+        lo = keep.tile([P, R_PASSES, PACK], F32, name="lo")
+        hi = keep.tile([P, R_PASSES, PACK], F32, name="hi")
+        nc.sync.dma_start(lo[:], reserve.rearrange("(b p t) -> p b t", p=P, t=PACK))
+        nc.sync.dma_start(hi[:], ceiling.rearrange("(b p t) -> p b t", p=P, t=PACK))
+        load_seller()
         for i in range(PACK, ROW_SETS):
             put_rows(i)
 

@@ -21,17 +21,19 @@ MIN = mybir.AluOpType.min
 P = 128
 PACK = 4
 QUADRANTS = 4
+QUADRANT = P // QUADRANTS
 PER_COLUMN = 16
 K_PASSES = K // (P * PACK)
 R_PASSES = H // (P * PACK)
 ROW_SETS = R_PASSES * PACK
 BANK = 512
+BANKS = 8
 N_TILES = N // P
 CHUNKS = ((0, 512), (512, 256), (768, 256))
 W2_PIECES = ((0, 512), (512, N))
-SELLER_COLS = N_TILES * M // 4
 MOVED_ROWS = 112
 LEAD = 256
+H_BANK, FIRST_SET_BANK, TURNED_BANK = 0, 2, 5
 
 
 def tile_list_auction_guide_clip_kernel(
@@ -59,7 +61,7 @@ def tile_list_auction_guide_clip_kernel(
         nc.gpsimd.memset(tab_sc[:].bitcast(I32), 0)
         nc.vector.memset(w1_sc[:].bitcast(I32), 0)
         for a in range(1, K_PASSES):
-            nc.vector.memset(v_sc[a][P - 32 : P, :].bitcast(I32), 0)
+            nc.vector.memset(v_sc[a][P - QUADRANT : P, :].bitcast(I32), 0)
 
         tab = [keep.tile([P, T], I32, name=f"tab{a}", tag=f"big{a}") for a in range(K_PASSES)]
 
@@ -69,32 +71,30 @@ def tile_list_auction_guide_clip_kernel(
         weights = [keep.tile([P, S], F32, name=f"wgs{t}") for t in range(PACK)]
         pages = {}
         page_rows = page0.rearrange("(b p t) c -> b t p c", t=PACK, p=P)
-
         turned = []
-        spread = []
 
         def turn_wgs():
             rows = keep.tile([P, S], F32, name="wgs_rows", tag="page5")
             nc.sync.dma_start(rows[:], wgs)
             for half in range(S // BANK):
-                bank = psum.tile([P, BANK // P, P], F32, name="turned", tag=f"bank{5 + half}")
+                bank = psum.tile([P, BANK // P, P], F32, name="turned", tag=f"bank{TURNED_BANK + half}")
                 for n in range(BANK // P):
                     j0 = half * BANK + n * P
                     nc.tensor.transpose(bank[:, n, :], rows[:, j0 : j0 + P], identity[:])
                 turned.append(bank)
-            spread.extend(keep.tile([P, 2, S], F32, name="spread", tag=f"page{6 + u}") for u in range(2))
 
         def deal_wgs(t):
+            spread = keep.tile([P, S], F32, name="spread", tag="page6")
             for half in range(S // BANK):
                 cols = slice(half * BANK, (half + 1) * BANK)
-                dealt = spread[t // 2][:, t % 2, cols]
+                dealt = spread[:, cols]
+                rows_t = turned[half][:].rearrange("p n (u t) -> p n t u", t=PACK)[:, :, t : t + 1, :]
                 nc.scalar.copy(
-                    dealt.rearrange("p (n q u) -> p n q u", q=QUADRANTS, u=32),
-                    turned[half][:].rearrange("p n (u t) -> p n t u", t=PACK)[:, :, t : t + 1, :].to_broadcast(
-                        [P, BANK // P, QUADRANTS, 32]
-                    ),
+                    dealt.rearrange("p (n q u) -> p n q u", q=QUADRANTS, u=QUADRANT),
+                    rows_t.to_broadcast([P, BANK // P, QUADRANTS, QUADRANT]),
                 )
-                bank = psum.tile([P, BANK // P, P], F32, name="back", tag=f"bank{(7, 0, 1)[(2 * t + half) % 3]}")
+                first_bank = H_BANK if t == 0 else FIRST_SET_BANK
+                bank = psum.tile([P, BANK // P, P], F32, name="back", tag=f"bank{first_bank + half}")
                 for n in range(BANK // P):
                     nc.tensor.transpose(bank[:, n, :], dealt[:, n * P : (n + 1) * P], identity[:])
                 nc.scalar.copy(weights[t][:, cols], bank[:].rearrange("p n j -> p (n j)"))
@@ -103,12 +103,14 @@ def tile_list_auction_guide_clip_kernel(
             pages[i] = keep.tile([P, T], F32, name=f"page{i}", tag=f"page{i}")
             nc.sync.dma_start(pages[i][:], page_rows[i // PACK, i % PACK])
 
-        w1_raw = keep.tile([P, K_PASSES, 2 * H], U8, name="w1_raw", align_bytes=64)
-        nc.sync.dma_start(w1_raw[:].bitcast(I32), w1_words.rearrange("a p c -> p a c").bitcast(I32))
+        w1_raw = [keep.tile([P, K_PASSES, H], U8, name=f"w1_raw{b}", align_bytes=64) for b in range(R_PASSES)]
+        for b in range(R_PASSES):
+            w1_half = w1_words[:, :, b * H : (b + 1) * H]
+            nc.sync.dma_start(w1_raw[b][:].bitcast(I32), w1_half.rearrange("a p c -> p a c").bitcast(I32))
         nc.sync.dma_start(idx[:], offs)
         for q in range(QUADRANTS):
             (nc.sync if q % 2 == 0 else nc.scalar).dma_start(
-                tab_sc[32 * q : 32 * q + 4 * K_PASSES, :].bitcast(I32),
+                tab_sc[QUADRANT * q : QUADRANT * q + 4 * K_PASSES, :].bitcast(I32),
                 tab_scales[:, 4 * q : 4 * q + 4, :].bitcast(I32),
             )
         load_tab(0)
@@ -117,34 +119,32 @@ def tile_list_auction_guide_clip_kernel(
         turn_wgs()
         for q in range(QUADRANTS):
             nc.sync.dma_start(
-                w1_sc[32 * q : 32 * q + 4, :, :].bitcast(I32),
+                w1_sc[QUADRANT * q : QUADRANT * q + 4, :, :].bitcast(I32),
                 w1_scales[:, 4 * q : 4 * q + 4, :].rearrange("a j c -> j a c").bitcast(I32),
             )
         load_tab(1)
         load_tab(2)
         nc.sync.dma_start(idx2[:], offs2)
 
-        def lower_scale_rows(scales):
-            for a in range(1, K_PASSES):
-                nc.sync.dma_start(
-                    scales[a][0:MOVED_ROWS, :].bitcast(I32),
-                    scales[0][4 * a : 4 * a + MOVED_ROWS, :].bitcast(I32),
-                )
-
-        w1p = keep.tile([P, K_PASSES * R_PASSES, 2 * P * PACK], U8, name="w1p", align_bytes=64)
-        nc.vector.tensor_copy(
-            w1p[:].bitcast(U16).rearrange("p g (t c e) -> p g c t e", t=PACK, e=8),
-            w1_raw[:].bitcast(U16).rearrange("p a (b c e t) -> p (a b) c t e", b=R_PASSES, t=PACK, e=8),
-        )
+        w1p = [keep.tile([P, K_PASSES, H], U8, name=f"w1p{b}", align_bytes=64) for b in range(R_PASSES)]
+        for b in range(R_PASSES):
+            nc.vector.tensor_copy(
+                w1p[b][:].bitcast(U16).rearrange("p a (t c e) -> p c a t e", t=PACK, e=8),
+                w1_raw[b][:].bitcast(U16).rearrange("p a (c e t) -> p c a t e", t=PACK, e=8),
+            )
         nc.vector.tensor_copy(v_sc[0][:], tab_sc[:].indirect(idx[:]))
-        lower_scale_rows(v_sc)
+        for a in range(1, K_PASSES):
+            nc.sync.dma_start(
+                v_sc[a][0:MOVED_ROWS, :].bitcast(I32),
+                v_sc[0][4 * a : 4 * a + MOVED_ROWS, :].bitcast(I32),
+            )
         load_page(0)
         nc.vector.tensor_copy(
             w1p_sc[:].rearrange("p a (b t c e) -> p (a b) c t e", b=R_PASSES, t=PACK, e=16),
             w1_sc[:].rearrange("p a (b c e t) -> p (a b) c t e", b=R_PASSES, t=PACK, e=16),
         )
-        for t in range(1, PACK):
-            load_page(t)
+        for i in range(1, PACK):
+            load_page(i)
 
         v = [keep.tile([P, S], U32, name=f"v{a}", align_bytes=64) for a in range(K_PASSES)]
         last = K_PASSES - 1
@@ -164,7 +164,7 @@ def tile_list_auction_guide_clip_kernel(
                     cols = slice(c0, c0 + step)
                     nc.tensor.matmul_mx(
                         acc[:, c0 - j0 : c0 - j0 + step],
-                        lhsT=w1p[:, a * R_PASSES + b, 2 * P * t : 2 * P * (t + 1)].bitcast(FP4X4),
+                        lhsT=w1p[b][:, a, 2 * P * t : 2 * P * (t + 1)].bitcast(FP4X4),
                         lhsT_scale=w1p_sc[:, a, P * i : P * (i + 1)],
                         rhs=v[a][:, cols].bitcast(FP8X4),
                         rhs_scale=v_sc[a][:, cols],
@@ -177,9 +177,9 @@ def tile_list_auction_guide_clip_kernel(
             if i % 2 == 0:
                 h_pairs.append(keep.tile([P, 2, S], F32, name="h_pair", tag=f"work{i // 2}", align_bytes=64))
             h = h_pairs[i // 2][:, i % 2, :]
-            cuts = (0, LEAD, BANK, S) if i == 0 else (0, BANK, S)
+            cuts, first_bank = ((0, LEAD, BANK, S), FIRST_SET_BANK) if i == 0 else ((0, BANK, S), H_BANK)
             for n in range(len(cuts) - 1):
-                make_h(i, h, cuts[n], cuts[n + 1], n + 2 if i == 0 else n)
+                make_h(i, h, cuts[n], cuts[n + 1], first_bank + n)
             for j0, j1 in ((0, LEAD), (LEAD, S)) if i == 0 else ((0, S),):
                 nc.vector.tensor_tensor(
                     pages[i][:].indirect(entries(idx2, j0, j1 - j0)), h[:, j0:j1], weights[i % PACK][:, j0:j1], MULT
@@ -227,7 +227,8 @@ def tile_list_auction_guide_clip_kernel(
         def load_seller():
             for pair, tag in enumerate(("big2", "big0", "big1")):
                 tile = keep.tile([P, 2, M], F32, name="factors", tag=tag)
-                nc.sync.dma_start(tile[:], seller[2 * pair * P : 2 * (pair + 1) * P, :].rearrange("(n p) m -> p n m", p=P))
+                seller_rows = seller[2 * pair * P : 2 * (pair + 1) * P, :]
+                nc.sync.dma_start(tile[:], seller_rows.rearrange("(n p) m -> p n m", p=P))
                 factors.append(tile)
 
         banks = {}
@@ -238,7 +239,8 @@ def tile_list_auction_guide_clip_kernel(
             cols = slice(m0, m0 + width)
             for n0 in range(0, N_TILES, per_bank):
                 if b == 0:
-                    banks[c, n0] = psum.tile([P, per_bank, width], F32, name="acc", tag=f"bank{(len(banks) + 2) % 8}")
+                    tag = f"bank{(FIRST_SET_BANK + len(banks)) % BANKS}"
+                    banks[c, n0] = psum.tile([P, per_bank, width], F32, name="acc", tag=tag)
                 for n in range(per_bank):
                     n_cols = slice((n0 + n) * P, (n0 + n + 1) * P)
                     nc.tensor.matmul_mx(
@@ -257,8 +259,8 @@ def tile_list_auction_guide_clip_kernel(
             n = n0 % 2
             factor = factors[n0 // 2][:, n : n + per_bank, m0 : m0 + width]
             if y is None:
-                fresh = stage.tile([P, BANK], F32, name="y")
-                y = fresh[:]
+                staged = stage.tile([P, BANK], F32, name="y")
+                y = staged[:]
             y = y.rearrange("p (n m) -> p n m", n=per_bank)
             nc.vector.tensor_tensor(y, banks[c, n0][:], factor, MULT)
             nc.sync.dma_start(
@@ -268,11 +270,11 @@ def tile_list_auction_guide_clip_kernel(
         for i in range(PACK):
             deal_wgs(i)
             put_rows(i)
-        load_page(4)
-        load_page(5)
+        for i in range(PACK, ROW_SETS - R_PASSES):
+            load_page(i)
         for b in range(R_PASSES):
             quantise_w2(b)
-            load_page(6 + b)
+            load_page(ROW_SETS - R_PASSES + b)
         nc.sync.dma_start(idx3[:], offs3)
         lo = keep.tile([P, R_PASSES, PACK], F32, name="lo")
         hi = keep.tile([P, R_PASSES, PACK], F32, name="hi")
@@ -282,30 +284,31 @@ def tile_list_auction_guide_clip_kernel(
         for i in range(PACK, ROW_SETS):
             put_rows(i)
 
-        w00 = fetch(0, 0, 512, "work3")
-        w10 = fetch(1, 0, 512, "work2")
-        quantise_z(0, 0, w00)
+        (m_wide, wide), (m_second, narrow), (m_last, narrow) = CHUNKS
+        woven_0_wide = fetch(0, m_wide, wide, "work3")
+        woven_1_wide = fetch(1, m_wide, wide, "work2")
+        quantise_z(0, m_wide, woven_0_wide)
         multiply(0, 0)
-        w01 = fetch(0, 512, 512, "work3")
-        quantise_z(1, 0, w10)
+        woven_0_narrow = fetch(0, m_second, 2 * narrow, "work3")
+        quantise_z(1, m_wide, woven_1_wide)
         multiply(1, 0)
-        w11 = fetch(1, 512, 256, "work2", "late1")
-        for n0 in range(4):
+        woven_1_second = fetch(1, m_second, narrow, "work2", "second")
+        for n0 in range(N_TILES - 2):
             finish(0, n0)
-        quantise_z(0, 512, w01)
+        quantise_z(0, m_second, woven_0_narrow)
         multiply(0, 1)
-        quantise_z(1, 512, w11)
+        quantise_z(1, m_second, woven_1_second)
         multiply(1, 1)
         multiply(0, 2)
-        w12 = fetch(1, 768, 256, "late1", "late2")
+        woven_1_last = fetch(1, m_last, narrow, "second", "last")
         held = keep.tile([P, 2, BANK], F32, name="held", tag="page4")
-        finish(0, 4, held[:, 0, :])
-        finish(0, 5, held[:, 1, :])
+        for n in range(2):
+            finish(0, N_TILES - 2 + n, held[:, n, :])
         finish(1, 0)
-        quantise_z(1, 768, w12)
+        quantise_z(1, m_last, woven_1_last)
         multiply(1, 2)
-        held = keep.tile([P, 2, BANK], F32, name="held", tag="late2", align_bytes=64)
-        finish(1, 2, held[:, 0, :])
-        finish(1, 4, held[:, 1, :])
+        held_last = keep.tile([P, 2, BANK], F32, name="held_last", tag="last", align_bytes=64)
+        for n in range(2):
+            finish(1, 2 + 2 * n, held_last[:, n, :])
         for n0 in range(0, N_TILES, 2):
             finish(2, n0)

@@ -103,10 +103,9 @@ def tile_list_auction_guide_clip_kernel(
             pages[i] = keep.tile([P, T], F32, name=f"page{i}", tag=f"page{i}")
             nc.sync.dma_start(pages[i][:], page_rows[i // PACK, i % PACK])
 
-        w1_raw = [keep.tile([P, K_PASSES, H], U8, name=f"w1_raw{b}", align_bytes=64) for b in range(R_PASSES)]
-        for b in range(R_PASSES):
-            w1_half = w1_words[:, :, b * H : (b + 1) * H]
-            nc.sync.dma_start(w1_raw[b][:].bitcast(I32), w1_half.rearrange("a p c -> p a c").bitcast(I32))
+        w1_raw = [keep.tile([P, 2 * H], U8, name=f"w1_raw{a}", align_bytes=64) for a in range(K_PASSES)]
+        for a in range(K_PASSES):
+            nc.sync.dma_start(w1_raw[a][:].bitcast(I32), w1_words[a].bitcast(I32))
         nc.sync.dma_start(idx[:], offs)
         for q in range(QUADRANTS):
             (nc.sync if q % 2 == 0 else nc.scalar).dma_start(
@@ -117,20 +116,18 @@ def tile_list_auction_guide_clip_kernel(
         identity = keep.tile([P, P], F32, name="identity")
         make_identity(nc, identity[:])
         turn_wgs()
-        for q in range(QUADRANTS):
-            nc.sync.dma_start(
-                w1_sc[QUADRANT * q : QUADRANT * q + 4, :, :].bitcast(I32),
-                w1_scales[:, 4 * q : 4 * q + 4, :].rearrange("a j c -> j a c").bitcast(I32),
-            )
+        w1_scale_rows = w1_scales.rearrange("a (q j) c -> j q a c", j=4)
+        for j in range(4):
+            nc.sync.dma_start(w1_sc[j:P:QUADRANT, :, :].bitcast(I32), w1_scale_rows[j].bitcast(I32))
         load_tab(1)
         load_tab(2)
         nc.sync.dma_start(idx2[:], offs2)
 
-        w1p = [keep.tile([P, K_PASSES, H], U8, name=f"w1p{b}", align_bytes=64) for b in range(R_PASSES)]
-        for b in range(R_PASSES):
+        w1p = [keep.tile([P, 2 * H], U8, name=f"w1p{a}", align_bytes=64) for a in range(K_PASSES)]
+        for a in range(K_PASSES):
             nc.vector.tensor_copy(
-                w1p[b][:].bitcast(U16).rearrange("p a (t c e) -> p c a t e", t=PACK, e=8),
-                w1_raw[b][:].bitcast(U16).rearrange("p a (c e t) -> p c a t e", t=PACK, e=8),
+                w1p[a][:].bitcast(U16).rearrange("p (b t c e) -> p b c t e", b=R_PASSES, t=PACK, e=8),
+                w1_raw[a][:].bitcast(U16).rearrange("p (b c e t) -> p b c t e", b=R_PASSES, t=PACK, e=8),
             )
         nc.vector.tensor_copy(v_sc[0][:], tab_sc[:].indirect(idx[:]))
         for a in range(1, K_PASSES):
@@ -156,7 +153,6 @@ def tile_list_auction_guide_clip_kernel(
         h_pairs = []
 
         def make_h(i, h, j0, j1, bank):
-            b, t = divmod(i, PACK)
             step = BANK if j1 - j0 == BANK else P
             acc = psum.tile([P, j1 - j0], F32, name="acc", tag=f"bank{bank}")
             for a in range(K_PASSES):
@@ -164,7 +160,7 @@ def tile_list_auction_guide_clip_kernel(
                     cols = slice(c0, c0 + step)
                     nc.tensor.matmul_mx(
                         acc[:, c0 - j0 : c0 - j0 + step],
-                        lhsT=w1p[b][:, a, 2 * P * t : 2 * P * (t + 1)].bitcast(FP4X4),
+                        lhsT=w1p[a][:, 2 * P * i : 2 * P * (i + 1)].bitcast(FP4X4),
                         lhsT_scale=w1p_sc[:, a, P * i : P * (i + 1)],
                         rhs=v[a][:, cols].bitcast(FP8X4),
                         rhs_scale=v_sc[a][:, cols],

@@ -203,12 +203,12 @@ def tile_list_auction_guide_clip_kernel(
                 woven = interleave(raw[:, :, col0:col1])
                 nc.vector.quantize_mx(w2_codes[b][:, col0:col1].bitcast(FP8X4), w2_sc[b][:, col0:col1], woven[:])
 
-        def fetch(b, first, count, x_tag, woven_tag=None):
+        def fetch(b, first, count, x_tag, woven_tag=None, clip=nc.gpsimd):
             x = keep.tile([P, PACK, count], F32, name="x", tag=x_tag, align_bytes=64)
             for t in range(PACK):
                 nc.vector.tensor_copy(x[:, t, :], pages[b * PACK + t][:].indirect(entries(idx3, first, count)))
             for t in range(PACK):
-                nc.vector.tensor_scalar(x[:, t, :], x[:, t, :], lo[:, b, t : t + 1], hi[:, b, t : t + 1], MAX, MIN)
+                clip.tensor_scalar(x[:, t, :], x[:, t, :], hi[:, b, t : t + 1], lo[:, b, t : t + 1], MIN, MAX)
             return interleave(x[:], woven_tag)
 
         z_codes = [keep.tile([P, M], U32, name=f"z_codes{b}", align_bytes=64) for b in range(R_PASSES)]
@@ -296,7 +296,7 @@ def tile_list_auction_guide_clip_kernel(
         quantise_z(1, m_second, woven_1_second)
         multiply(1, 1)
         multiply(0, 2)
-        woven_1_last = fetch(1, m_last, narrow, "second", "last")
+        woven_1_last = fetch(1, m_last, narrow, "second", "last", nc.vector)
         held = keep.tile([P, 2, BANK], F32, name="held", tag="page4")
         for n in range(2):
             finish(0, N_TILES - 2 + n, held[:, n, :])

@@ -31,7 +31,7 @@ BANKS = 8
 N_TILES = N // P
 CHUNKS = ((0, 512), (512, 256), (768, 256))
 W2_PIECES = ((0, 512), (512, N))
-MOVED_ROWS = 112
+MOVED_ROWS = 100
 LEAD = 256
 H_BANK, FIRST_SET_BANK, TURNED_BANK = 0, 2, 5
 
@@ -203,12 +203,12 @@ def tile_list_auction_guide_clip_kernel(
                 woven = interleave(raw[:, :, col0:col1])
                 nc.vector.quantize_mx(w2_codes[b][:, col0:col1].bitcast(FP8X4), w2_sc[b][:, col0:col1], woven[:])
 
-        def fetch(b, first, count, x_tag, woven_tag=None, clip=nc.gpsimd):
+        def fetch(b, first, count, x_tag, woven_tag=None):
             x = keep.tile([P, PACK, count], F32, name="x", tag=x_tag, align_bytes=64)
             for t in range(PACK):
                 nc.vector.tensor_copy(x[:, t, :], pages[b * PACK + t][:].indirect(entries(idx3, first, count)))
             for t in range(PACK):
-                clip.tensor_scalar(x[:, t, :], x[:, t, :], hi[:, b, t : t + 1], lo[:, b, t : t + 1], MIN, MAX)
+                nc.gpsimd.tensor_scalar(x[:, t, :], x[:, t, :], hi[:, b, t : t + 1], lo[:, b, t : t + 1], MIN, MAX)
             return interleave(x[:], woven_tag)
 
         z_codes = [keep.tile([P, M], U32, name=f"z_codes{b}", align_bytes=64) for b in range(R_PASSES)]
@@ -249,7 +249,7 @@ def tile_list_auction_guide_clip_kernel(
                         stop=(b == R_PASSES - 1 and n == per_bank - 1),
                     )
 
-        def finish(c, n0, y=None):
+        def finish(c, n0, y=None, pool=False):
             m0, width = CHUNKS[c]
             per_bank = BANK // width
             n = n0 % 2
@@ -258,7 +258,12 @@ def tile_list_auction_guide_clip_kernel(
                 staged = stage.tile([P, BANK], F32, name="y")
                 y = staged[:]
             y = y.rearrange("p (n m) -> p n m", n=per_bank)
-            nc.vector.tensor_tensor(y, banks[c, n0][:], factor, MULT)
+            if pool:
+                staged = stage.tile([P, per_bank, width], F32, name="y")
+                nc.scalar.copy(staged[:], banks[c, n0][:])
+                nc.gpsimd.tensor_tensor(y, staged[:], factor, MULT)
+            else:
+                nc.vector.tensor_tensor(y, banks[c, n0][:], factor, MULT)
             nc.sync.dma_start(
                 out[n0 * P : (n0 + per_bank) * P, m0 : m0 + width].rearrange("(n p) m -> p n m", p=P), y
             )
@@ -289,22 +294,24 @@ def tile_list_auction_guide_clip_kernel(
         quantise_z(1, m_wide, woven_1_wide)
         multiply(1, 0)
         woven_1_second = fetch(1, m_second, narrow, "work2", "second")
-        for n0 in range(N_TILES - 2):
+        finish(0, 0, pool=True)
+        for n0 in range(1, N_TILES - 2):
             finish(0, n0)
         quantise_z(0, m_second, woven_0_narrow)
         multiply(0, 1)
         quantise_z(1, m_second, woven_1_second)
         multiply(1, 1)
         multiply(0, 2)
-        woven_1_last = fetch(1, m_last, narrow, "second", "last", nc.vector)
+        woven_1_last = fetch(1, m_last, narrow, "second", "last")
         held = keep.tile([P, 2, BANK], F32, name="held", tag="page4")
-        for n in range(2):
-            finish(0, N_TILES - 2 + n, held[:, n, :])
-        finish(1, 0)
+        held_pool = keep.tile([P, BANK], F32, name="held_pool", tag="page7")
+        finish(0, N_TILES - 2, held_pool[:], pool=True)
+        finish(0, N_TILES - 1, held[:, 0, :])
+        finish(1, 0, held[:, 1, :])
+        finish(1, 2)
         quantise_z(1, m_last, woven_1_last)
         multiply(1, 2)
-        held_last = keep.tile([P, 2, BANK], F32, name="held_last", tag="last", align_bytes=64)
-        for n in range(2):
-            finish(1, 2 + 2 * n, held_last[:, n, :])
+        held_last = keep.tile([P, BANK], F32, name="held_last", tag="last", align_bytes=64)
+        finish(1, 4, held_last[:])
         for n0 in range(0, N_TILES, 2):
             finish(2, n0)

@@ -22,6 +22,7 @@ P = 128
 PACK = 4
 QUADRANTS = 4
 QUADRANT = P // QUADRANTS
+RUN = 4
 PER_COLUMN = 16
 K_PASSES = K // (P * PACK)
 R_PASSES = H // (P * PACK)
@@ -70,7 +71,7 @@ def tile_list_auction_guide_clip_kernel(
 
         weights = [keep.tile([P, S], F32, name=f"wgs{t}") for t in range(PACK)]
         pages = {}
-        page_rows = page0.rearrange("(b p t) c -> b t p c", t=PACK, p=P)
+        page_rows = page0.rearrange("(b g t u) c -> b t g u c", b=R_PASSES, t=PACK, u=RUN)
         turned = []
 
         def turn_wgs():
@@ -88,10 +89,10 @@ def tile_list_auction_guide_clip_kernel(
             for half in range(S // BANK):
                 cols = slice(half * BANK, (half + 1) * BANK)
                 dealt = spread[:, cols]
-                rows_t = turned[half][:].rearrange("p n (u t) -> p n t u", t=PACK)[:, :, t : t + 1, :]
+                rows_t = turned[half][:].rearrange("p n (g t u) -> p n t g u", t=PACK, u=RUN)[:, :, t : t + 1, :, :]
                 nc.scalar.copy(
-                    dealt.rearrange("p (n q u) -> p n q u", q=QUADRANTS, u=QUADRANT),
-                    rows_t.to_broadcast([P, BANK // P, QUADRANTS, QUADRANT]),
+                    dealt.rearrange("p (n q g u) -> p n q g u", q=QUADRANTS, u=RUN, g=QUADRANT // RUN),
+                    rows_t.to_broadcast([P, BANK // P, QUADRANTS, QUADRANT // RUN, RUN]),
                 )
                 first_bank = H_BANK if t == 0 else FIRST_SET_BANK
                 bank = psum.tile([P, BANK // P, P], F32, name="back", tag=f"bank{first_bank + half}")
@@ -103,9 +104,11 @@ def tile_list_auction_guide_clip_kernel(
             pages[i] = keep.tile([P, T], F32, name=f"page{i}", tag=f"page{i}")
             nc.sync.dma_start(pages[i][:], page_rows[i // PACK, i % PACK])
 
-        w1_raw = [keep.tile([P, 2 * H], U8, name=f"w1_raw{a}", align_bytes=64) for a in range(K_PASSES)]
-        for a in range(K_PASSES):
-            nc.sync.dma_start(w1_raw[a][:].bitcast(I32), w1_words[a].bitcast(I32))
+        w1_first = keep.tile([P, 2 * H], U8, name="w1_first")
+        w1_rest = keep.tile([P, K_PASSES - 1, 2 * H], U8, name="w1_rest")
+        nc.sync.dma_start(w1_first[:].bitcast(I32), w1_words[0].bitcast(I32))
+        nc.sync.dma_start(w1_rest[:].bitcast(I32), w1_words[1:].rearrange("a p c -> p a c").bitcast(I32))
+        w1_raw = [w1_first[:]] + [w1_rest[:, a, :] for a in range(K_PASSES - 1)]
         nc.sync.dma_start(idx[:], offs)
         for q in range(QUADRANTS):
             (nc.sync if q % 2 == 0 else nc.scalar).dma_start(
@@ -126,8 +129,8 @@ def tile_list_auction_guide_clip_kernel(
         w1p = [keep.tile([P, 2 * H], U8, name=f"w1p{a}", align_bytes=64) for a in range(K_PASSES)]
         for a in range(K_PASSES):
             nc.vector.tensor_copy(
-                w1p[a][:].bitcast(U16).rearrange("p (b t c e) -> p b c t e", b=R_PASSES, t=PACK, e=8),
-                w1_raw[a][:].bitcast(U16).rearrange("p (b c e t) -> p b c t e", b=R_PASSES, t=PACK, e=8),
+                w1p[a][:].bitcast(I32).rearrange("p (b t g e) -> p b t g e", b=R_PASSES, t=PACK, e=2),
+                w1_raw[a].bitcast(I32).rearrange("p (b g t e) -> p b t g e", b=R_PASSES, t=PACK, e=2),
             )
         nc.vector.tensor_copy(v_sc[0][:], tab_sc[:].indirect(idx[:]))
         for a in range(1, K_PASSES):
@@ -137,8 +140,8 @@ def tile_list_auction_guide_clip_kernel(
             )
         load_page(0)
         nc.vector.tensor_copy(
-            w1p_sc[:].rearrange("p a (b t c e) -> p (a b) c t e", b=R_PASSES, t=PACK, e=16),
-            w1_sc[:].rearrange("p a (b c e t) -> p (a b) c t e", b=R_PASSES, t=PACK, e=16),
+            w1p_sc[:].bitcast(I32).rearrange("p a (b t c e) -> p (a b) c t e", b=R_PASSES, t=PACK, e=4),
+            w1_sc[:].bitcast(I32).rearrange("p a (b c e t) -> p (a b) c t e", b=R_PASSES, t=PACK, e=4),
         )
         for i in range(1, PACK):
             load_page(i)
@@ -196,9 +199,10 @@ def tile_list_auction_guide_clip_kernel(
         w2_sc = [keep.tile([P, N], U8, name=f"w2_sc{b}", align_bytes=64) for b in range(R_PASSES)]
 
         def quantise_w2(b):
-            w2_pass = w2[b * P * PACK : (b + 1) * P * PACK, :].rearrange("(p t) n -> p t n", t=PACK)
+            w2_pass = w2[b * P * PACK : (b + 1) * P * PACK, :].rearrange("(g t u) n -> t g u n", t=PACK, u=RUN)
             raw = keep.tile([P, PACK, N], F32, name="w2_raw", tag=f"big{b}")
-            nc.sync.dma_start(raw[:], w2_pass)
+            for t in range(PACK):
+                nc.sync.dma_start(raw[:, t, :], w2_pass[t])
             for col0, col1 in W2_PIECES:
                 woven = interleave(raw[:, :, col0:col1])
                 nc.vector.quantize_mx(w2_codes[b][:, col0:col1].bitcast(FP8X4), w2_sc[b][:, col0:col1], woven[:])
@@ -208,7 +212,8 @@ def tile_list_auction_guide_clip_kernel(
             for t in range(PACK):
                 nc.vector.tensor_copy(x[:, t, :], pages[b * PACK + t][:].indirect(entries(idx3, first, count)))
             for t in range(PACK):
-                nc.gpsimd.tensor_scalar(x[:, t, :], x[:, t, :], hi[:, b, t : t + 1], lo[:, b, t : t + 1], MIN, MAX)
+                i = b * PACK + t
+                nc.gpsimd.tensor_scalar(x[:, t, :], x[:, t, :], bounds[:, 1, i : i + 1], bounds[:, 0, i : i + 1], MIN, MAX)
             return interleave(x[:], woven_tag)
 
         z_codes = [keep.tile([P, M], U32, name=f"z_codes{b}", align_bytes=64) for b in range(R_PASSES)]
@@ -264,7 +269,7 @@ def tile_list_auction_guide_clip_kernel(
                 nc.gpsimd.tensor_tensor(y, staged[:], factor, MULT)
             else:
                 nc.vector.tensor_tensor(y, banks[c, n0][:], factor, MULT)
-            nc.sync.dma_start(
+            (nc.scalar if pool else nc.sync).dma_start(
                 out[n0 * P : (n0 + per_bank) * P, m0 : m0 + width].rearrange("(n p) m -> p n m", p=P), y
             )
 
@@ -277,10 +282,17 @@ def tile_list_auction_guide_clip_kernel(
             quantise_w2(b)
             load_page(ROW_SETS - R_PASSES + b)
         nc.sync.dma_start(idx3[:], offs3)
-        lo = keep.tile([P, R_PASSES, PACK], F32, name="lo")
-        hi = keep.tile([P, R_PASSES, PACK], F32, name="hi")
-        nc.sync.dma_start(lo[:], reserve.rearrange("(b p t) -> p b t", p=P, t=PACK))
-        nc.sync.dma_start(hi[:], ceiling.rearrange("(b p t) -> p b t", p=P, t=PACK))
+        bound_rows = keep.tile([P, P], F32, name="bound_rows")
+        nc.gpsimd.memset(bound_rows[:], 0.0)
+        for n, source in enumerate((reserve, ceiling)):
+            rows = source.rearrange("(b g t u) -> b t g u", b=R_PASSES, t=PACK, u=RUN)
+            for b in range(R_PASSES):
+                first = n * ROW_SETS + b * PACK
+                nc.sync.dma_start(bound_rows[first : first + PACK, :].rearrange("t (g u) -> t g u", u=RUN), rows[b])
+        bound_bank = psum.tile([P, P], F32, name="bound_bank", tag=f"bank{BANKS - 1}")
+        nc.tensor.transpose(bound_bank[:], bound_rows[:], identity[:])
+        bounds = keep.tile([P, 2, ROW_SETS], F32, name="bounds")
+        nc.scalar.copy(bounds[:].rearrange("p n i -> p (n i)"), bound_bank[:, 0 : 2 * ROW_SETS])
         load_seller()
         for i in range(PACK, ROW_SETS):
             put_rows(i)

@@ -23,6 +23,7 @@ PACK = 4
 QUADRANTS = 4
 QUADRANT = P // QUADRANTS
 RUN = 4
+SCALE_ROWS = 4
 PER_COLUMN = 16
 K_PASSES = K // (P * PACK)
 R_PASSES = H // (P * PACK)
@@ -32,8 +33,9 @@ BANKS = 8
 N_TILES = N // P
 CHUNKS = ((0, 512), (512, 256), (768, 256))
 W2_PIECES = ((0, 512), (512, N))
-MOVED_ROWS = 100
+MOVED_ROWS = P - QUADRANT + SCALE_ROWS
 LEAD = 256
+SHORT_CLIP = 32
 H_BANK, FIRST_SET_BANK, TURNED_BANK = 0, 2, 5
 
 
@@ -112,15 +114,15 @@ def tile_list_auction_guide_clip_kernel(
         nc.sync.dma_start(idx[:], offs)
         for q in range(QUADRANTS):
             (nc.sync if q % 2 == 0 else nc.scalar).dma_start(
-                tab_sc[QUADRANT * q : QUADRANT * q + 4 * K_PASSES, :].bitcast(I32),
-                tab_scales[:, 4 * q : 4 * q + 4, :].bitcast(I32),
+                tab_sc[QUADRANT * q : QUADRANT * q + SCALE_ROWS * K_PASSES, :].bitcast(I32),
+                tab_scales[:, SCALE_ROWS * q : SCALE_ROWS * (q + 1), :].bitcast(I32),
             )
         load_tab(0)
         identity = keep.tile([P, P], F32, name="identity")
         make_identity(nc, identity[:])
         turn_wgs()
-        w1_scale_rows = w1_scales.rearrange("a (q j) c -> j q a c", j=4)
-        for j in range(4):
+        w1_scale_rows = w1_scales.rearrange("a (q j) c -> j q a c", j=SCALE_ROWS)
+        for j in range(SCALE_ROWS):
             nc.sync.dma_start(w1_sc[j:P:QUADRANT, :, :].bitcast(I32), w1_scale_rows[j].bitcast(I32))
         load_tab(1)
         load_tab(2)
@@ -136,7 +138,7 @@ def tile_list_auction_guide_clip_kernel(
         for a in range(1, K_PASSES):
             nc.sync.dma_start(
                 v_sc[a][0:MOVED_ROWS, :].bitcast(I32),
-                v_sc[0][4 * a : 4 * a + MOVED_ROWS, :].bitcast(I32),
+                v_sc[0][SCALE_ROWS * a : SCALE_ROWS * a + MOVED_ROWS, :].bitcast(I32),
             )
         load_page(0)
         nc.vector.tensor_copy(
@@ -207,13 +209,16 @@ def tile_list_auction_guide_clip_kernel(
                 woven = interleave(raw[:, :, col0:col1])
                 nc.vector.quantize_mx(w2_codes[b][:, col0:col1].bitcast(FP8X4), w2_sc[b][:, col0:col1], woven[:])
 
-        def fetch(b, first, count, x_tag, woven_tag=None):
+        def fetch(b, first, count, x_tag, woven_tag=None, short=0):
             x = keep.tile([P, PACK, count], F32, name="x", tag=x_tag, align_bytes=64)
             for t in range(PACK):
                 nc.vector.tensor_copy(x[:, t, :], pages[b * PACK + t][:].indirect(entries(idx3, first, count)))
             for t in range(PACK):
                 i = b * PACK + t
-                nc.gpsimd.tensor_scalar(x[:, t, :], x[:, t, :], bounds[:, 1, i : i + 1], bounds[:, 0, i : i + 1], MIN, MAX)
+                low, high = bounds[:, 0, i : i + 1], bounds[:, 1, i : i + 1]
+                cuts = (0, short, count) if short and t == PACK - 1 else (0, count)
+                for c0, c1 in zip(cuts, cuts[1:]):
+                    nc.gpsimd.tensor_scalar(x[:, t, c0:c1], x[:, t, c0:c1], high, low, MIN, MAX)
             return interleave(x[:], woven_tag)
 
         z_codes = [keep.tile([P, M], U32, name=f"z_codes{b}", align_bytes=64) for b in range(R_PASSES)]
@@ -254,7 +259,7 @@ def tile_list_auction_guide_clip_kernel(
                         stop=(b == R_PASSES - 1 and n == per_bank - 1),
                     )
 
-        def finish(c, n0, y=None, pool=False):
+        def finish(c, n0, y=None, on_gpsimd=False):
             m0, width = CHUNKS[c]
             per_bank = BANK // width
             n = n0 % 2
@@ -263,13 +268,13 @@ def tile_list_auction_guide_clip_kernel(
                 staged = stage.tile([P, BANK], F32, name="y")
                 y = staged[:]
             y = y.rearrange("p (n m) -> p n m", n=per_bank)
-            if pool:
-                staged = stage.tile([P, per_bank, width], F32, name="y")
-                nc.scalar.copy(staged[:], banks[c, n0][:])
-                nc.gpsimd.tensor_tensor(y, staged[:], factor, MULT)
+            if on_gpsimd:
+                emptied = stage.tile([P, per_bank, width], F32, name="y")
+                nc.scalar.copy(emptied[:], banks[c, n0][:])
+                nc.gpsimd.tensor_tensor(y, emptied[:], factor, MULT)
             else:
                 nc.vector.tensor_tensor(y, banks[c, n0][:], factor, MULT)
-            (nc.scalar if pool else nc.sync).dma_start(
+            (nc.scalar if on_gpsimd else nc.sync).dma_start(
                 out[n0 * P : (n0 + per_bank) * P, m0 : m0 + width].rearrange("(n p) m -> p n m", p=P), y
             )
 
@@ -299,14 +304,14 @@ def tile_list_auction_guide_clip_kernel(
 
         (m_wide, wide), (m_second, narrow), (m_last, narrow) = CHUNKS
         woven_0_wide = fetch(0, m_wide, wide, "work3")
-        woven_1_wide = fetch(1, m_wide, wide, "work2")
+        woven_1_wide = fetch(1, m_wide, wide, "work2", short=SHORT_CLIP)
         quantise_z(0, m_wide, woven_0_wide)
         multiply(0, 0)
-        woven_0_narrow = fetch(0, m_second, 2 * narrow, "work3")
+        woven_0_narrow = fetch(0, m_second, 2 * narrow, "work3", short=SHORT_CLIP)
         quantise_z(1, m_wide, woven_1_wide)
         multiply(1, 0)
         woven_1_second = fetch(1, m_second, narrow, "work2", "second")
-        finish(0, 0, pool=True)
+        finish(0, 0, on_gpsimd=True)
         for n0 in range(1, N_TILES - 2):
             finish(0, n0)
         quantise_z(0, m_second, woven_0_narrow)
@@ -316,8 +321,8 @@ def tile_list_auction_guide_clip_kernel(
         multiply(0, 2)
         woven_1_last = fetch(1, m_last, narrow, "second", "last")
         held = keep.tile([P, 2, BANK], F32, name="held", tag="page4")
-        held_pool = keep.tile([P, BANK], F32, name="held_pool", tag="page7")
-        finish(0, N_TILES - 2, held_pool[:], pool=True)
+        held_gpsimd = keep.tile([P, BANK], F32, name="held_gpsimd", tag="page7")
+        finish(0, N_TILES - 2, held_gpsimd[:], on_gpsimd=True)
         finish(0, N_TILES - 1, held[:, 0, :])
         finish(1, 0, held[:, 1, :])
         finish(1, 2)

@@ -28,6 +28,9 @@ PER_COLUMN = 16
 K_PASSES = K // (P * PACK)
 R_PASSES = H // (P * PACK)
 ROW_SETS = R_PASSES * PACK
+HALF = P * PACK
+QUARTER = 256
+LAST_PASS_ROW = 4
 BANK = 512
 BANKS = 8
 N_TILES = N // P
@@ -57,96 +60,111 @@ def tile_list_auction_guide_clip_kernel(
         def entries(offsets, first, count):
             return offsets[:, first // PER_COLUMN : (first + count) // PER_COLUMN]
 
-        tab_sc = keep.tile([P, T], U8, name="tab_sc", align_bytes=64)
-        w1_sc = keep.tile([P, K_PASSES, H], U8, name="w1_sc", align_bytes=64)
+        tab_sc = keep.tile([P, T], U8, name="tab_sc", tag="page0")
         v_sc = [keep.tile([P, S], U8, name=f"v_sc{a}", align_bytes=64) for a in range(K_PASSES)]
-        w1p_sc = keep.tile([P, K_PASSES, H], U8, name="w1p_sc", align_bytes=64)
+        w1_sc = [keep.tile([P, K_PASSES, HALF], U8, name=f"w1_sc{b}", align_bytes=64) for b in range(R_PASSES)]
         nc.gpsimd.memset(tab_sc[:].bitcast(I32), 0)
-        nc.vector.memset(w1_sc[:].bitcast(I32), 0)
-        for a in range(1, K_PASSES):
-            nc.vector.memset(v_sc[a][P - QUADRANT : P, :].bitcast(I32), 0)
+        nc.vector.memset(w1_sc[0][:].bitcast(I32), 0)
+        nc.vector.memset(v_sc[1][P - QUADRANT : P, :].bitcast(I32), 0)
+        nc.vector.memset(v_sc[2][:].bitcast(I32), 0)
+        nc.vector.memset(w1_sc[1][:].bitcast(I32), 0)
 
         tab = [keep.tile([P, T], I32, name=f"tab{a}", tag=f"big{a}") for a in range(K_PASSES)]
 
         def load_tab(a):
             nc.sync.dma_start(tab[a][:], tab_words[a].rearrange("p t i -> p (t i)").bitcast(I32))
 
-        weights = [keep.tile([P, S], F32, name=f"wgs{t}") for t in range(PACK)]
         pages = {}
         page_rows = page0.rearrange("(b g t u) c -> b t g u c", b=R_PASSES, t=PACK, u=RUN)
-        turned = []
-
-        def turn_wgs():
-            rows = keep.tile([P, S], F32, name="wgs_rows", tag="page5")
-            nc.sync.dma_start(rows[:], wgs)
-            for half in range(S // BANK):
-                bank = psum.tile([P, BANK // P, P], F32, name="turned", tag=f"bank{TURNED_BANK + half}")
-                for n in range(BANK // P):
-                    j0 = half * BANK + n * P
-                    nc.tensor.transpose(bank[:, n, :], rows[:, j0 : j0 + P], identity[:])
-                turned.append(bank)
-
-        def deal_wgs(t):
-            spread = keep.tile([P, S], F32, name="spread", tag="page6")
-            for half in range(S // BANK):
-                cols = slice(half * BANK, (half + 1) * BANK)
-                dealt = spread[:, cols]
-                rows_t = turned[half][:].rearrange("p n (g t u) -> p n t g u", t=PACK, u=RUN)[:, :, t : t + 1, :, :]
-                nc.scalar.copy(
-                    dealt.rearrange("p (n q g u) -> p n q g u", q=QUADRANTS, u=RUN, g=QUADRANT // RUN),
-                    rows_t.to_broadcast([P, BANK // P, QUADRANTS, QUADRANT // RUN, RUN]),
-                )
-                first_bank = H_BANK if t == 0 else FIRST_SET_BANK
-                bank = psum.tile([P, BANK // P, P], F32, name="back", tag=f"bank{first_bank + half}")
-                for n in range(BANK // P):
-                    nc.tensor.transpose(bank[:, n, :], dealt[:, n * P : (n + 1) * P], identity[:])
-                nc.scalar.copy(weights[t][:, cols], bank[:].rearrange("p n j -> p (n j)"))
 
         def load_page(i):
             pages[i] = keep.tile([P, T], F32, name=f"page{i}", tag=f"page{i}")
             nc.sync.dma_start(pages[i][:], page_rows[i // PACK, i % PACK])
 
-        w1_first = keep.tile([P, 2 * H], U8, name="w1_first")
-        w1_rest = keep.tile([P, K_PASSES - 1, 2 * H], U8, name="w1_rest")
-        nc.sync.dma_start(w1_first[:].bitcast(I32), w1_words[0].bitcast(I32))
-        nc.sync.dma_start(w1_rest[:].bitcast(I32), w1_words[1:].rearrange("a p c -> p a c").bitcast(I32))
-        w1_raw = [w1_first[:]] + [w1_rest[:, a, :] for a in range(K_PASSES - 1)]
-        nc.sync.dma_start(idx[:], offs)
-        for q in range(QUADRANTS):
-            (nc.sync if q % 2 == 0 else nc.scalar).dma_start(
-                tab_sc[QUADRANT * q : QUADRANT * q + SCALE_ROWS * K_PASSES, :].bitcast(I32),
-                tab_scales[:, SCALE_ROWS * q : SCALE_ROWS * (q + 1), :].bitcast(I32),
+        weights = [keep.tile([P, S], F32, name=f"wgs{t}") for t in range(PACK)]
+        wgs_rows = wgs.rearrange("(g t u) n -> g t (u n)", t=PACK, u=RUN)
+        wgs_rows = wgs_rows.rearrange("g t (e n) -> t g e n", n=QUARTER)
+        wgs_cut = {}
+
+        def load_wgs(t):
+            wgs_cut[t] = keep.tile([P, QUARTER], F32, name=f"wgs_cut{t}")
+            nc.sync.dma_start(wgs_cut[t][:], wgs_rows[t])
+
+        def deal_wgs(t):
+            turned = psum.tile([P, QUARTER // P, P], F32, name="turned", tag=f"bank{TURNED_BANK if t == 0 else FIRST_SET_BANK + 2}")
+            for n in range(QUARTER // P):
+                nc.tensor.transpose(turned[:, n, :], wgs_cut[t][:, n * P : (n + 1) * P], identity[:])
+            by_quarter = turned[:].rearrange("p n (r c) -> p c n r", c=S // QUARTER).unsqueeze(3)
+            spread = keep.tile([P, S], F32, name="spread", tag="page6")
+            for half in range(S // BANK):
+                cols = slice(half * BANK, (half + 1) * BANK)
+                dealt = spread[:, cols]
+                nc.scalar.copy(
+                    dealt.rearrange("p (c n q r) -> p c n q r", c=2, q=QUADRANTS, r=QUADRANT),
+                    by_quarter[:, 2 * half : 2 * half + 2].to_broadcast([P, 2, QUARTER // P, QUADRANTS, QUADRANT]),
+                )
+                bank = psum.tile([P, BANK // P, P], F32, name="back", tag=f"bank{TURNED_BANK + 1 + half}")
+                for n in range(BANK // P):
+                    nc.tensor.transpose(bank[:, n, :], dealt[:, n * P : (n + 1) * P], identity[:])
+                nc.scalar.copy(weights[t][:, cols], bank[:].rearrange("p n j -> p (n j)"))
+
+        w1_raw = [keep.tile([P, K_PASSES, 2 * HALF], U8, name=f"w1_raw{b}") for b in range(R_PASSES)]
+        w1p = [keep.tile([P, K_PASSES, 2 * HALF], U8, name=f"w1p{b}", align_bytes=64) for b in range(R_PASSES)]
+        w1p_sc = [keep.tile([P, K_PASSES, HALF], U8, name=f"w1p_sc{b}", align_bytes=64) for b in range(R_PASSES)]
+        w1_scale_rows = w1_scales.rearrange("a (q j) c -> j q a c", j=SCALE_ROWS)
+
+        def load_w1(b):
+            words = w1_words.rearrange("a p c -> p a c")[:, :, 2 * HALF * b : 2 * HALF * (b + 1)]
+            nc.sync.dma_start(w1_raw[b][:].bitcast(I32), words.bitcast(I32))
+
+        def load_w1_scales(b):
+            for j in range(SCALE_ROWS):
+                rows = w1_scale_rows[j][:, :, HALF * b : HALF * (b + 1)]
+                nc.sync.dma_start(w1_sc[b][j:P:QUADRANT, :, :].bitcast(I32), rows.bitcast(I32))
+
+        def deal_w1(b, copy, dtype):
+            copy(
+                w1p[b][:].bitcast(dtype).rearrange("p a (t g e) -> p t a g e", t=PACK, e=2),
+                w1_raw[b][:].bitcast(dtype).rearrange("p a (g t e) -> p t a g e", t=PACK, e=2),
             )
+
+        def deal_w1_scales(b):
+            nc.scalar.copy(
+                w1p_sc[b][:].bitcast(U32).rearrange("p a (t c e) -> p a c t e", t=PACK, e=4),
+                w1_sc[b][:].bitcast(U32).rearrange("p a (c e t) -> p a c t e", t=PACK, e=4),
+            )
+
+        load_w1(0)
+        nc.sync.dma_start(idx[:], offs)
+        tab_scale_rows = tab_scales[0:2].rearrange("a (q j) c -> j q a c", j=SCALE_ROWS)
+        nc.sync.dma_start(tab_sc[LAST_PASS_ROW:P:8, :].bitcast(I32), tab_scales[2].bitcast(I32))
+        for j in range(SCALE_ROWS):
+            nc.sync.dma_start(tab_sc[j:P:16, :].bitcast(I32), tab_scale_rows[j].bitcast(I32))
         load_tab(0)
+        load_wgs(0)
+        load_w1_scales(0)
+        load_tab(1)
+        nc.sync.dma_start(idx2[:], offs2)
+        load_tab(2)
         identity = keep.tile([P, P], F32, name="identity")
         make_identity(nc, identity[:])
-        turn_wgs()
-        w1_scale_rows = w1_scales.rearrange("a (q j) c -> j q a c", j=SCALE_ROWS)
-        for j in range(SCALE_ROWS):
-            nc.sync.dma_start(w1_sc[j:P:QUADRANT, :, :].bitcast(I32), w1_scale_rows[j].bitcast(I32))
-        load_tab(1)
-        load_tab(2)
-        nc.sync.dma_start(idx2[:], offs2)
-
-        w1p = [keep.tile([P, 2 * H], U8, name=f"w1p{a}", align_bytes=64) for a in range(K_PASSES)]
-        for a in range(K_PASSES):
-            nc.vector.tensor_copy(
-                w1p[a][:].bitcast(I32).rearrange("p (b t g e) -> p b t g e", b=R_PASSES, t=PACK, e=2),
-                w1_raw[a].bitcast(I32).rearrange("p (b g t e) -> p b t g e", b=R_PASSES, t=PACK, e=2),
-            )
+        deal_w1(0, nc.vector.tensor_copy, I32)
         nc.vector.tensor_copy(v_sc[0][:], tab_sc[:].indirect(idx[:]))
-        for a in range(1, K_PASSES):
+        nc.sync.dma_start(v_sc[1][0:MOVED_ROWS, :].bitcast(I32), v_sc[0][16 : 16 + MOVED_ROWS, :].bitcast(I32))
+        for j in range(SCALE_ROWS):
             nc.sync.dma_start(
-                v_sc[a][0:MOVED_ROWS, :].bitcast(I32),
-                v_sc[0][SCALE_ROWS * a : SCALE_ROWS * a + MOVED_ROWS, :].bitcast(I32),
+                v_sc[2][j:P:QUADRANT, :].bitcast(I32), v_sc[0][8 * j + LAST_PASS_ROW : P : QUADRANT, :].bitcast(I32)
             )
         load_page(0)
-        nc.vector.tensor_copy(
-            w1p_sc[:].bitcast(I32).rearrange("p a (b t c e) -> p (a b) c t e", b=R_PASSES, t=PACK, e=4),
-            w1_sc[:].bitcast(I32).rearrange("p a (b c e t) -> p (a b) c t e", b=R_PASSES, t=PACK, e=4),
-        )
-        for i in range(1, PACK):
-            load_page(i)
+        deal_w1_scales(0)
+        load_wgs(1)
+        load_page(1)
+        for t in range(2, PACK):
+            load_wgs(t)
+        load_page(2)
+        load_w1(1)
+        load_w1_scales(1)
+        load_page(3)
 
         v = [keep.tile([P, S], U32, name=f"v{a}", align_bytes=64) for a in range(K_PASSES)]
         last = K_PASSES - 1
@@ -158,6 +176,7 @@ def tile_list_auction_guide_clip_kernel(
         h_pairs = []
 
         def make_h(i, h, j0, j1, bank):
+            b, t = divmod(i, PACK)
             step = BANK if j1 - j0 == BANK else P
             acc = psum.tile([P, j1 - j0], F32, name="acc", tag=f"bank{bank}")
             for a in range(K_PASSES):
@@ -165,8 +184,8 @@ def tile_list_auction_guide_clip_kernel(
                     cols = slice(c0, c0 + step)
                     nc.tensor.matmul_mx(
                         acc[:, c0 - j0 : c0 - j0 + step],
-                        lhsT=w1p[a][:, 2 * P * i : 2 * P * (i + 1)].bitcast(FP4X4),
-                        lhsT_scale=w1p_sc[:, a, P * i : P * (i + 1)],
+                        lhsT=w1p[b][:, a, 2 * P * t : 2 * P * (t + 1)].bitcast(FP4X4),
+                        lhsT_scale=w1p_sc[b][:, a, P * t : P * (t + 1)],
                         rhs=v[a][:, cols].bitcast(FP8X4),
                         rhs_scale=v_sc[a][:, cols],
                         start=(a == 0 and c0 == j0),
@@ -281,6 +300,8 @@ def tile_list_auction_guide_clip_kernel(
         for i in range(PACK):
             deal_wgs(i)
             put_rows(i)
+        deal_w1(1, nc.scalar.copy, U32)
+        deal_w1_scales(1)
         for i in range(PACK, ROW_SETS - R_PASSES):
             load_page(i)
         for b in range(R_PASSES):

@@ -63,7 +63,7 @@ def tile_list_auction_guide_clip_kernel(
         tab_sc = keep.tile([P, T], U8, name="tab_sc", tag="page0")
         v_sc = [keep.tile([P, S], U8, name=f"v_sc{a}", align_bytes=64) for a in range(K_PASSES)]
         w1_sc = [keep.tile([P, K_PASSES, HALF], U8, name=f"w1_sc{b}", align_bytes=64) for b in range(R_PASSES)]
-        nc.gpsimd.memset(tab_sc[:].bitcast(I32), 0)
+        nc.vector.memset(tab_sc[:].bitcast(I32), 0)
         nc.vector.memset(w1_sc[0][:].bitcast(I32), 0)
         nc.vector.memset(v_sc[1][P - QUADRANT : P, :].bitcast(I32), 0)
         nc.vector.memset(v_sc[2][:].bitcast(I32), 0)

@@ -63,11 +63,11 @@ def tile_list_auction_guide_clip_kernel(
         tab_sc = keep.tile([P, T], U8, name="tab_sc", tag="page0")
         v_sc = [keep.tile([P, S], U8, name=f"v_sc{a}", align_bytes=64) for a in range(K_PASSES)]
         w1_sc = [keep.tile([P, K_PASSES, HALF], U8, name=f"w1_sc{b}", align_bytes=64) for b in range(R_PASSES)]
-        nc.vector.memset(tab_sc[:].bitcast(I32), 0)
-        nc.vector.memset(w1_sc[0][:].bitcast(I32), 0)
-        nc.vector.memset(v_sc[1][P - QUADRANT : P, :].bitcast(I32), 0)
-        nc.vector.memset(v_sc[2][:].bitcast(I32), 0)
-        nc.vector.memset(w1_sc[1][:].bitcast(I32), 0)
+        nc.gpsimd.memset(tab_sc[:].bitcast(I32), 0)
+        nc.gpsimd.memset(w1_sc[0][:].bitcast(I32), 0)
+        nc.gpsimd.memset(v_sc[1][P - QUADRANT : P, :].bitcast(I32), 0)
+        nc.gpsimd.memset(v_sc[2][:].bitcast(I32), 0)
+        nc.gpsimd.memset(w1_sc[1][:].bitcast(I32), 0)
 
         tab = [keep.tile([P, T], I32, name=f"tab{a}", tag=f"big{a}") for a in range(K_PASSES)]
 
@@ -83,26 +83,28 @@ def tile_list_auction_guide_clip_kernel(
 
         weights = [keep.tile([P, S], F32, name=f"wgs{t}") for t in range(PACK)]
         wgs_rows = wgs.rearrange("(g t u) n -> g t (u n)", t=PACK, u=RUN)
-        wgs_rows = wgs_rows.rearrange("g t (e n) -> t g e n", n=QUARTER)
+        wgs_rows = wgs_rows.rearrange("(f y) t (x n) -> t f x y n", f=2, n=P)
         wgs_cut = {}
 
         def load_wgs(t):
-            wgs_cut[t] = keep.tile([P, QUARTER], F32, name=f"wgs_cut{t}")
-            nc.sync.dma_start(wgs_cut[t][:], wgs_rows[t])
+            wgs_cut[t] = keep.tile([P, 2, P], F32, name=f"wgs_cut{t}")
+            for f in range(2):
+                nc.sync.dma_start(wgs_cut[t][:, f, :], wgs_rows[t, f])
 
         def deal_wgs(t):
-            turned = psum.tile([P, QUARTER // P, P], F32, name="turned", tag=f"bank{TURNED_BANK if t == 0 else FIRST_SET_BANK + 2}")
-            for n in range(QUARTER // P):
-                nc.tensor.transpose(turned[:, n, :], wgs_cut[t][:, n * P : (n + 1) * P], identity[:])
-            by_quarter = turned[:].rearrange("p n (r c) -> p c n r", c=S // QUARTER).unsqueeze(3)
+            turned = psum.tile([P, 2, P], F32, name="turned", tag=f"bank{TURNED_BANK}")
+            for f in range(2):
+                nc.tensor.transpose(turned[:, f, :], wgs_cut[t][:, f, :], identity[:])
+            by_block = turned[:].rearrange("p f (u c y) -> p f c y u", u=RUN, y=4).unsqueeze(3)
             spread = keep.tile([P, S], F32, name="spread", tag="page6")
             for half in range(S // BANK):
                 cols = slice(half * BANK, (half + 1) * BANK)
                 dealt = spread[:, cols]
-                nc.scalar.copy(
-                    dealt.rearrange("p (c n q r) -> p c n q r", c=2, q=QUADRANTS, r=QUADRANT),
-                    by_quarter[:, 2 * half : 2 * half + 2].to_broadcast([P, 2, QUARTER // P, QUADRANTS, QUADRANT]),
-                )
+                for f in range(2):
+                    nc.scalar.copy(
+                        dealt.rearrange("p (c q f y u) -> p f c q y u", q=QUADRANTS, f=2, y=4, u=RUN)[:, f],
+                        by_block[:, f, 4 * half : 4 * half + 4].to_broadcast([P, 4, QUADRANTS, 4, RUN]),
+                    )
                 bank = psum.tile([P, BANK // P, P], F32, name="back", tag=f"bank{TURNED_BANK + 1 + half}")
                 for n in range(BANK // P):
                     nc.tensor.transpose(bank[:, n, :], dealt[:, n * P : (n + 1) * P], identity[:])
@@ -198,6 +200,8 @@ def tile_list_auction_guide_clip_kernel(
                 h_pairs.append(keep.tile([P, 2, S], F32, name="h_pair", tag=f"work{i // 2}", align_bytes=64))
             h = h_pairs[i // 2][:, i % 2, :]
             cuts, first_bank = ((0, LEAD, BANK, S), FIRST_SET_BANK) if i == 0 else ((0, BANK, S), H_BANK)
+            if 2 <= i < PACK:
+                first_bank = TURNED_BANK + 1
             for n in range(len(cuts) - 1):
                 make_h(i, h, cuts[n], cuts[n + 1], first_bank + n)
             for j0, j1 in ((0, LEAD), (LEAD, S)) if i == 0 else ((0, S),):

@@ -30,7 +30,7 @@ R_PASSES = H // (P * PACK)
 ROW_SETS = R_PASSES * PACK
 HALF = P * PACK
 QUARTER = 256
-LAST_PASS_ROW = 4
+FIRST_SCALE_ROW = (0, 4, 2)
 BANK = 512
 BANKS = 8
 N_TILES = N // P
@@ -61,12 +61,12 @@ def tile_list_auction_guide_clip_kernel(
             return offsets[:, first // PER_COLUMN : (first + count) // PER_COLUMN]
 
         tab_sc = keep.tile([P, T], U8, name="tab_sc", tag="page0")
-        v_sc = [keep.tile([P, S], U8, name=f"v_sc{a}", align_bytes=64) for a in range(K_PASSES)]
+        picked_sc = keep.tile([P, S], U8, name="picked_sc")
+        v_sc = keep.tile([P, K_PASSES, S], U8, name="v_sc", align_bytes=64)
         w1_sc = [keep.tile([P, K_PASSES, HALF], U8, name=f"w1_sc{b}", align_bytes=64) for b in range(R_PASSES)]
         nc.gpsimd.memset(tab_sc[:].bitcast(I32), 0)
         nc.gpsimd.memset(w1_sc[0][:].bitcast(I32), 0)
-        nc.gpsimd.memset(v_sc[1][P - QUADRANT : P, :].bitcast(I32), 0)
-        nc.gpsimd.memset(v_sc[2][:].bitcast(I32), 0)
+        nc.gpsimd.memset(v_sc[:].bitcast(I32), 0)
         nc.gpsimd.memset(w1_sc[1][:].bitcast(I32), 0)
 
         tab = [keep.tile([P, T], I32, name=f"tab{a}", tag=f"big{a}") for a in range(K_PASSES)]
@@ -138,25 +138,26 @@ def tile_list_auction_guide_clip_kernel(
 
         load_w1(0)
         nc.sync.dma_start(idx[:], offs)
-        tab_scale_rows = tab_scales[0:2].rearrange("a (q j) c -> j q a c", j=SCALE_ROWS)
-        nc.sync.dma_start(tab_sc[LAST_PASS_ROW:P:8, :].bitcast(I32), tab_scales[2].bitcast(I32))
-        for j in range(SCALE_ROWS):
-            nc.sync.dma_start(tab_sc[j:P:16, :].bitcast(I32), tab_scale_rows[j].bitcast(I32))
+        for a, row in enumerate(FIRST_SCALE_ROW):
+            nc.sync.dma_start(tab_sc[row:P:8, :].bitcast(I32), tab_scales[a].bitcast(I32))
         load_tab(0)
         load_wgs(0)
         load_w1_scales(0)
         load_tab(1)
         nc.sync.dma_start(idx2[:], offs2)
-        load_tab(2)
         identity = keep.tile([P, P], F32, name="identity")
         make_identity(nc, identity[:])
         deal_w1(0, nc.vector.tensor_copy, I32)
-        nc.vector.tensor_copy(v_sc[0][:], tab_sc[:].indirect(idx[:]))
-        nc.sync.dma_start(v_sc[1][0:MOVED_ROWS, :].bitcast(I32), v_sc[0][16 : 16 + MOVED_ROWS, :].bitcast(I32))
-        for j in range(SCALE_ROWS):
+        nc.vector.tensor_copy(picked_sc[:], tab_sc[:].indirect(idx[:]))
+        for q in range(QUADRANTS):
+            rows = slice(QUADRANT * q, QUADRANT * (q + 1), 4)
             nc.sync.dma_start(
-                v_sc[2][j:P:QUADRANT, :].bitcast(I32), v_sc[0][8 * j + LAST_PASS_ROW : P : QUADRANT, :].bitcast(I32)
+                v_sc[QUADRANT * q : QUADRANT * q + SCALE_ROWS, 0:2, :].bitcast(I32), picked_sc[rows, :].bitcast(I32)
             )
+        load_tab(2)
+        for j in range(SCALE_ROWS):
+            rows = slice(8 * j + FIRST_SCALE_ROW[2], P, QUADRANT)
+            nc.sync.dma_start(v_sc[j:P:QUADRANT, 2, :].bitcast(I32), picked_sc[rows, :].bitcast(I32))
         load_page(0)
         deal_w1_scales(0)
         load_wgs(1)
@@ -189,7 +190,7 @@ def tile_list_auction_guide_clip_kernel(
                         lhsT=w1p[b][:, a, 2 * P * t : 2 * P * (t + 1)].bitcast(FP4X4),
                         lhsT_scale=w1p_sc[b][:, a, P * t : P * (t + 1)],
                         rhs=v[a][:, cols].bitcast(FP8X4),
-                        rhs_scale=v_sc[a][:, cols],
+                        rhs_scale=v_sc[:, a, cols],
                         start=(a == 0 and c0 == j0),
                         stop=(a == last and c0 + step == j1),
                     )

@@ -92,19 +92,18 @@ def tile_list_auction_guide_clip_kernel(
                 nc.sync.dma_start(wgs_cut[t][:, f, :], wgs_rows[t, f])
 
         def deal_wgs(t):
-            turned = psum.tile([P, 2, P], F32, name="turned", tag=f"bank{TURNED_BANK}")
+            turned = psum.tile([P, QUADRANT, 2, 4], F32, name="turned", tag=f"bank{TURNED_BANK}")
             for f in range(2):
-                nc.tensor.transpose(turned[:, f, :], wgs_cut[t][:, f, :], identity[:])
-            by_block = turned[:].rearrange("p f (u c y) -> p f c y u", u=RUN, y=4).unsqueeze(3)
+                nc.tensor.transpose(turned[:, :, f, :], wgs_cut[t][:, f, :], identity[:])
+            by_block = turned[:].rearrange("p (u c) f y -> p c (f y) u", u=RUN).unsqueeze(2)
             spread = keep.tile([P, S], F32, name="spread", tag="page6")
             for half in range(S // BANK):
                 cols = slice(half * BANK, (half + 1) * BANK)
                 dealt = spread[:, cols]
-                for f in range(2):
-                    nc.scalar.copy(
-                        dealt.rearrange("p (c q f y u) -> p f c q y u", q=QUADRANTS, f=2, y=4, u=RUN)[:, f],
-                        by_block[:, f, 4 * half : 4 * half + 4].to_broadcast([P, 4, QUADRANTS, 4, RUN]),
-                    )
+                nc.scalar.copy(
+                    dealt.rearrange("p (c q g u) -> p c q g u", q=QUADRANTS, g=QUADRANT // RUN, u=RUN),
+                    by_block[:, 4 * half : 4 * half + 4].to_broadcast([P, 4, QUADRANTS, QUADRANT // RUN, RUN]),
+                )
                 bank = psum.tile([P, BANK // P, P], F32, name="back", tag=f"bank{TURNED_BANK + 1 + half}")
                 for n in range(BANK // P):
                     nc.tensor.transpose(bank[:, n, :], dealt[:, n * P : (n + 1) * P], identity[:])
@@ -115,19 +114,19 @@ def tile_list_auction_guide_clip_kernel(
         w1p_sc = [keep.tile([P, K_PASSES, HALF], U8, name=f"w1p_sc{b}", align_bytes=64) for b in range(R_PASSES)]
         w1_scale_rows = w1_scales.rearrange("a (q j) c -> j q a c", j=SCALE_ROWS)
 
-        def load_w1(b):
-            words = w1_words.rearrange("a p c -> p a c")[:, :, 2 * HALF * b : 2 * HALF * (b + 1)]
-            nc.sync.dma_start(w1_raw[b][:].bitcast(I32), words.bitcast(I32))
+        def load_w1(b, a0, a1):
+            words = w1_words.rearrange("a p c -> p a c")[:, a0:a1, 2 * HALF * b : 2 * HALF * (b + 1)]
+            nc.sync.dma_start(w1_raw[b][:, a0:a1, :].bitcast(I32), words.bitcast(I32))
 
         def load_w1_scales(b):
             for j in range(SCALE_ROWS):
                 rows = w1_scale_rows[j][:, :, HALF * b : HALF * (b + 1)]
                 nc.sync.dma_start(w1_sc[b][j:P:QUADRANT, :, :].bitcast(I32), rows.bitcast(I32))
 
-        def deal_w1(b, copy, dtype):
-            copy(
-                w1p[b][:].bitcast(dtype).rearrange("p a (t g e) -> p t a g e", t=PACK, e=2),
-                w1_raw[b][:].bitcast(dtype).rearrange("p a (g t e) -> p t a g e", t=PACK, e=2),
+        def deal_w1(b, a0, a1):
+            nc.scalar.copy(
+                w1p[b][:, a0:a1, :].bitcast(U32).rearrange("p a (t g e) -> p t a g e", t=PACK, e=2),
+                w1_raw[b][:, a0:a1, :].bitcast(U32).rearrange("p a (g t e) -> p t a g e", t=PACK, e=2),
             )
 
         def deal_w1_scales(b):
@@ -136,18 +135,18 @@ def tile_list_auction_guide_clip_kernel(
                 w1_sc[b][:].bitcast(U32).rearrange("p a (c e t) -> p a c t e", t=PACK, e=4),
             )
 
-        load_w1(0)
+        load_w1(0, 0, K_PASSES)
         nc.sync.dma_start(idx[:], offs)
         for a, row in enumerate(FIRST_SCALE_ROW):
             nc.sync.dma_start(tab_sc[row:P:8, :].bitcast(I32), tab_scales[a].bitcast(I32))
         load_tab(0)
-        load_wgs(0)
         load_w1_scales(0)
+        load_wgs(0)
         load_tab(1)
         nc.sync.dma_start(idx2[:], offs2)
         identity = keep.tile([P, P], F32, name="identity")
         make_identity(nc, identity[:])
-        deal_w1(0, nc.vector.tensor_copy, I32)
+        deal_w1(0, 0, K_PASSES)
         nc.vector.tensor_copy(picked_sc[:], tab_sc[:].indirect(idx[:]))
         for q in range(QUADRANTS):
             rows = slice(QUADRANT * q, QUADRANT * (q + 1), 4)
@@ -165,7 +164,7 @@ def tile_list_auction_guide_clip_kernel(
         for t in range(2, PACK):
             load_wgs(t)
         load_page(2)
-        load_w1(1)
+        load_w1(1, 0, K_PASSES)
         load_w1_scales(1)
         load_page(3)
 
@@ -305,7 +304,7 @@ def tile_list_auction_guide_clip_kernel(
         for i in range(PACK):
             deal_wgs(i)
             put_rows(i)
-        deal_w1(1, nc.scalar.copy, U32)
+        deal_w1(1, 0, K_PASSES)
         deal_w1_scales(1)
         for i in range(PACK, ROW_SETS - R_PASSES):
             load_page(i)

@@ -38,6 +38,7 @@ CHUNKS = ((0, 512), (512, 256), (768, 256))
 W2_PIECES = ((0, 512), (512, N))
 MOVED_ROWS = P - QUADRANT + SCALE_ROWS
 LEAD = 256
+FIRST_CUTS = (0, LEAD, S - LEAD, S)
 SHORT_CLIP = 32
 H_BANK, FIRST_SET_BANK, TURNED_BANK = 0, 2, 5
 
@@ -172,34 +173,31 @@ def tile_list_auction_guide_clip_kernel(
         last = K_PASSES - 1
         for a in range(last):
             nc.vector.tensor_copy(v[a][:], tab[a][:].bitcast(U32).indirect(idx[:]))
-        for j0, j1 in ((0, LEAD), (LEAD, S)):
+        for j0, j1 in zip(FIRST_CUTS, FIRST_CUTS[1:]):
             nc.vector.tensor_copy(v[last][:, j0:j1], tab[last][:].bitcast(U32).indirect(entries(idx, j0, j1 - j0)))
 
         h_pairs = []
 
         def make_h(i, h, j0, j1, bank):
             b, t = divmod(i, PACK)
-            step = BANK if j1 - j0 == BANK else P
             acc = psum.tile([P, j1 - j0], F32, name="acc", tag=f"bank{bank}")
             for a in range(K_PASSES):
-                for c0 in range(j0, j1, step):
-                    cols = slice(c0, c0 + step)
-                    nc.tensor.matmul_mx(
-                        acc[:, c0 - j0 : c0 - j0 + step],
-                        lhsT=w1p[b][:, a, 2 * P * t : 2 * P * (t + 1)].bitcast(FP4X4),
-                        lhsT_scale=w1p_sc[b][:, a, P * t : P * (t + 1)],
-                        rhs=v[a][:, cols].bitcast(FP8X4),
-                        rhs_scale=v_sc[:, a, cols],
-                        start=(a == 0 and c0 == j0),
-                        stop=(a == last and c0 + step == j1),
-                    )
+                nc.tensor.matmul_mx(
+                    acc[:],
+                    lhsT=w1p[b][:, a, 2 * P * t : 2 * P * (t + 1)].bitcast(FP4X4),
+                    lhsT_scale=w1p_sc[b][:, a, P * t : P * (t + 1)],
+                    rhs=v[a][:, j0:j1].bitcast(FP8X4),
+                    rhs_scale=v_sc[:, a, j0:j1],
+                    start=(a == 0),
+                    stop=(a == last),
+                )
             nc.scalar.copy(h[:, j0:j1], acc[:])
 
         def put_rows(i):
             if i % 2 == 0:
                 h_pairs.append(keep.tile([P, 2, S], F32, name="h_pair", tag=f"work{i // 2}", align_bytes=64))
             h = h_pairs[i // 2][:, i % 2, :]
-            cuts, first_bank = ((0, LEAD, BANK, S), FIRST_SET_BANK) if i == 0 else ((0, BANK, S), H_BANK)
+            cuts, first_bank = (FIRST_CUTS, FIRST_SET_BANK) if i == 0 else ((0, BANK, S), H_BANK)
             if 2 <= i < PACK:
                 first_bank = TURNED_BANK + 1
             for n in range(len(cuts) - 1):

@@ -15,6 +15,7 @@ U8 = mybir.dt.uint8
 FP8X4 = mybir.dt.float8_e4m3fn_x4
 FP4X4 = mybir.dt.float4_e2m1fn_x4
 MULT = mybir.AluOpType.mult
+ADD = mybir.AluOpType.add
 MAX = mybir.AluOpType.max
 MIN = mybir.AluOpType.min
 
@@ -230,7 +231,7 @@ def tile_list_auction_guide_clip_kernel(
                 woven = interleave(raw[:, :, col0:col1])
                 nc.vector.quantize_mx(w2_codes[b][:, col0:col1].bitcast(FP8X4), w2_sc[b][:, col0:col1], woven[:])
 
-        def fetch(b, first, count, x_tag, woven_tag=None, short=0):
+        def fetch(b, first, count, x_tag, woven_tag=None, short=0, shared=0):
             x = keep.tile([P, PACK, count], F32, name="x", tag=x_tag, align_bytes=64)
             for t in range(PACK):
                 nc.vector.tensor_copy(x[:, t, :], pages[b * PACK + t][:].indirect(entries(idx3, first, count)))
@@ -240,7 +241,19 @@ def tile_list_auction_guide_clip_kernel(
                 cuts = (0, short, count) if short and t == PACK - 1 else (0, count)
                 for c0, c1 in zip(cuts, cuts[1:]):
                     nc.gpsimd.tensor_scalar(x[:, t, c0:c1], x[:, t, c0:c1], high, low, MIN, MAX)
-            return interleave(x[:], woven_tag)
+            if not shared:
+                return interleave(x[:], woven_tag)
+            woven = keep.tile([P, count * PACK], BF16, name="woven", tag=woven_tag, align_bytes=64)
+            own = count - shared
+            nc.scalar.copy(
+                woven[:, 0 : own * PACK].rearrange("p (c e t) -> p c t e", t=PACK, e=2),
+                x[:, :, 0:own].rearrange("p t (c e) -> p c t e", e=2),
+            )
+            nc.gpsimd.tensor_scalar(
+                woven[:, own * PACK :].rearrange("p (c t) -> p c t", t=PACK),
+                x[:, :, own:count].rearrange("p t c -> p c t"), 1.0, 0.0, MULT, ADD,
+            )
+            return woven
 
         z_codes = [keep.tile([P, M], U32, name=f"z_codes{b}", align_bytes=64) for b in range(R_PASSES)]
         z_sc = [keep.tile([P, M], U8, name=f"z_sc{b}", align_bytes=64) for b in range(R_PASSES)]
@@ -342,16 +355,15 @@ def tile_list_auction_guide_clip_kernel(
         quantise_z(1, m_second, woven_1_second)
         multiply(1, 1)
         multiply(0, 2)
-        woven_1_last = fetch(1, m_last, narrow, "second", "last")
+        woven_1_last = fetch(1, m_last, narrow, "second", "last", shared=96)
         held = keep.tile([P, 2, BANK], F32, name="held", tag="page4")
-        held_gpsimd = keep.tile([P, BANK], F32, name="held_gpsimd", tag="page7")
-        finish(0, N_TILES - 2, held_gpsimd[:], on_gpsimd=True)
         finish(0, N_TILES - 1, held[:, 0, :])
         finish(1, 0, held[:, 1, :])
         finish(1, 2)
         quantise_z(1, m_last, woven_1_last)
         multiply(1, 2)
-        held_last = keep.tile([P, BANK], F32, name="held_last", tag="last", align_bytes=64)
-        finish(1, 4, held_last[:])
+        held_last = keep.tile([P, 2, BANK], F32, name="held_last", tag="last", align_bytes=64)
+        finish(1, 4, held_last[:, 0, :])
+        finish(0, N_TILES - 2, held_last[:, 1, :])
         for n0 in range(0, N_TILES, 2):
             finish(2, n0)

@@ -35,12 +35,14 @@ FIRST_SCALE_ROW = (0, 4, 2)
 BANK = 512
 BANKS = 8
 N_TILES = N // P
-CHUNKS = ((0, 512), (512, 256), (768, 256))
-W2_PIECES = ((0, 512), (512, N))
+CHUNK = 256
+CHUNKS = M // CHUNK
+PAIRS = N_TILES // 2
+SHARED = 96
+W2_PIECES = ((0, 1024), (1024, R_PASSES * N))
 MOVED_ROWS = P - QUADRANT + SCALE_ROWS
 LEAD = 256
 FIRST_CUTS = (0, LEAD, S - LEAD, S)
-SHORT_CLIP = 32
 H_BANK, FIRST_SET_BANK, TURNED_BANK = 0, 2, 5
 
 
@@ -51,7 +53,6 @@ def tile_list_auction_guide_clip_kernel(
     nc = tc.nc
     with ExitStack() as ctx:
         keep = ctx.enter_context(tc.tile_pool(name="keep", bufs=1))
-        ring = ctx.enter_context(tc.tile_pool(name="ring", bufs=4))
         stage = ctx.enter_context(tc.tile_pool(name="stage", bufs=6))
         psum = ctx.enter_context(tc.psum_pool(name="psum", bufs=1))
 
@@ -177,7 +178,7 @@ def tile_list_auction_guide_clip_kernel(
         for j0, j1 in zip(FIRST_CUTS, FIRST_CUTS[1:]):
             nc.vector.tensor_copy(v[last][:, j0:j1], tab[last][:].bitcast(U32).indirect(entries(idx, j0, j1 - j0)))
 
-        h_pairs = []
+        work = keep.tile([P, 2 * ROW_SETS, BANK], F32, name="work", align_bytes=64)
 
         def make_h(i, h, j0, j1, bank):
             b, t = divmod(i, PACK)
@@ -195,9 +196,7 @@ def tile_list_auction_guide_clip_kernel(
             nc.scalar.copy(h[:, j0:j1], acc[:])
 
         def put_rows(i):
-            if i % 2 == 0:
-                h_pairs.append(keep.tile([P, 2, S], F32, name="h_pair", tag=f"work{i // 2}", align_bytes=64))
-            h = h_pairs[i // 2][:, i % 2, :]
+            h = work[:, 2 * i : 2 * i + 2, :].rearrange("p r c -> p (r c)")
             cuts, first_bank = (FIRST_CUTS, FIRST_SET_BANK) if i == 0 else ((0, BANK, S), H_BANK)
             if 2 <= i < PACK:
                 first_bank = TURNED_BANK + 1
@@ -208,59 +207,35 @@ def tile_list_auction_guide_clip_kernel(
                     pages[i][:].indirect(entries(idx2, j0, j1 - j0)), h[:, j0:j1], weights[i % PACK][:, j0:j1], MULT
                 )
 
-        def interleave(rows, tag=None):
-            if tag is None:
-                woven = ring.tile([P, rows.shape[2] * PACK], BF16, name="woven", align_bytes=64)
-            else:
-                woven = keep.tile([P, rows.shape[2] * PACK], BF16, name="woven", tag=tag, align_bytes=64)
+        woven = keep.tile([P, R_PASSES * PACK * M], BF16, name="woven", align_bytes=64)
+
+        def interleave(rows, first):
             nc.scalar.copy(
-                woven[:].rearrange("p (c e t) -> p c t e", t=PACK, e=2),
+                woven[:, first * PACK : (first + rows.shape[2]) * PACK].rearrange("p (c e t) -> p c t e", t=PACK, e=2),
                 rows.rearrange("p t (c e) -> p c t e", e=2),
             )
-            return woven
 
-        w2_codes = [keep.tile([P, N], U32, name=f"w2_codes{b}", align_bytes=64) for b in range(R_PASSES)]
-        w2_sc = [keep.tile([P, N], U8, name=f"w2_sc{b}", align_bytes=64) for b in range(R_PASSES)]
+        w2_codes = keep.tile([P, R_PASSES * N], U32, name="w2_codes", align_bytes=64)
+        w2_sc = keep.tile([P, R_PASSES * N], U8, name="w2_sc", align_bytes=64)
 
-        def quantise_w2(b):
+        def load_w2(b):
             w2_pass = w2[b * P * PACK : (b + 1) * P * PACK, :].rearrange("(g t u) n -> t g u n", t=PACK, u=RUN)
             raw = keep.tile([P, PACK, N], F32, name="w2_raw", tag=f"big{b}")
             for t in range(PACK):
                 nc.sync.dma_start(raw[:, t, :], w2_pass[t])
-            for col0, col1 in W2_PIECES:
-                woven = interleave(raw[:, :, col0:col1])
-                nc.vector.quantize_mx(w2_codes[b][:, col0:col1].bitcast(FP8X4), w2_sc[b][:, col0:col1], woven[:])
+            interleave(raw[:], b * N)
 
-        def fetch(b, first, count, x_tag, woven_tag=None, short=0, shared=0):
-            x = keep.tile([P, PACK, count], F32, name="x", tag=x_tag, align_bytes=64)
-            for t in range(PACK):
-                nc.vector.tensor_copy(x[:, t, :], pages[b * PACK + t][:].indirect(entries(idx3, first, count)))
-            for t in range(PACK):
-                i = b * PACK + t
-                low, high = bounds[:, 0, i : i + 1], bounds[:, 1, i : i + 1]
-                cuts = (0, short, count) if short and t == PACK - 1 else (0, count)
-                for c0, c1 in zip(cuts, cuts[1:]):
-                    nc.gpsimd.tensor_scalar(x[:, t, c0:c1], x[:, t, c0:c1], high, low, MIN, MAX)
-            if not shared:
-                return interleave(x[:], woven_tag)
-            woven = keep.tile([P, count * PACK], BF16, name="woven", tag=woven_tag, align_bytes=64)
-            own = count - shared
-            nc.scalar.copy(
-                woven[:, 0 : own * PACK].rearrange("p (c e t) -> p c t e", t=PACK, e=2),
-                x[:, :, 0:own].rearrange("p t (c e) -> p c t e", e=2),
+        def quantise(codes, scales, first, last):
+            nc.vector.quantize_mx(
+                codes[:, first:last].bitcast(FP8X4), scales[:, first:last], woven[:, first * PACK : last * PACK]
             )
-            nc.gpsimd.tensor_scalar(
-                woven[:, own * PACK :].rearrange("p (c t) -> p c t", t=PACK),
-                x[:, :, own:count].rearrange("p t c -> p c t"), 1.0, 0.0, MULT, ADD,
-            )
-            return woven
 
-        z_codes = [keep.tile([P, M], U32, name=f"z_codes{b}", align_bytes=64) for b in range(R_PASSES)]
-        z_sc = [keep.tile([P, M], U8, name=f"z_sc{b}", align_bytes=64) for b in range(R_PASSES)]
+        def fetch(i, x, first):
+            nc.vector.tensor_copy(x, pages[i][:].indirect(entries(idx3, first, x.shape[1])))
+            nc.gpsimd.tensor_scalar(x, x, bounds[:, 1, i : i + 1], bounds[:, 0, i : i + 1], MIN, MAX)
 
-        def quantise_z(b, first, woven):
-            cols = slice(first, first + woven.shape[1] // PACK)
-            nc.vector.quantize_mx(z_codes[b][:, cols].bitcast(FP8X4), z_sc[b][:, cols], woven[:])
+        z_codes = keep.tile([P, R_PASSES * M], U32, name="z_codes", align_bytes=64)
+        z_sc = keep.tile([P, R_PASSES * M], U8, name="z_sc", align_bytes=64)
 
         factors = []
 
@@ -273,43 +248,37 @@ def tile_list_auction_guide_clip_kernel(
 
         banks = {}
 
-        def multiply(b, c):
-            m0, width = CHUNKS[c]
-            per_bank = BANK // width
-            cols = slice(m0, m0 + width)
-            for n0 in range(0, N_TILES, per_bank):
-                if b == 0:
-                    tag = f"bank{(FIRST_SET_BANK + len(banks)) % BANKS}"
-                    banks[c, n0] = psum.tile([P, per_bank, width], F32, name="acc", tag=tag)
-                for n in range(per_bank):
-                    n_cols = slice((n0 + n) * P, (n0 + n + 1) * P)
-                    nc.tensor.matmul_mx(
-                        banks[c, n0][:, n, :],
-                        lhsT=w2_codes[b][:, n_cols].bitcast(FP8X4),
-                        lhsT_scale=w2_sc[b][:, n_cols],
-                        rhs=z_codes[b][:, cols].bitcast(FP8X4),
-                        rhs_scale=z_sc[b][:, cols],
-                        start=(b == 0 and n == 0),
-                        stop=(b == R_PASSES - 1 and n == per_bank - 1),
-                    )
+        def multiply(b, c, pair):
+            cols = slice(b * M + c * CHUNK, b * M + (c + 1) * CHUNK)
+            if b == 0:
+                tag = f"bank{(FIRST_SET_BANK + len(banks)) % BANKS}"
+                banks[c, pair] = psum.tile([P, 2, CHUNK], F32, name="acc", tag=tag)
+            for n in range(2):
+                n_cols = slice(b * N + (2 * pair + n) * P, b * N + (2 * pair + n + 1) * P)
+                nc.tensor.matmul_mx(
+                    banks[c, pair][:, n, :],
+                    lhsT=w2_codes[:, n_cols].bitcast(FP8X4),
+                    lhsT_scale=w2_sc[:, n_cols],
+                    rhs=z_codes[:, cols].bitcast(FP8X4),
+                    rhs_scale=z_sc[:, cols],
+                    start=(b == 0 and n == 0),
+                    stop=(b == R_PASSES - 1 and n == 1),
+                )
 
-        def finish(c, n0, y=None, on_gpsimd=False):
-            m0, width = CHUNKS[c]
-            per_bank = BANK // width
-            n = n0 % 2
-            factor = factors[n0 // 2][:, n : n + per_bank, m0 : m0 + width]
+        def finish(c, pair, y=None, on_gpsimd=False):
+            factor = factors[pair][:, :, c * CHUNK : (c + 1) * CHUNK]
             if y is None:
                 staged = stage.tile([P, BANK], F32, name="y")
                 y = staged[:]
-            y = y.rearrange("p (n m) -> p n m", n=per_bank)
+            y = y.rearrange("p (n m) -> p n m", n=2)
             if on_gpsimd:
-                emptied = stage.tile([P, per_bank, width], F32, name="y")
-                nc.scalar.copy(emptied[:], banks[c, n0][:])
+                emptied = stage.tile([P, 2, CHUNK], F32, name="y")
+                nc.scalar.copy(emptied[:], banks[c, pair][:])
                 nc.gpsimd.tensor_tensor(y, emptied[:], factor, MULT)
             else:
-                nc.vector.tensor_tensor(y, banks[c, n0][:], factor, MULT)
+                nc.vector.tensor_tensor(y, banks[c, pair][:], factor, MULT)
             (nc.scalar if on_gpsimd else nc.sync).dma_start(
-                out[n0 * P : (n0 + per_bank) * P, m0 : m0 + width].rearrange("(n p) m -> p n m", p=P), y
+                out[2 * pair * P : 2 * (pair + 1) * P, c * CHUNK : (c + 1) * CHUNK].rearrange("(n p) m -> p n m", p=P), y
             )
 
         for i in range(PACK):
@@ -317,12 +286,12 @@ def tile_list_auction_guide_clip_kernel(
             put_rows(i)
         deal_w1(1, 0, K_PASSES)
         deal_w1_scales(1)
-        for i in range(PACK, ROW_SETS - R_PASSES):
-            load_page(i)
         for b in range(R_PASSES):
-            quantise_w2(b)
-            load_page(ROW_SETS - R_PASSES + b)
-        nc.sync.dma_start(idx3[:], offs3)
+            load_w2(b)
+            load_page(PACK + b)
+        for first, end in W2_PIECES:
+            quantise(w2_codes, w2_sc, first, end)
+        load_page(ROW_SETS - 2)
         bound_rows = keep.tile([P, P], F32, name="bound_rows")
         nc.gpsimd.memset(bound_rows[:], 0.0)
         for n, source in enumerate((reserve, ceiling)):
@@ -334,36 +303,68 @@ def tile_list_auction_guide_clip_kernel(
         nc.tensor.transpose(bound_bank[:], bound_rows[:], identity[:])
         bounds = keep.tile([P, 2, ROW_SETS], F32, name="bounds")
         nc.scalar.copy(bounds[:].rearrange("p n i -> p (n i)"), bound_bank[:, 0 : 2 * ROW_SETS])
+        nc.sync.dma_start(idx3[:], offs3)
+        load_page(ROW_SETS - 1)
         load_seller()
-        for i in range(PACK, ROW_SETS):
+        for i in range(PACK, ROW_SETS - 1):
             put_rows(i)
 
-        (m_wide, wide), (m_second, narrow), (m_last, narrow) = CHUNKS
-        woven_0_wide = fetch(0, m_wide, wide, "work3")
-        woven_1_wide = fetch(1, m_wide, wide, "work2", short=SHORT_CLIP)
-        quantise_z(0, m_wide, woven_0_wide)
-        multiply(0, 0)
-        woven_0_narrow = fetch(0, m_second, 2 * narrow, "work3", short=SHORT_CLIP)
-        quantise_z(1, m_wide, woven_1_wide)
-        multiply(1, 0)
-        woven_1_second = fetch(1, m_second, narrow, "work2", "second")
-        finish(0, 0, on_gpsimd=True)
-        for n0 in range(1, N_TILES - 2):
-            finish(0, n0)
-        quantise_z(0, m_second, woven_0_narrow)
-        multiply(0, 1)
-        quantise_z(1, m_second, woven_1_second)
-        multiply(1, 1)
-        multiply(0, 2)
-        woven_1_last = fetch(1, m_last, narrow, "second", "last", shared=96)
-        held = keep.tile([P, 2, BANK], F32, name="held", tag="page4")
-        finish(0, N_TILES - 1, held[:, 0, :])
-        finish(1, 0, held[:, 1, :])
-        finish(1, 2)
-        quantise_z(1, m_last, woven_1_last)
-        multiply(1, 2)
-        held_last = keep.tile([P, 2, BANK], F32, name="held_last", tag="last", align_bytes=64)
-        finish(1, 4, held_last[:, 0, :])
-        finish(0, N_TILES - 2, held_last[:, 1, :])
-        for n0 in range(0, N_TILES, 2):
-            finish(2, n0)
+        x_0 = work[:, 2:10, :].rearrange("p (t r) c -> p t (r c)", t=PACK)
+        x_wide = work[:, 0:4, :]
+        x_third = work[:, 4:8, 0:CHUNK]
+        x_last = work[:, 0:8:2, 0:CHUNK]
+        for t in range(PACK - 1):
+            fetch(t, x_0[:, t, :], 0)
+        for first in (0, BANK):
+            fetch(PACK - 1, x_0[:, PACK - 1, first : first + BANK], first)
+        interleave(x_0, 0)
+        fetch(PACK, x_wide[:, 0, :], 0)
+        put_rows(ROW_SETS - 1)
+        fetch(PACK + 1, x_wide[:, 1, :], 0)
+        quantise(z_codes, z_sc, 0, M)
+        order = [(c, pair) for c in range(CHUNKS) for pair in range(PAIRS)]
+        for c, pair in order[:BANKS]:
+            multiply(0, c, pair)
+        for t in range(2, PACK):
+            fetch(PACK + t, x_wide[:, t, :], 0)
+        for c in range(2):
+            interleave(x_wide[:, :, c * CHUNK : (c + 1) * CHUNK], M + c * CHUNK)
+        for t in range(PACK):
+            fetch(PACK + t, x_third[:, t, :], 2 * CHUNK)
+        interleave(x_third, M + 2 * CHUNK)
+
+        def second_pass(c):
+            quantise(z_codes, z_sc, M + c * CHUNK, M + (c + 1) * CHUNK)
+            for pair in range(PAIRS):
+                if (c, pair) in banks:
+                    multiply(1, c, pair)
+
+        second_pass(0)
+        fetch(PACK, x_last[:, 0, :], 3 * CHUNK)
+        second_pass(1)
+        finish(0, 0, work[:, 1, :])
+        multiply(0, 2, 2)
+        fetch(PACK + 1, x_last[:, 1, :], 3 * CHUNK)
+        second_pass(2)
+        finish(0, 1, on_gpsimd=True)
+        finish(0, 2, work[:, 5, :])
+        finish(1, 0, work[:, 7, :])
+        for pair in range(PAIRS):
+            multiply(0, 3, pair)
+        for t in range(2, PACK):
+            fetch(PACK + t, x_last[:, t, :], 3 * CHUNK)
+        own = CHUNK - SHARED
+        interleave(x_last[:, :, 0:own], M + 3 * CHUNK)
+        nc.gpsimd.tensor_scalar(
+            woven[:, (M + 3 * CHUNK + own) * PACK :].rearrange("p (c t) -> p c t", t=PACK),
+            x_last[:, :, own:].rearrange("p t c -> p c t"), 1.0, 0.0, MULT, ADD,
+        )
+        held = keep.tile([P, 3, BANK], F32, name="held", tag=f"page{ROW_SETS - 2}")
+        finish(1, 1, held[:, 0, :])
+        finish(1, 2, held[:, 1, :])
+        finish(2, 0, held[:, 2, :])
+        second_pass(3)
+        finish(2, 1, work[:, 0, :])
+        finish(2, 2, work[:, 2, :])
+        for pair in range(PAIRS):
+            finish(3, pair)

@@ -31,7 +31,8 @@ R_PASSES = H // (P * PACK)
 ROW_SETS = R_PASSES * PACK
 HALF = P * PACK
 QUARTER = 256
-FIRST_SCALE_ROW = (0, 4, 2)
+SCALE_ROWS_AT = (slice(32, 64, 2), slice(33, 64, 2), slice(112, P))
+ZEROED = (slice(0, 32), slice(64, 112))
 BANK = 512
 BANKS = 8
 N_TILES = N // P
@@ -67,8 +68,9 @@ def tile_list_auction_guide_clip_kernel(
         picked_sc = keep.tile([P, S], U8, name="picked_sc")
         v_sc = keep.tile([P, K_PASSES, S], U8, name="v_sc", align_bytes=64)
         w1_sc = [keep.tile([P, K_PASSES, HALF], U8, name=f"w1_sc{b}", align_bytes=64) for b in range(R_PASSES)]
-        nc.gpsimd.memset(tab_sc[:].bitcast(I32), 0)
         nc.gpsimd.memset(w1_sc[0][:].bitcast(I32), 0)
+        for rows in ZEROED:
+            nc.vector.memset(tab_sc[rows, :].bitcast(I32), 0)
         nc.gpsimd.memset(v_sc[:].bitcast(I32), 0)
         nc.gpsimd.memset(w1_sc[1][:].bitcast(I32), 0)
 
@@ -140,8 +142,8 @@ def tile_list_auction_guide_clip_kernel(
 
         load_w1(0, 0, K_PASSES)
         nc.sync.dma_start(idx[:], offs)
-        for a, row in enumerate(FIRST_SCALE_ROW):
-            nc.sync.dma_start(tab_sc[row:P:8, :].bitcast(I32), tab_scales[a].bitcast(I32))
+        for a, rows in enumerate(SCALE_ROWS_AT):
+            nc.sync.dma_start(tab_sc[rows, :].bitcast(I32), tab_scales[a].bitcast(I32))
         load_tab(0)
         load_w1_scales(0)
         load_wgs(0)
@@ -152,13 +154,13 @@ def tile_list_auction_guide_clip_kernel(
         deal_w1(0, 0, K_PASSES)
         nc.vector.tensor_copy(picked_sc[:], tab_sc[:].indirect(idx[:]))
         for q in range(QUADRANTS):
-            rows = slice(QUADRANT * q, QUADRANT * (q + 1), 4)
+            rows = slice(QUADRANT + 8 * q, QUADRANT + 8 * (q + 1))
             nc.sync.dma_start(
                 v_sc[QUADRANT * q : QUADRANT * q + SCALE_ROWS, 0:2, :].bitcast(I32), picked_sc[rows, :].bitcast(I32)
             )
         load_tab(2)
         for j in range(SCALE_ROWS):
-            rows = slice(8 * j + FIRST_SCALE_ROW[2], P, QUADRANT)
+            rows = slice(SCALE_ROWS_AT[2].start + j, P, SCALE_ROWS)
             nc.sync.dma_start(v_sc[j:P:QUADRANT, 2, :].bitcast(I32), picked_sc[rows, :].bitcast(I32))
         load_page(0)
         deal_w1_scales(0)

from contextlib import ExitStack

import concourse.mybir as mybir
from concourse.masks import make_identity

K, H, N, T, S, M = 1536, 1024, 768, 2048, 1024, 1024
FLOPS = 2 * K * H * S + 2 * H * N * M

F32 = mybir.dt.float32
BF16 = mybir.dt.bfloat16
I32 = mybir.dt.int32
U32 = mybir.dt.uint32
U16 = mybir.dt.uint16
U8 = mybir.dt.uint8
FP8X4 = mybir.dt.float8_e4m3fn_x4
FP4X4 = mybir.dt.float4_e2m1fn_x4
MULT = mybir.AluOpType.mult
ADD = mybir.AluOpType.add
MAX = mybir.AluOpType.max
MIN = mybir.AluOpType.min

P = 128
PACK = 4
QUADRANTS = 4
QUADRANT = P // QUADRANTS
RUN = 4
SCALE_ROWS = 4
PER_COLUMN = 16
K_PASSES = K // (P * PACK)
R_PASSES = H // (P * PACK)
ROW_SETS = R_PASSES * PACK
HALF = P * PACK
QUARTER = 256
SCALE_ROWS_AT = (slice(32, 64, 2), slice(33, 64, 2), slice(112, P))
ZEROED = (slice(0, 32), slice(64, 112))
BANK = 512
BANKS = 8
N_TILES = N // P
CHUNK = 256
CHUNKS = M // CHUNK
PAIRS = N_TILES // 2
SHARED = 96
W2_PIECES = ((0, 1024), (1024, R_PASSES * N))
MOVED_ROWS = P - QUADRANT + SCALE_ROWS
LEAD = 256
FIRST_CUTS = (0, LEAD, S - LEAD, S)
H_BANK, FIRST_SET_BANK, TURNED_BANK = 0, 2, 5


def tile_list_auction_guide_clip_kernel(
    tc, tab_words, tab_scales, offs, w1_words, w1_scales, wgs, page0, offs2, offs3,
    reserve, ceiling, w2, seller, out,
):
    nc = tc.nc
    with ExitStack() as ctx:
        keep = ctx.enter_context(tc.tile_pool(name="keep", bufs=1))
        stage = ctx.enter_context(tc.tile_pool(name="stage", bufs=6))
        psum = ctx.enter_context(tc.psum_pool(name="psum", bufs=1))

        idx = keep.tile([P, S // PER_COLUMN], U16, name="idx")
        idx2 = keep.tile([P, S // PER_COLUMN], U16, name="idx2")
        idx3 = keep.tile([P, M // PER_COLUMN], U16, name="idx3")

        def entries(offsets, first, count):
            return offsets[:, first // PER_COLUMN : (first + count) // PER_COLUMN]

        tab_sc = keep.tile([P, T], U8, name="tab_sc", tag="page0")
        picked_sc = keep.tile([P, S], U8, name="picked_sc")
        v_sc = keep.tile([P, K_PASSES, S], U8, name="v_sc", align_bytes=64)
        w1_sc = [keep.tile([P, K_PASSES, HALF], U8, name=f"w1_sc{b}", align_bytes=64) for b in range(R_PASSES)]
        nc.gpsimd.memset(w1_sc[0][:].bitcast(I32), 0)
        for rows in ZEROED:
            nc.vector.memset(tab_sc[rows, :].bitcast(I32), 0)
        nc.gpsimd.memset(v_sc[:].bitcast(I32), 0)
        nc.gpsimd.memset(w1_sc[1][:].bitcast(I32), 0)

        tab = [keep.tile([P, T], I32, name=f"tab{a}", tag=f"big{a}") for a in range(K_PASSES)]

        def load_tab(a):
            nc.sync.dma_start(tab[a][:], tab_words[a].rearrange("p t i -> p (t i)").bitcast(I32))

        pages = {}
        page_rows = page0.rearrange("(b g t u) c -> b t g u c", b=R_PASSES, t=PACK, u=RUN)

        def load_page(i):
            pages[i] = keep.tile([P, T], F32, name=f"page{i}", tag=f"page{i}")
            nc.sync.dma_start(pages[i][:], page_rows[i // PACK, i % PACK])

        weights = [keep.tile([P, S], F32, name=f"wgs{t}") for t in range(PACK)]
        wgs_rows = wgs.rearrange("(g t u) n -> g t (u n)", t=PACK, u=RUN)
        wgs_rows = wgs_rows.rearrange("(f y) t (x n) -> t f x y n", f=2, n=P)
        wgs_cut = {}

        def load_wgs(t):
            wgs_cut[t] = keep.tile([P, 2, P], F32, name=f"wgs_cut{t}")
            for f in range(2):
                nc.sync.dma_start(wgs_cut[t][:, f, :], wgs_rows[t, f])

        def deal_wgs(t):
            turned = psum.tile([P, QUADRANT, 2, 4], F32, name="turned", tag=f"bank{TURNED_BANK}")
            for f in range(2):
                nc.tensor.transpose(turned[:, :, f, :], wgs_cut[t][:, f, :], identity[:])
            by_block = turned[:].rearrange("p (u c) f y -> p c (f y) u", u=RUN).unsqueeze(2)
            spread = keep.tile([P, S], F32, name="spread", tag="page6")
            for half in range(S // BANK):
                cols = slice(half * BANK, (half + 1) * BANK)
                dealt = spread[:, cols]
                nc.scalar.copy(
                    dealt.rearrange("p (c q g u) -> p c q g u", q=QUADRANTS, g=QUADRANT // RUN, u=RUN),
                    by_block[:, 4 * half : 4 * half + 4].to_broadcast([P, 4, QUADRANTS, QUADRANT // RUN, RUN]),
                )
                bank = psum.tile([P, BANK // P, P], F32, name="back", tag=f"bank{TURNED_BANK + 1 + half}")
                for n in range(BANK // P):
                    nc.tensor.transpose(bank[:, n, :], dealt[:, n * P : (n + 1) * P], identity[:])
                nc.scalar.copy(weights[t][:, cols], bank[:].rearrange("p n j -> p (n j)"))

        w1_raw = [keep.tile([P, K_PASSES, 2 * HALF], U8, name=f"w1_raw{b}") for b in range(R_PASSES)]
        w1p = [keep.tile([P, K_PASSES, 2 * HALF], U8, name=f"w1p{b}", align_bytes=64) for b in range(R_PASSES)]
        w1p_sc = [keep.tile([P, K_PASSES, HALF], U8, name=f"w1p_sc{b}", align_bytes=64) for b in range(R_PASSES)]
        w1_scale_rows = w1_scales.rearrange("a (q j) c -> j q a c", j=SCALE_ROWS)

        def load_w1(b, a0, a1):
            words = w1_words.rearrange("a p c -> p a c")[:, a0:a1, 2 * HALF * b : 2 * HALF * (b + 1)]
            nc.sync.dma_start(w1_raw[b][:, a0:a1, :].bitcast(I32), words.bitcast(I32))

        def load_w1_scales(b):
            for j in range(SCALE_ROWS):
                rows = w1_scale_rows[j][:, :, HALF * b : HALF * (b + 1)]
                nc.sync.dma_start(w1_sc[b][j:P:QUADRANT, :, :].bitcast(I32), rows.bitcast(I32))

        def deal_w1(b, a0, a1):
            nc.scalar.copy(
                w1p[b][:, a0:a1, :].bitcast(U32).rearrange("p a (t g e) -> p t a g e", t=PACK, e=2),
                w1_raw[b][:, a0:a1, :].bitcast(U32).rearrange("p a (g t e) -> p t a g e", t=PACK, e=2),
            )

        def deal_w1_scales(b):
            nc.scalar.copy(
                w1p_sc[b][:].bitcast(U32).rearrange("p a (t c e) -> p a c t e", t=PACK, e=4),
                w1_sc[b][:].bitcast(U32).rearrange("p a (c e t) -> p a c t e", t=PACK, e=4),
            )

        load_w1(0, 0, K_PASSES)
        nc.sync.dma_start(idx[:], offs)
        for a, rows in enumerate(SCALE_ROWS_AT):
            nc.sync.dma_start(tab_sc[rows, :].bitcast(I32), tab_scales[a].bitcast(I32))
        load_tab(0)
        load_w1_scales(0)
        load_wgs(0)
        load_tab(1)
        nc.sync.dma_start(idx2[:], offs2)
        identity = keep.tile([P, P], F32, name="identity")
        make_identity(nc, identity[:])
        deal_w1(0, 0, K_PASSES)
        nc.vector.tensor_copy(picked_sc[:], tab_sc[:].indirect(idx[:]))
        for q in range(QUADRANTS):
            rows = slice(QUADRANT + 8 * q, QUADRANT + 8 * (q + 1))
            nc.sync.dma_start(
                v_sc[QUADRANT * q : QUADRANT * q + SCALE_ROWS, 0:2, :].bitcast(I32), picked_sc[rows, :].bitcast(I32)
            )
        load_tab(2)
        for j in range(SCALE_ROWS):
            rows = slice(SCALE_ROWS_AT[2].start + j, P, SCALE_ROWS)
            nc.sync.dma_start(v_sc[j:P:QUADRANT, 2, :].bitcast(I32), picked_sc[rows, :].bitcast(I32))
        load_page(0)
        deal_w1_scales(0)
        load_wgs(1)
        load_page(1)
        for t in range(2, PACK):
            load_wgs(t)
        load_page(2)
        load_w1(1, 0, K_PASSES)
        load_w1_scales(1)
        load_page(3)

        v = [keep.tile([P, S], U32, name=f"v{a}", align_bytes=64) for a in range(K_PASSES)]
        last = K_PASSES - 1
        for a in range(last):
            nc.vector.tensor_copy(v[a][:], tab[a][:].bitcast(U32).indirect(idx[:]))
        for j0, j1 in zip(FIRST_CUTS, FIRST_CUTS[1:]):
            nc.vector.tensor_copy(v[last][:, j0:j1], tab[last][:].bitcast(U32).indirect(entries(idx, j0, j1 - j0)))

        work = keep.tile([P, 2 * ROW_SETS, BANK], F32, name="work", align_bytes=64)

        def make_h(i, h, j0, j1, bank):
            b, t = divmod(i, PACK)
            acc = psum.tile([P, j1 - j0], F32, name="acc", tag=f"bank{bank}")
            for a in range(K_PASSES):
                nc.tensor.matmul_mx(
                    acc[:],
                    lhsT=w1p[b][:, a, 2 * P * t : 2 * P * (t + 1)].bitcast(FP4X4),
                    lhsT_scale=w1p_sc[b][:, a, P * t : P * (t + 1)],
                    rhs=v[a][:, j0:j1].bitcast(FP8X4),
                    rhs_scale=v_sc[:, a, j0:j1],
                    start=(a == 0),
                    stop=(a == last),
                )
            nc.scalar.copy(h[:, j0:j1], acc[:])

        def put_rows(i):
            h = work[:, 2 * i : 2 * i + 2, :].rearrange("p r c -> p (r c)")
            cuts, first_bank = (FIRST_CUTS, FIRST_SET_BANK) if i == 0 else ((0, BANK, S), H_BANK)
            if 2 <= i < PACK:
                first_bank = TURNED_BANK + 1
            for n in range(len(cuts) - 1):
                make_h(i, h, cuts[n], cuts[n + 1], first_bank + n)
            for j0, j1 in ((0, LEAD), (LEAD, S)) if i == 0 else ((0, S),):
                nc.vector.tensor_tensor(
                    pages[i][:].indirect(entries(idx2, j0, j1 - j0)), h[:, j0:j1], weights[i % PACK][:, j0:j1], MULT
                )

        woven = keep.tile([P, R_PASSES * PACK * M], BF16, name="woven", align_bytes=64)

        def interleave(rows, first):
            nc.scalar.copy(
                woven[:, first * PACK : (first + rows.shape[2]) * PACK].rearrange("p (c e t) -> p c t e", t=PACK, e=2),
                rows.rearrange("p t (c e) -> p c t e", e=2),
            )

        w2_codes = keep.tile([P, R_PASSES * N], U32, name="w2_codes", align_bytes=64)
        w2_sc = keep.tile([P, R_PASSES * N], U8, name="w2_sc", align_bytes=64)

        def load_w2(b):
            w2_pass = w2[b * P * PACK : (b + 1) * P * PACK, :].rearrange("(g t u) n -> t g u n", t=PACK, u=RUN)
            raw = keep.tile([P, PACK, N], F32, name="w2_raw", tag=f"big{b}")
            for t in range(PACK):
                nc.sync.dma_start(raw[:, t, :], w2_pass[t])
            interleave(raw[:], b * N)

        def quantise(codes, scales, first, last):
            nc.vector.quantize_mx(
                codes[:, first:last].bitcast(FP8X4), scales[:, first:last], woven[:, first * PACK : last * PACK]
            )

        def fetch(i, x, first):
            nc.vector.tensor_copy(x, pages[i][:].indirect(entries(idx3, first, x.shape[1])))
            nc.gpsimd.tensor_scalar(x, x, bounds[:, 1, i : i + 1], bounds[:, 0, i : i + 1], MIN, MAX)

        z_codes = keep.tile([P, R_PASSES * M], U32, name="z_codes", align_bytes=64)
        z_sc = keep.tile([P, R_PASSES * M], U8, name="z_sc", align_bytes=64)

        factors = []

        def load_seller():
            for pair, tag in enumerate(("big2", "big0", "big1")):
                tile = keep.tile([P, 2, M], F32, name="factors", tag=tag)
                seller_rows = seller[2 * pair * P : 2 * (pair + 1) * P, :]
                nc.sync.dma_start(tile[:], seller_rows.rearrange("(n p) m -> p n m", p=P))
                factors.append(tile)

        banks = {}

        def multiply(b, c, pair):
            cols = slice(b * M + c * CHUNK, b * M + (c + 1) * CHUNK)
            if b == 0:
                tag = f"bank{(FIRST_SET_BANK + len(banks)) % BANKS}"
                banks[c, pair] = psum.tile([P, 2, CHUNK], F32, name="acc", tag=tag)
            for n in range(2):
                n_cols = slice(b * N + (2 * pair + n) * P, b * N + (2 * pair + n + 1) * P)
                nc.tensor.matmul_mx(
                    banks[c, pair][:, n, :],
                    lhsT=w2_codes[:, n_cols].bitcast(FP8X4),
                    lhsT_scale=w2_sc[:, n_cols],
                    rhs=z_codes[:, cols].bitcast(FP8X4),
                    rhs_scale=z_sc[:, cols],
                    start=(b == 0 and n == 0),
                    stop=(b == R_PASSES - 1 and n == 1),
                )

        def finish(c, pair, y=None, on_gpsimd=False):
            factor = factors[pair][:, :, c * CHUNK : (c + 1) * CHUNK]
            if y is None:
                staged = stage.tile([P, BANK], F32, name="y")
                y = staged[:]
            y = y.rearrange("p (n m) -> p n m", n=2)
            if on_gpsimd:
                emptied = stage.tile([P, 2, CHUNK], F32, name="y")
                nc.scalar.copy(emptied[:], banks[c, pair][:])
                nc.gpsimd.tensor_tensor(y, emptied[:], factor, MULT)
            else:
                nc.vector.tensor_tensor(y, banks[c, pair][:], factor, MULT)
            (nc.scalar if on_gpsimd else nc.sync).dma_start(
                out[2 * pair * P : 2 * (pair + 1) * P, c * CHUNK : (c + 1) * CHUNK].rearrange("(n p) m -> p n m", p=P), y
            )

        for i in range(PACK):
            deal_wgs(i)
            put_rows(i)
        deal_w1(1, 0, K_PASSES)
        deal_w1_scales(1)
        for b in range(R_PASSES):
            load_w2(b)
            load_page(PACK + b)
        for first, end in W2_PIECES:
            quantise(w2_codes, w2_sc, first, end)
        load_page(ROW_SETS - 2)
        bound_rows = keep.tile([P, P], F32, name="bound_rows")
        nc.gpsimd.memset(bound_rows[:], 0.0)
        for n, source in enumerate((reserve, ceiling)):
            rows = source.rearrange("(b g t u) -> b t g u", b=R_PASSES, t=PACK, u=RUN)
            for b in range(R_PASSES):
                first = n * ROW_SETS + b * PACK
                nc.sync.dma_start(bound_rows[first : first + PACK, :].rearrange("t (g u) -> t g u", u=RUN), rows[b])
        bound_bank = psum.tile([P, P], F32, name="bound_bank", tag=f"bank{BANKS - 1}")
        nc.tensor.transpose(bound_bank[:], bound_rows[:], identity[:])
        bounds = keep.tile([P, 2, ROW_SETS], F32, name="bounds")
        nc.scalar.copy(bounds[:].rearrange("p n i -> p (n i)"), bound_bank[:, 0 : 2 * ROW_SETS])
        nc.sync.dma_start(idx3[:], offs3)
        load_page(ROW_SETS - 1)
        load_seller()
        for i in range(PACK, ROW_SETS - 1):
            put_rows(i)

        x_0 = work[:, 2:10, :].rearrange("p (t r) c -> p t (r c)", t=PACK)
        x_wide = work[:, 0:4, :]
        x_third = work[:, 4:8, 0:CHUNK]
        x_last = work[:, 0:8:2, 0:CHUNK]
        for t in range(PACK - 1):
            fetch(t, x_0[:, t, :], 0)
        for first in (0, BANK):
            fetch(PACK - 1, x_0[:, PACK - 1, first : first + BANK], first)
        interleave(x_0, 0)
        fetch(PACK, x_wide[:, 0, :], 0)
        put_rows(ROW_SETS - 1)
        fetch(PACK + 1, x_wide[:, 1, :], 0)
        quantise(z_codes, z_sc, 0, M)
        order = [(c, pair) for c in range(CHUNKS) for pair in range(PAIRS)]
        for c, pair in order[:BANKS]:
            multiply(0, c, pair)
        for t in range(2, PACK):
            fetch(PACK + t, x_wide[:, t, :], 0)
        for c in range(2):
            interleave(x_wide[:, :, c * CHUNK : (c + 1) * CHUNK], M + c * CHUNK)
        for t in range(PACK):
            fetch(PACK + t, x_third[:, t, :], 2 * CHUNK)
        interleave(x_third, M + 2 * CHUNK)

        def second_pass(c):
            quantise(z_codes, z_sc, M + c * CHUNK, M + (c + 1) * CHUNK)
            for pair in range(PAIRS):
                if (c, pair) in banks:
                    multiply(1, c, pair)

        second_pass(0)
        fetch(PACK, x_last[:, 0, :], 3 * CHUNK)
        second_pass(1)
        finish(0, 0, work[:, 1, :])
        multiply(0, 2, 2)
        fetch(PACK + 1, x_last[:, 1, :], 3 * CHUNK)
        second_pass(2)
        finish(0, 1, on_gpsimd=True)
        finish(0, 2, work[:, 5, :])
        finish(1, 0, work[:, 7, :])
        for pair in range(PAIRS):
            multiply(0, 3, pair)
        for t in range(2, PACK):
            fetch(PACK + t, x_last[:, t, :], 3 * CHUNK)
        own = CHUNK - SHARED
        interleave(x_last[:, :, 0:own], M + 3 * CHUNK)
        nc.gpsimd.tensor_scalar(
            woven[:, (M + 3 * CHUNK + own) * PACK :].rearrange("p (c t) -> p c t", t=PACK),
            x_last[:, :, own:].rearrange("p t c -> p c t"), 1.0, 0.0, MULT, ADD,
        )
        held = keep.tile([P, 3, BANK], F32, name="held", tag=f"page{ROW_SETS - 2}")
        finish(1, 1, held[:, 0, :])
        finish(1, 2, held[:, 1, :])
        finish(2, 0, held[:, 2, :])
        second_pass(3)
        finish(2, 1, work[:, 0, :])
        finish(2, 2, work[:, 2, :])
        for pair in range(PAIRS):
            finish(3, pair)
